import numpy as np, ml_dtypes
CORES = [6,15,38,47]
N = 4
import mx_ref
BF = ml_dtypes.bfloat16
def gcols(t, e):
    v = np.concatenate([t.reshape(8, 16, -1, 4), np.zeros((8, 16, 1, 4), BF)], axis=2)
    return np.ascontiguousarray(np.stack([v[g][:, e[g]] for g in range(8)])).reshape(128, -1)
def tile(rs):
    return np.stack(rs, axis=2).reshape(128, -1).astype(BF)
def cut(t, i, w=512):
    return t[:, w * i:w * i + w]
def pick(q, e):
    c = np.concatenate([q[0].reshape(128, -1, 4), np.zeros((128, 1, 4), np.uint8)], axis=1); s = np.concatenate([q[1], np.ones((16, 1), np.uint8)], axis=1)
    return (np.ascontiguousarray(c[:, e].reshape(128, -1)), np.ascontiguousarray(s[:, e]))
def join(*qs):
    return (np.concatenate([q[0] for q in qs], axis=1), np.concatenate([q[1] for q in qs], axis=1))
def put(q, e, v):
    c, s = q[0].reshape(128, -1, 4).copy(), q[1].copy(); c[:, e] = v[0].reshape(128, -1, 4); s[:, e] = v[1]
    return (c.reshape(128, -1), s)
def pk(c, s):
    return (np.ascontiguousarray(c), mx_ref.live(s))
def emit(q):
    return q[0], q[1]
def packed(v, rng):
    q = [mx_ref.quantize(np.ascontiguousarray(v[r])) for r in range(N)]
    return np.stack([a for a, b in q]), np.stack([mx_ref.plane(b, rng) for a, b in q])
def values_of_codes():
    e, c = np.zeros((128, 128, 4), np.float32), np.zeros((128, 2, 4), np.uint8)
    e[np.arange(128), np.arange(128), 0] = 1
    c[:127, :, 0] = np.arange(256).reshape(2, 128).T[:127]
    return mx_ref.matmul(mx_ref.quantize(e.reshape(128, 512).astype(BF)), (c.reshape(128, 8), np.full((16, 2), 127, np.uint8))).T.reshape(-1).astype(np.float64)
CODE_VALUE, SCALE_VALUE = values_of_codes(), 2.0 ** (np.arange(256) - 127.0)
def decode(q):
    return (CODE_VALUE[q[0]].reshape(16, 8, -1, 4) * SCALE_VALUE[q[1]][:, None, :, None] + 0.0).reshape(128, -1).astype(np.float32)
def f(rng, *shape):
    return mx_ref.flush((rng.standard_normal(shape, dtype=np.float32) * np.exp2(rng.integers(-2, 3, shape[:-1] + (1,)))).astype(BF))
def wide(rng, *shape, cols=0):
    v = rng.standard_normal(shape, dtype=np.float32) * np.exp2(rng.integers(-12, 13, shape)).astype(np.float32)
    if cols: v *= np.repeat(np.exp2(rng.integers(-cols, cols + 1, shape[:-2] + (1, shape[-1] // 4))) * (rng.random(shape[:-2] + (1, shape[-1] // 4)) > 0.0625), 4, axis=-1).astype(np.float32)
    return mx_ref.flush(v.astype(BF))
C, K, R = 384, 64, 3
def choose(p):
    o = np.argsort(-(p[::16] + np.float32(0.0)), axis=1, kind="stable")
    return np.sort(o[:, :K], axis=1), np.sort(o[:, C - K:], axis=1)
def edit(hi, lo):
    e = []
    for g in range(8):
        stay = np.delete(np.arange(C), lo[g])
        key = np.concatenate([2 * stay, 2 * hi[g] + 1])
        e.append(np.concatenate([stay, C + np.arange(K)])[np.argsort(key)])
    return np.stack(e)
def numbers_of(rng):
    return {"x": np.array(f(rng, N, 128, 4 * C)), "u": np.array(f(rng, N, 128, 512)), "v": np.array(f(rng, N, 128, 512))}
def weights(rng, w, z):
    wc, ws = packed(w, rng)
    zc, zs = packed(z, rng)
    return {"wc": wc, "ws": ws, "zc": zc, "zs": zs}
def still(rng):
    w = np.zeros((N, 128, 4, 128, 4), np.float32)
    i = np.arange(128)
    for b in range(4): w[:, i, b, i, b] = 64
    return weights(rng, w.reshape(N, 128, 2048).astype(BF), np.zeros((N, 128, 2048), BF))
def signs(rng):
    return np.stack([rng.permutation(8) % 2 * 2.0 - 1.0 for r in range(N)])
def marks():
    n = np.arange(K)
    h = C - 2 * K
    v = np.ones((8, C), np.float32)
    cases = ((n, h + K + n), (h + K + n, n), (2 * n, 2 * n + 1), (2 * n + 1, 2 * n), (h + 2 * n, h + 2 * n + 1), (h + 2 * n + 1, h + 2 * n), (n, K + n), (K + n, n))
    for g in range(8):
        v[g, cases[g][0]] = 4
        v[g, cases[g][1]] = -2
    return v
def setup_inputs(rng):
    return {**numbers_of(rng), **weights(rng, f(rng, N, 128, 2048), f(rng, N, 128, 2048))}
def setup_inputs_ties(rng):
    d = numbers_of(rng)
    e = rng.permutation(N)
    x = d["x"].reshape(N, 8, 16, C, 4)
    for r in range(N):
        k = np.zeros(C, int) if r == e[0] else rng.permutation(C) % 3
        a = x[r][:, :8, :3].copy()
        a[:, :, 2] = 0
        x[r][:, :8] = a[:, :, k]
    x[e[1]] = 0
    u = d["u"].reshape(N, 8, 16, 128, 4)
    u[:, :, 8:, ::16] = 0
    w = np.array(f(rng, N, 128, 2048)).reshape(N, 8, 16, 4, 8, 16, 4)
    z = np.array(f(rng, N, 128, 2048)).reshape(N, 8, 16, 4, 8, 16, 4)
    for a in (w, z): a[:, :, 8:, :, :, :8] = 0
    return {"x": x.reshape(N, 128, 4 * C), "u": u.reshape(N, 128, 512), "v": d["v"], **weights(rng, w.reshape(N, 128, 2048), z.reshape(N, 128, 2048))}
def setup_inputs_ends(rng):
    d = numbers_of(rng)
    x = d["x"].reshape(N, 8, 16, C, 4)
    u = d["u"].reshape(N, 8, 16, 128, 4)
    x[:, :, 0] = 0
    u[:, :, :, ::16] = 0
    for r in range(N): x[r, :, 0, :, 0] = marks()[rng.permutation(8)].astype(BF)
    for g in range(8): u[:, g, 0, 16 * g, 0] = 1
    w = f(rng, N, 128, 2048).astype(np.float32).reshape(N, 8, 16, 4, 8, 16, 4)
    z = f(rng, N, 128, 2048).astype(np.float32).reshape(N, 8, 16, 4, 8, 16, 4)
    for a in (w, z):
        a[:, :, 15] = 0
        a[:, :, :, :, :, 15] *= np.float32(8192)
    return {**d, "x": x.reshape(N, 128, 4 * C), "u": u.reshape(N, 128, 512), **weights(rng, w.reshape(N, 128, 2048).astype(BF), z.reshape(N, 128, 2048).astype(BF))}
def setup_inputs_near(rng):
    d = numbers_of(rng)
    x = d["x"].astype(np.float32).reshape(N, 8, 16, C, 4)
    s = np.minimum((np.arange(C) + 1) // 2, 255)
    g = ((s[:, None] >> np.arange(8)) & 1) * np.exp2(np.arange(8) - 23.0)
    x[:, :, 0] = 0
    x[:, :, 0, :, 0] = signs(rng)[:, :, None]
    for r in rng.permutation(N)[:N // 2]:
        x[r, :, 0, C - 1, 0] = 16
        x[r, :, 0, 0, 0] = -16
    x[:, :, 8] = g[:, :4]
    x[:, :, 9] = g[:, 4:]
    x[:, :, 10:] = rng.integers(4, 8, (N, 8, 6, C, 4)) * rng.choice([-1.0, 1.0], (N, 8, 6, C, 4)) * 2.0 ** -20
    k = np.exp2(-1.0 * rng.permutation(np.arange(N) * 30 // (N - 1))).astype(np.float32).astype(BF)
    u = d["u"].reshape(N, 128, 128, 4)
    u[:, :, ::16] = 0
    for h in range(0, 128, 16):
        u[:, h, h, 0] = k
        u[:, h + 8:h + 10, h] = k[:, None, None]
    return {"x": x.reshape(N, 128, 4 * C).astype(BF), "u": u.reshape(N, 128, 512), "v": d["v"], **still(rng)}
def setup_inputs_huge(rng):
    d = numbers_of(rng)
    x = 2.0 ** 30 * (0.6 + 0.4 * rng.random((N, 128, C, 4)))
    c = np.stack([rng.permutation(C) % 2 * 2.0 - 1.0 for r in range(N)])
    c[rng.permutation(N) < N // 2] = 1
    x *= c[:, None, :, None]
    u = d["u"].reshape(N, 128, 128, 4)
    a = 2.0 ** 30 * (1 - 0.25 * rng.random((N, 128, 8, 4))) * signs(rng)[:, None, :, None]
    u[:, :, ::16] = a.astype(np.float32).astype(BF)
    return {"x": x.astype(np.float32).reshape(N, 128, 4 * C).astype(BF), "u": u.reshape(N, 128, 512), "v": d["v"], **still(rng)}
def setup_inputs_spread(rng):
    d = setup_inputs(rng)
    d["x"] = wide(rng, N, 128, 4 * C, cols=6)
    return d
def check_inputs(d):
    b = []
    for k in ("x", "u", "v"):
        a = np.abs(d[k].astype(np.float32))
        if not (np.isfinite(a).all() and ((a == 0) | (a >= 2.0 ** -30) & (a <= 2.0 ** 30)).all()): b.append("a value of " + k)
    return b
def reference(x, u, v, wc, ws, zc, zs):
    qu = [mx_ref.quantize(u[r]) for r in range(N)]
    w, z = [pk(wc[r], ws[r]) for r in range(N)], [pk(zc[r], zs[r]) for r in range(N)]
    now = [x[r] for r in range(N)]
    behind = (np.arange(C) + 1) % C
    ol = np.zeros((N, 8, C), np.float32)
    for t in range(R):
        hi, lo, border = [], [], []
        for r in range(N):
            h, l = choose(mx_ref.matmul(qu[r], mx_ref.quantize(now[r])))
            hi.append(h)
            lo.append(l)
            border.append(mx_ref.quantize(gcols(now[r], l)))
        came = decode(join(*border)).astype(BF)
        for r in range(N):
            a = (r - 1) % N
            e = edit(hi[r], lo[r])
            q = mx_ref.quantize(gcols(np.concatenate([now[r], cut(came, a, 4 * K)], axis=1), e))
            made = []
            for b in range(4):
                c = np.arange(128 * b, 128 * b + 128)
                made.append((mx_ref.matmul(pick(w[r], c), q) + mx_ref.matmul(pick(z[r], c), q)[:, behind]) * np.float32(0.015625))
            now[r] = tile(made)
            ol[r] = np.take_along_axis(np.concatenate([np.tile(np.arange(C), (8, 1)), C + lo[a]], axis=1), e, axis=1)
    y = np.zeros((N, 128, C), np.float32)
    oc, osc = np.zeros((N, 128, 4 * C), np.uint8), np.zeros((N, 16, C), np.uint8)
    for r in range(N):
        q = mx_ref.quantize(now[r])
        y[r] = mx_ref.matmul(mx_ref.quantize(v[r]), q)
        oc[r], osc[r] = emit(q)
    return {"y": y, "ol": ol, "oc": oc, "osc": osc}

@@ -1,0 +1,441 @@
+from concourse.mybir import dt, AluOpType, ActivationFunctionType
+
+A, F = AluOpType, ActivationFunctionType
+C, K, R = 384, 64, 3
+H = C // 2
+Q4, U8, BF, F32, I32, U16, F16 = "float8_e4m3fn_x4", "uint8", "bfloat16", "float32", "int32", "uint16", "float16"
+
+
+def _sb(n, d):
+    return ("sbuf", [128, n], d)
+
+
+SCRATCH = {
+    "ut": _sb(512, BF), "vt": _sb(512, BF),
+    "quc": _sb(128, Q4), "qus": _sb(128, U8), "puc": _sb(384, Q4), "pus": _sb(384, U8),
+    "qvc": _sb(128, Q4), "qvs": _sb(128, U8),
+    "wq": _sb(512, Q4), "wp": _sb(512, U8), "zq": _sb(512, Q4), "zp": _sb(512, U8),
+    "gt": _sb(516, BF), "ones": _sb(516, BF), "ec": _sb(512, Q4), "es": _sb(512, U8),
+    "ci": _sb(48, I32), "cu": _sb(48, U16), "pi": _sb(24, I32), "pj": _sb(24, I32), "pu": _sb(24, U16), "qf": _sb(2, F32),
+    "ia": _sb(24, F32), "il": _sb(24, F32), "ip": _sb(4, F32), "c2": _sb(4, F32),
+    "im": _sb(16, I32), "im2": _sb(16, I32), "c16": _sb(16, F32), "m16": _sb(16, F32),
+    "msk": _sb(C, BF), "ctl": _sb(C, BF), "ctl2": _sb(C, BF),
+    "zero": _sb(C, BF), "io448": _sb(C + K, BF), "ow": _sb(C + K, F32),
+    "qxc": _sb(C, Q4), "qxs": _sb(C, U8), "pt": _sb(C, F32),
+    "flg": _sb(11 * C, BF), "sj": _sb(11 * H, BF), "sg": _sb(14 * C, BF), "acc": _sb(13, F32),
+    "z4": _sb(48, F32), "yc": _sb(48, F32), "rb": _sb(2, F32),
+    "k1l": _sb(C, F16), "yl": _sb(C, F16), "k1h": _sb(C, BF), "yh": _sb(C, BF),
+    "mxl": _sb(H, F16), "mnl": _sb(H, F32), "mxh": _sb(H, BF), "mnh": _sb(H, BF), "sml": _sb(4, F32), "smh": _sb(4, BF),
+    "dl": _sb(4, F32), "dh": _sb(4, F32), "dm": _sb(4, F32), "sgl": _sb(4 * C, BF), "sgh": _sb(4 * C, BF), "sgm": _sb(4 * K, BF),
+    "lo": _sb(20, U16), "chl": _sb(K, BF), "bt": _sb(512, BF),
+    "qbc": _sb(R * 128, Q4), "qbs": _sb(R * 128, U8), "landc": _sb(320, Q4), "lands": _sb(320, U8),
+    "lsend": _sb(K, BF), "lland": _sb(K, BF),
+    "cva": _sb(C, BF), "cvb": _sb(C, BF), "cvc": _sb(C, BF),
+    "t1": _sb(24, F32), "bq": _sb(24, F32), "lm": _sb(24, F32), "lm2": _sb(24, F32), "pp": _sb(24, F32), "oo": _sb(24, F32),
+    "ou": _sb(24, U16), "a1": _sb(4, F32), "a2": _sb(4, F32), "au": _sb(4, U16),
+    "ew": _sb(2 * C + K, BF), "em": _sb(C, BF), "ex": _sb(C, BF), "eo": _sb(120, U16),
+    "ta": _sb(4 * 208, BF), "tb": _sb(4 * 196, BF),
+    "qtc": _sb(4 * H, Q4), "qts": _sb(4 * H, U8),
+    "ysb": _sb(C, F32), "olb": _sb(C, F32),
+}
+for _s in ("l", "h"):
+    for _n in ("f", "pf", "eq", "s1", "x1", "x2"):
+        SCRATCH[_n + _s] = _sb(C, BF)
+    SCRATCH["cn" + _s] = _sb(C + 16, BF)
+for _r in range(R + 1):
+    SCRATCH["xw%d" % _r] = _sb(4 * (C + K), BF)
+for _b in range(8):
+    SCRATCH["ps%d" % _b] = ("psum", [128, 512], F32)
+
+_NDMA = 17
+SEMAPHORES = ["sv", "ss", "sp", "sq", "sent", "arr0", "arr1", "arr2", "arrl"] + ["d%d" % _i for _i in range(_NDMA)]
+
+
+def rank_program(g, core, T, topo):
+    rank = T.rank_of(core)
+    if rank is None:
+        return
+    nxt = T.cores[(rank + 1) % len(T.cores)]
+    rid, pid = topo.addr(nxt)[0], topo.addr(nxt)[1]
+    mask = topo.mask(core, nxt)
+    neng = len(topo.engines(core, nxt))
+
+    queue = {"v": g.vector, "s": g.scalar, "p": g.tensor, "q": g, "y": g.sync}
+    semof = {"v": "sv", "s": "ss", "p": "sp", "q": "sq"}
+    count = {}
+    waited = {k: {} for k in queue}
+    lastw, readers = {}, {}
+    ndma = [0]
+
+    def wait(e, tok):
+        if waited[e].get(tok[0], 0) < tok[1]:
+            queue[e].wait_ge(T.sem[tok[0]], tok[1])
+            waited[e][tok[0]] = tok[1]
+
+    def before(e, rd, wr, chain=False):
+        need = {}
+        for k in rd:
+            if k in lastw:
+                need[lastw[k][0]] = max(need.get(lastw[k][0], 0), lastw[k][1])
+        for k in wr:
+            toks = list(readers.get(k, []))
+            if k in lastw and not chain:
+                toks.append(lastw[k])
+            for t in toks:
+                need[t[0]] = max(need.get(t[0], 0), t[1])
+        for s in need:
+            wait(e, (s, need[s]))
+
+    def after(tok, rd, wr):
+        for k in rd:
+            readers.setdefault(k, []).append(tok)
+        for k in wr:
+            lastw[k] = tok
+            readers[k] = []
+
+    def op(e, make, rd, wr, chain=False):
+        wr = list(wr) + [k for k in rd if k.startswith("ps")]
+        before(e, rd, wr, chain)
+        s = semof[e]
+        count[s] = count.get(s, 0) + 1
+        make().then_inc(T.sem[s], 1)
+        after((s, count[s]), rd, wr)
+
+    def dma(e, out, in_, rd, wr):
+        before(e, rd, wr)
+        s = "d%d" % ndma[0]
+        ndma[0] += 1
+        queue[e].dma_start(out, in_).then_inc(T.sem[s], 16)
+        count[s] = 16
+        after((s, 16), rd, wr)
+
+    def send(out, in_, sem, rd):
+        before("q", rd, [])
+        g.remote_dma(out, in_, T.sem[sem], T.sem.sent, pid, rid, mask)
+        count["sent"] = count.get("sent", 0) + neng
+        count[sem] = count.get(sem, 0) + neng
+
+    V, S, P = g.vector, g.scalar, g.tensor
+
+    def ts(out, in0, s1, s2, o0, o1, rd, wr):
+        if o1 is None:
+            op("v", lambda: V.tensor_scalar(out, in0, s1, None, o0), rd, wr)
+        else:
+            op("v", lambda: V.tensor_scalar(out, in0, s1, s2, o0, o1), rd, wr)
+
+    def tt(out, a, b, o, rd, wr):
+        op("v", lambda: V.tensor_tensor(out, a, b, o), rd, wr)
+
+    def cp(out, in_, rd, wr):
+        op("v", lambda: V.tensor_copy(out, in_), rd, wr)
+
+    def scan(out, d0, d1, init, o0, o1, rd, wr):
+        op("v", lambda: V.tensor_tensor_scan(out, d0, d1, init, o0, o1), rd, wr)
+
+    def quant(oc, osc, in_, rd, wr):
+        op("v", lambda: V.quantize_mx(oc, osc, in_), rd, wr)
+
+    def act(out, in_, func, rd, wr, **kw):
+        op("s", lambda: S.activation(out, in_, func, **kw), rd, wr)
+
+    def mm(bank, n, lc, ls, rc, rs, start, stop, rd):
+        op("p", lambda: P.matmul_mx(T["ps%d" % bank][:, 0:n], lc, ls, rc, rs, start, stop), rd, ["ps%d" % bank], chain=not start)
+
+    def iota(out, pat, base, cm, wr, fl=False):
+        if fl:
+            op("q", lambda: g.iota(out, pat, base, cm, allow_small_or_imprecise_dtypes=True), [], wr)
+        else:
+            op("q", lambda: g.iota(out, pat, base, cm), [], wr)
+
+    def fill(ap, c, wr):
+        op("v", lambda: V.memset(ap, c), [], wr)
+
+    def xkeys(r, halves=(0, 1)):
+        return ["x%d_%d_%d" % (r, h, b) for h in halves for b in range(4)]
+
+    dma("s", T.ut[:], T.u[:], [], ["ut"])
+    dma("y", T.xw0[:, 0:4 * H], T.x[:, 0:4 * H], [], xkeys(0, (0,)))
+    dma("y", T.xw0[:, 4 * H:4 * C], T.x[:, 4 * H:4 * C], [], xkeys(0, (1,)))
+    dma("y", T.wq[:].bitcast(dt.uint8), T.wc[:], [], ["wq"])
+    dma("y", T.zq[:].bitcast(dt.uint8), T.zc[:], [], ["zq"])
+    dma("y", T.wp[:], T.ws[:], [], ["wp"])
+    dma("y", T.zp[:], T.zs[:], [], ["zp"])
+    dma("y", T.vt[:], T.v[:], [], ["vt"])
+
+    btk = ["bt0", "bt1", "bt2", "bt3"]
+    iota(T.pi[:], [[0, 24]], 0, 1, ["pi"])
+    iota(T.im[:], [[1, 16]], 0, -1, ["im"])
+    iota(T.ci[:, 0:8], [[16, 8]], 0, 0, ["ci0"])
+    iota(T.ci[:, 8:16], [[32, 4], [0, 2]], 0, 0, ["ci1"])
+    iota(T.ci[:, 16:24], [[32, 4], [0, 2]], 16, 0, ["ci2"])
+    iota(T.ci[:, 24:48], [[1, 12], [12, 2]], 0, 0, ["ci3"])
+    iota(T.ia[:], [[16, 24]], 0, 0, ["ia"], True)
+    fill(T.ones[:], 1.0, ["ones"])
+    fill(T.bt[:], 0.0, btk)
+    fill(T.zero[:], 0.0, ["zero"])
+    fill(T.ctl2[:], -256.0, ["ctl2"])
+    fill(T.cnl[:, 0:16], 0.0, ["cnl"])
+    fill(T.cnh[:, 0:16], 0.0, ["cnh"])
+    fill(T.ctl2[:, 0:C:16], 768.0, ["ctl2"])
+    op("q", lambda: g.affine_select(T.gt[:], T.ones[:], [[1, 516]], A.is_equal, 0.0, -3, -4), ["ones"], ["gt"])
+    iota(T.io448[:], [[1, C + K]], -192, 0, ["io448"], True)
+    iota(T.ow[:, 0:C], [[1, C]], 0, 0, ["ow0"], True)
+    quant(T.landc[:, 64:192], T.lands[:, 64:192], T.bt[:], btk, ["landz"])
+    ts(T.pj[:], T.pi[:], 15, None, A.bitwise_and, None, ["pi"], ["pj"])
+    ts(T.im2[:], T.im[:], 15, None, A.bitwise_and, None, ["im"], ["im2"])
+    cp(T.pu[:], T.pj[:], ["pj"], ["pu"])
+    ts(T.c16[:], T.im2[:], 15.0, 128.0, A.is_equal, A.mult, ["im2"], ["c16"])
+    ts(T.m16[:], T.im2[:], 0.0, 1024.0, A.not_equal, A.mult, ["im2"], ["m16"])
+    cp(T.qf[:], T.pj[:, 0:2], ["pj"], ["qf"])
+    cp(T.cu[:], T.ci[:], ["ci0", "ci1", "ci2", "ci3"], ["cu"])
+    ts(T.il[:], T.ia[:], T.qf[:, 0:1], None, A.add, None, ["ia", "qf"], ["il"])
+    act(T.ctl[:], T.c16[:].indirect(T.pu[:]), F.Copy, ["c16", "pu"], ["ctl"])
+    quant(T.quc[:], T.qus[:], T.ut[:], ["ut"], ["qu"])
+    act(T.pus[:], T.qus[:].indirect(T.cu[:, 0:24]), F.Copy, ["qu", "cu"], ["pus"])
+    cp(T.puc[:].bitcast(dt.uint32), T.quc[:].bitcast(dt.uint32).indirect(T.cu[:, 0:24]), ["qu", "cu"], ["puc"])
+    act(T.msk[:], T.m16[:].indirect(T.pu[:]), F.Identity, ["m16", "pu"], ["msk"], bias=-256.0)
+    act(T.ip[:], T.il[:, 0:4], F.Identity, ["il"], ["ip"], bias=0.5)
+    act(T.c2[:], T.il[:, 0:4], F.Identity, ["il"], ["c2"], bias=322.0, scale=2.0)
+
+    def qx(r, h):
+        quant(T.qxc[:, H * h:H * h + H], T.qxs[:, H * h:H * h + H], T["xw%d" % r][:, 4 * H * h:4 * H * (h + 1)], xkeys(r, (h,)), ["qx%d" % h])
+
+    def score(bank, j, c0, c1, rd):
+        mm(bank, c1 - c0, T.puc[:, 128 * j:128 * j + 128], T.pus[:, 128 * j:128 * j + 128], T.qxc[:, c0:c1], T.qxs[:, c0:c1], True, True, ["puc", "pus"] + rd)
+
+    def turn(bank, h):
+        op("v", lambda: V.transpose(T.pt[:, H * h:H * h + H], T["ps%d" % bank][:, 0:H]), ["ps%d" % bank], ["pt%d" % h])
+
+    def cut(s):
+        y, f, pf, eq, s1, x1, x2, cn, sm = [T[n + s] for n in ("y", "f", "pf", "eq", "s1", "x1", "x2", "cn", "sm")]
+        mx, mn = T["mx" + s], T["mn" + s]
+        o = A.max if s == "l" else A.min
+        k = lambda *a: [n + s for n in a]
+        return {
+            "y": lambda: op("v", lambda: V.transpose(y[:], T["k1" + s][:]), k("k1"), k("y")),
+            "f": lambda: ts(f[:], y[:], 0.0, 0.5, A.is_gt, A.mult, k("y"), k("f")),
+            "mx": lambda: scan(mx[:], y[:, 0:H], y[:, H:C], -1.0, A.max, A.max, k("y"), k("mx")),
+            "mn": lambda: scan(mn[:], y[:, 0:H], y[:, H:C], 1.0, A.min, A.min, k("y"), k("mn")),
+            "pf": lambda: scan(pf[:], f[:], T.zero[:], -96.0, A.add, A.add, k("f") + ["zero"], k("pf")),
+            "sg": lambda: ts(sm[:, 0:1], pf[:, C - 1:C], -64.0, 0.5, A.is_ge, A.subtract, k("pf"), k("sg")),
+            "ty": lambda: ts(sm[:, 1:2], mx[:, H - 1:H], sm[:, 0:1], mn[:, H - 1:H], A.min, A.max, k("mx", "mn", "sg"), k("ty")),
+            "m2": lambda: ts(sm[:, 2:3], pf[:, C - 1:C], 32.0, -96.0, A.subtract, o, k("pf"), k("m2")),
+            "eq": lambda: ts(eq[:], y[:], sm[:, 1:2], sm[:, 0:1], A.is_equal, A.mult, k("y", "ty", "sg"), k("eq")),
+            "x2": lambda: ts(x2[:], pf[:], sm[:, 2:3], 2.0, A.subtract, A.mult, k("pf", "m2"), k("x2")),
+            "s1": lambda: scan(s1[:], f[:], eq[:], -96.0, A.add, A.subtract, k("f", "eq"), k("s1")),
+            "m1": lambda: ts(sm[:, 3:4], s1[:, C - 1:C], 32.0, -96.0, A.subtract, o, k("s1"), k("m1")),
+            "x1": lambda: ts(x1[:], s1[:], sm[:, 3:4], 2.0, A.subtract, A.mult, k("s1", "m1"), k("x1")),
+            "cn": lambda: scan(cn[:, 16:C + 16], x1[:], x2[:], 0.0, A.max, o, k("x1", "x2"), k("cn")),
+        }
+
+    def wrap(out, src, key, okey):
+        scan(out[:], src, T.ctl[:], 128.0, A.min, A.add, [key, "ctl"], [okey])
+
+    qx(0, 0)
+    score(0, 0, 0, H, ["qx0"])
+    qx(0, 1)
+    turn(0, 0)
+
+    for r in range(R):
+        last = r == R - 1
+        X, XN = T["xw%d" % r], T["xw%d" % (r + 1)]
+        xk = xkeys(r)
+        score(2, 2, 0, C, ["qx0", "qx1"])
+        score(1, 1, 0, C, ["qx0", "qx1"])
+        score(3, 0, H, C, ["qx1"])
+        score(4, 2, 0, C, ["qx0", "qx1"])
+        if r == 0:
+            for b in range(4):
+                quant(T.ec[:, 128 * b:128 * b + 128], T.es[:, 128 * b:128 * b + 128], T.gt[:, 3 - b:515 - b], ["gt"], ["e%d" % b])
+
+        def cmp(b):
+            ts(T.flg[:, C * b:C * b + C], T.ps2[:, 0:C], T.pt[:, 32 * b + 16:32 * b + 17], None, A.is_gt, None, ["ps2", "pt%d" % (b // 6)], ["flg%d" % b])
+
+        def cnt(b):
+            scan(T.sj[:, H * b:H * b + H], T.flg[:, C * b:C * b + H], T.flg[:, C * b + H:C * b + C], -192.0, A.add, A.add, ["flg%d" % b], ["sj%d" % b])
+
+        def sgn(b):
+            act(T.sg[:, C * b:C * b + C], T.ps1[:, 0:C], F.Sign, ["ps1", "pt%d" % (b // 6)], ["sg%d" % b, "acc%d" % b],
+                bias=T.pt[:, 32 * b:32 * b + 1], scale=-1.0, accum_out=T.acc[:, b:b + 1])
+
+        written = {k: lastw[k] for k in ("ps1", "ps2")}
+        for b in range(12):
+            if b < 11:
+                cmp(b)
+            if b == 0:
+                turn(3, 1)
+            else:
+                cnt(b - 1)
+            if b == 10:
+                act(T.sg[:, C * 12:C * 13], T.ps4[:, 0:C], F.Sign, ["ps4", "pt1"], ["sg12"], bias=T.pt[:, 32 * 11 + 16:32 * 11 + 17], scale=-1.0)
+            if b == 11:
+                act(T.sg[:, C * 13:C * 14], T.sg[:, C * 12:C * 13], F.Relu, ["sg12"], ["sg13", "acc12"], scale=-1.0, accum_out=T.acc[:, 12:13])
+            sgn(b)
+            for k, n in (("ps1", 11), ("ps2", 10)):
+                if b < n:
+                    readers[k] = []
+                    lastw[k] = written[k]
+        acck, sjk = ["acc%d" % b for b in range(12)], ["sj%d" % b for b in range(11)]
+        act(T.z4[:, 23:24], T.acc[:, 12:13], F.Identity, ["acc12"], ["z4e"], bias=-2562.0, scale=8.0)
+        act(T.z4[:, 47:48], T.acc[:, 12:13], F.Identity, ["acc12"], ["z4f"], bias=506.0, scale=-8.0)
+        act(T.z4[:, 0:12], T.acc[:, 0:12], F.Identity, acck, ["z4a"], bias=-1030.0, scale=-4.0)
+        act(T.z4[:, 24:36], T.acc[:, 0:12], F.Identity, acck, ["z4c"], bias=-1026.0, scale=4.0)
+        ts(T.z4[:, 12:23], T.sj[:, H - 1:11 * H:H], 8.0, -1026.0, A.mult, A.add, sjk, ["z4b"])
+        ts(T.z4[:, 36:47], T.sj[:, H - 1:11 * H:H], -8.0, -1030.0, A.mult, A.add, sjk, ["z4d"])
+        op("v", lambda: V.reciprocal(T.yc[:], T.z4[:]), ["z4" + c for c in "abcdef"], ["yc"])
+        act(T.k1h[:], T.yc[:, 24:48].indirect(T.cu[:, 24:48]), F.Copy, ["yc", "cu"], ["k1h"])
+        cp(T.k1l[:], T.yc[:, 0:24].indirect(T.cu[:, 24:48]), ["yc", "cu"], ["k1l"])
+
+        lo, hi = cut("l"), cut("h")
+        for n in ("y", "f", "mx", "pf", "mn", "sg", "ty", "eq", "s1", "m1", "x1"):
+            lo[n]()
+        act(T.rb[:, 0:1], T.pfl[:, C - 1:C], F.Relu, ["pfl"], ["rb0"], bias=128.0, scale=2.0)
+        act(T.rb[:, 1:2], T.rb[:, 0:1], F.Identity, ["rb0"], ["rb1"], bias=192.0, scale=-1.0)
+        act(T.x2l[:], T.pfl[:], F.Identity, ["pfl", "rb1"], ["x2l"], bias=T.rb[:, 1:2], scale=2.0)
+        lo["cn"]()
+        CLi, CLe, CHi, CHe = T.cnl[:, 16:C + 16], T.cnl[:, 15:C + 15], T.cnh[:, 16:C + 16], T.cnh[:, 15:C + 15]
+        for k in range(4):
+            act(T.sgl[:, C * k:C * k + C], CLi, F.Sign, ["cnl", "ip"], ["sgl%d" % k, "dl%d" % k], bias=T.ip[:, k:k + 1], scale=-1.0, accum_out=T.dl[:, k:k + 1])
+        dlk = ["dl%d" % k for k in range(4)]
+
+        hi["y"]()
+        wrap(T.cva, CLi, "cnl", "cva")
+        hi["f"]()
+        wrap(T.cvb, CLe, "cnl", "cvb")
+        hi["mx"]()
+        hi["pf"]()
+        hi["mn"]()
+        hi["sg"]()
+        tt(T.t1[:], T.cva[:, 15:C:16], T.cvb[:, 15:C:16], A.subtract, ["cva", "cvb"], ["t1"])
+        hi["ty"]()
+        hi["m2"]()
+        hi["eq"]()
+        for t in range(4):
+            ts(T.lo[:, 4 * t:4 * t + 4], T.dl[:], 2.0, 768.0 + t, A.mult, A.add, dlk, ["lo%d" % t])
+            act(T.bt[:, t:4 * K:4], X[:, 0:4 * C].indirect(T.lo[:, 4 * t:4 * t + 4]), F.Copy, xk + ["lo%d" % t], ["bt%d" % t])
+        ts(T.lo[:, 16:20], T.dl[:], 0.5, 192.0, A.mult, A.add, dlk, ["lo4"])
+        hi["s1"]()
+        hi["x2"]()
+        hi["m1"]()
+        quant(T.qbc[:, 128 * r:128 * r + 128], T.qbs[:, 128 * r:128 * r + 128], T.bt[:], btk, ["qb%d" % r])
+        l0 = (0, 192, 256)[r]
+        send(T.landc[:, l0:l0 + K].bitcast(dt.uint8), T.qbc[:, 128 * r:128 * r + K].bitcast(dt.uint8), "arr%d" % r, ["qb%d" % r])
+        send(T.lands[:, l0:l0 + K], T.qbs[:, 128 * r:128 * r + K], "arr%d" % r, ["qb%d" % r])
+        lastw["land%d" % r] = ("arr%d" % r, 2 * neng)
+        if last:
+            act(T.lsend[:], T.io448[:, 0:C].indirect(T.lo[:, 16:20]), F.Copy, ["io448", "lo4"], ["lsend"])
+            send(T.lland[:], T.lsend[:], "arrl", ["lsend"])
+            lastw["lland"] = ("arrl", neng)
+        hi["x1"]()
+        ts(T.lm[:], T.t1[:], 512.0, -64.0, A.mult, A.add, ["t1"], ["lm"])
+        hi["cn"]()
+        tt(T.bq[:], T.il[:], T.cvb[:, 15:C:16], A.subtract, ["il", "cvb"], ["bq"])
+        wrap(T.cvc, CHe, "cnh", "cvc")
+        tt(T.lm2[:], T.lm[:], T.il[:], A.add, ["lm", "il"], ["lm2"])
+        act(T.chl[:], CHi.indirect(T.lo[:, 16:20]), F.Copy, ["cnh", "lo4"], ["chl"])
+        for k in range(4):
+            act(T.sgh[:, C * k:C * k + C], CHi, F.Sign, ["cnh", "ip"], ["sgh%d" % k, "dh%d" % k], bias=T.ip[:, k:k + 1], scale=-1.0, accum_out=T.dh[:, k:k + 1])
+        for k in range(4):
+            act(T.sgm[:, K * k:K * k + K], T.chl[:], F.Sign, ["chl", "ip"], ["sgm%d" % k, "dm%d" % k], bias=T.ip[:, k:k + 1], scale=-1.0, accum_out=T.dm[:, k:k + 1])
+        tt(T.pp[:], T.cvc[:, 15:C:16], T.bq[:], A.add, ["cvc", "bq"], ["pp"])
+        tt(T.oo[:], T.pp[:], T.lm2[:], A.max, ["pp", "lm2"], ["oo"])
+        cp(T.ou[:], T.oo[:], ["oo"], ["ou"])
+        cp(T.ew[:].indirect(T.ou[:]), T.io448[:, 0:C], ["ou", "io448"], ["ew"])
+        tt(T.a1[:], T.dh[:], T.dm[:], A.subtract, ["dh%d" % k for k in range(4)] + ["dm%d" % k for k in range(4)], ["a1"])
+        tt(T.a2[:], T.a1[:], T.c2[:], A.add, ["a1", "c2"], ["a2"])
+        ts(T.au[:], T.a2[:], 0.5, None, A.mult, None, ["a2"], ["au"])
+        cp(T.ew[:].indirect(T.au[:]), T.io448[:, C:C + K], ["au", "io448"], ["ew"])
+        tt(T.em[:], T.ew[:, 0:C], T.msk[:], A.max, ["ew", "msk"], ["em"])
+        scan(T.ex[:], T.ctl2[:], T.em[:], 0.0, A.max, A.min, ["em", "ctl2"], ["ex"])
+
+        v0 = (0, 128, 192)[r]
+        lk = ["land%d" % r, "landz"] + (["land1"] if r == 2 else [])
+        for b in range(4):
+            mm(4 + b, 128, T.ec[:, 128 * b:128 * b + 128], T.es[:, 128 * b:128 * b + 128], T.landc[:, v0:v0 + 128], T.lands[:, v0:v0 + 128], True, True, ["e%d" % b] + lk)
+            act(X[:, 4 * C + b:4 * (C + K):4], T["ps%d" % (4 + b)][:, l0 - v0:l0 - v0 + K], F.Copy, ["ps%d" % (4 + b)], ["xa%d_%d" % (r, b)])
+        wk = xk + ["xa%d_%d" % (r, b) for b in range(4)]
+
+        for t in (2, 3, 0, 1):
+            ts(T.eo[:, 24 * t:24 * t + 24], T.ex[:, 15:C:16], 4.0, 768.0 + t, A.mult, A.add, ["ex"], ["eo%d" % t])
+
+        def gather(e, h, t):
+            if h == 0:
+                out, off, key = T.ta[:, t:4 * 208:4], T.eo[:, 24 * t:24 * t + 13], "ta%d" % t
+            else:
+                out, off, key = T.tb[:, t:4 * H:4], T.eo[:, 24 * t + 12:24 * t + 24], "tb%d" % t
+            if e == "v":
+                cp(out, X[:].indirect(off), wk + ["eo%d" % t], [key])
+            else:
+                act(out, X[:].indirect(off), F.Copy, wk + ["eo%d" % t], [key])
+
+        def qt(h, rot):
+            i = 2 * h + rot
+            src = T.ta if h == 0 else T.tb
+            rd = ["ta%d" % t for t in range(4)] if h == 0 else ["tb%d" % t for t in range(4)] + (["tbw"] if rot else [])
+            quant(T.qtc[:, H * i:H * i + H], T.qts[:, H * i:H * i + H], src[:, 4 * rot:4 * rot + 4 * H], rd, ["qt%d" % i])
+
+        def layer(h):
+            for tap, b in ((0, 0), (0, 1), (1, 0), (1, 1), (0, 2), (1, 2), (0, 3), (1, 3)):
+                i = 2 * h + tap
+                wq, wp, kk = (T.wq, T.wp, ["wq", "wp"]) if tap == 0 else (T.zq, T.zp, ["zq", "zp"])
+                mm(4 * h + b, H, wq[:, 128 * b:128 * b + 128], wp[:, 128 * b:128 * b + 128], T.qtc[:, H * i:H * i + H], T.qts[:, H * i:H * i + H], tap == 0, tap == 1, kk + ["qt%d" % i])
+
+        def evac(e, h, b):
+            out, ps, key = XN[:, 4 * H * h + b:4 * H * (h + 1):4], "ps%d" % (4 * h + b), "x%d_%d_%d" % (r + 1, h, b)
+            if e == "v":
+                ts(out, T[ps][:, 0:H], 0.015625, None, A.mult, None, [ps], [key])
+            else:
+                act(out, T[ps][:, 0:H], F.Copy, [ps], [key], scale=0.015625)
+
+        gather("s", 0, 2)
+        gather("s", 0, 3)
+        gather("v", 0, 0)
+        gather("v", 0, 1)
+        if last:
+            ts(T.eo[:, 96:120], T.ex[:, 15:C:16], 192.0, None, A.add, None, ["ex"], ["eo4"])
+        qt(0, 0)
+        qt(0, 1)
+        layer(0)
+        gather("s", 1, 2)
+        gather("s", 1, 3)
+        gather("v", 1, 0)
+        gather("s", 1, 1)
+        act(T.tb[:, 4 * H:4 * H + 4], T.ta[:, 0:4], F.Copy, ["ta%d" % t for t in range(4)], ["tbw"])
+        qt(1, 0)
+        qt(1, 1)
+        layer(1)
+        evac("s", 0, 0)
+        evac("s", 0, 1)
+        evac("v", 0, 2)
+        evac("s", 0, 3)
+        if r == 0:
+            quant(T.qvc[:], T.qvs[:], T.vt[:], ["vt"], ["qv"])
+        if last:
+            act(T.ow[:, C:C + K], T.lland[:], F.Identity, ["lland"], ["ow1"], bias=576.0)
+        qx(r + 1, 0)
+        evac("s", 1, 0)
+        evac("v", 1, 1)
+        evac("s", 1, 2)
+        if not last:
+            score(0, 0, 0, H, ["qx0"])
+            evac("v", 1, 3)
+            qx(r + 1, 1)
+            turn(0, 0)
+        else:
+            mm(0, H, T.qvc[:], T.qvs[:], T.qxc[:, 0:H], T.qxs[:, 0:H], True, True, ["qv", "qx0"])
+            dma("y", T.oc[:, 0:4 * H], T.qxc[:, 0:H].bitcast(dt.uint8), ["qx0"], [])
+            evac("v", 1, 3)
+            qx(r + 1, 1)
+            mm(1, H, T.qvc[:], T.qvs[:], T.qxc[:, H:C], T.qxs[:, H:C], True, True, ["qv", "qx1"])
+            act(T.olb[:], T.ow[:].indirect(T.eo[:, 96:120]), F.Copy, ["ow0", "ow1", "eo4"], ["olb"])
+            cp(T.ysb[:, 0:H], T.ps0[:, 0:H], ["ps0"], ["ya"])
+            dma("y", T.oc[:, 4 * H:4 * C], T.qxc[:, H:C].bitcast(dt.uint8), ["qx1"], [])
+            cp(T.ysb[:, H:C], T.ps1[:, 0:H], ["ps1"], ["yb"])
+            dma("y", T.y[:, 0:H], T.ysb[:, 0:H], ["ya"], [])
+            dma("y", T.y[:, H:C], T.ysb[:, H:C], ["yb"], [])
+            dma("s", T.ol[:], T.olb[0:128:16, :], ["olb"], [])
+            for k in range(4):
+                dma("s", T.osc[4 * k:4 * k + 4, :], T.qxs[32 * k:32 * k + 4, :], ["qx0", "qx1"], [])
+
+    for s in count:
+        wait("q", (s, count[s]))

@@ -3,6 +3,7 @@ from concourse.mybir import dt, AluOpType, ActivationFunctionType
 A, F = AluOpType, ActivationFunctionType
 C, K, R = 384, 64, 3
 H = C // 2
+Z = 96
 Q4, U8, BF, F32, I32, U16, F16 = "float8_e4m3fn_x4", "uint8", "bfloat16", "float32", "int32", "uint16", "float16"
 
 
@@ -17,23 +18,23 @@ SCRATCH = {
     "wq": _sb(512, Q4), "wp": _sb(512, U8), "zq": _sb(512, Q4), "zp": _sb(512, U8),
     "gt": _sb(516, BF), "ones": _sb(516, BF), "ec": _sb(512, Q4), "es": _sb(512, U8),
     "ci": _sb(48, I32), "cu": _sb(48, U16), "pi": _sb(24, I32), "pj": _sb(24, I32), "pu": _sb(24, U16), "qf": _sb(2, F32),
-    "ia": _sb(24, F32), "il": _sb(24, F32), "ip": _sb(4, F32), "c2": _sb(4, F32),
+    "ia": _sb(24, F32), "il": _sb(24, F32), "ip": _sb(4, F32), "cc": _sb(2, F32),
     "im": _sb(16, I32), "im2": _sb(16, I32), "c16": _sb(16, F32), "m16": _sb(16, F32),
-    "msk": _sb(C, BF), "ctl": _sb(C, BF), "ctl2": _sb(C, BF),
+    "msk": _sb(C, BF), "ctl": _sb(C, BF), "ctlc": _sb(C, F16), "ctl2": _sb(C, BF),
     "zero": _sb(C, BF), "io448": _sb(C + K, BF), "ow": _sb(C + K, F32),
     "qxc": _sb(C, Q4), "qxs": _sb(C, U8), "pt": _sb(C, F32),
     "flg": _sb(11 * C, BF), "sj": _sb(11 * H, BF), "sg": _sb(14 * C, BF), "acc": _sb(13, F32),
-    "z4": _sb(48, F32), "yc": _sb(48, F32), "rb": _sb(2, F32),
+    "z4": _sb(48, F32), "yc": _sb(48, F32), "rb": _sb(4, F32),
     "k1l": _sb(C, F16), "yl": _sb(C, F16), "k1h": _sb(C, BF), "yh": _sb(C, BF),
     "mxl": _sb(H, F16), "mnl": _sb(H, F32), "mxh": _sb(H, BF), "mnh": _sb(H, BF), "sml": _sb(4, F32), "smh": _sb(4, BF),
-    "dl": _sb(4, F32), "dh": _sb(4, F32), "dm": _sb(4, F32), "sgl": _sb(4 * C, BF), "sgh": _sb(4 * C, BF), "sgm": _sb(4 * K, BF),
+    "dl": _sb(4, F32), "dh": _sb(4, F32), "dm": _sb(4, F32), "sgl": _sb(4 * C, BF), "sgh": _sb(4 * (C + Z), BF), "sgm": _sb(4 * K, BF),
     "lo": _sb(20, U16), "chl": _sb(K, BF), "bt": _sb(512, BF),
     "qbc": _sb(R * 128, Q4), "qbs": _sb(R * 128, U8), "landc": _sb(320, Q4), "lands": _sb(320, U8),
     "lsend": _sb(K, BF), "lland": _sb(K, BF),
-    "cva": _sb(C, BF), "cvb": _sb(C, BF), "cvc": _sb(C, BF),
-    "t1": _sb(24, F32), "bq": _sb(24, F32), "lm": _sb(24, F32), "lm2": _sb(24, F32), "pp": _sb(24, F32), "oo": _sb(24, F32),
-    "ou": _sb(24, U16), "a1": _sb(4, F32), "a2": _sb(4, F32), "au": _sb(4, U16),
-    "ew": _sb(2 * C + K, BF), "em": _sb(C, BF), "ex": _sb(C, BF), "eo": _sb(120, U16),
+    "cva": _sb(C, BF), "cvb": _sb(C, BF), "cvc": _sb(C, F16),
+    "t1": _sb(24, F32), "lm": _sb(24, F32), "wm": _sb(24, F32), "oo": _sb(24, F32),
+    "ou": _sb(24, U16), "a1": _sb(4, F32), "au": _sb(4, U16),
+    "ew": _sb(960, BF), "em": _sb(C, BF), "ex": _sb(C, BF), "eo": _sb(120, U16),
     "ta": _sb(4 * 208, BF), "tb": _sb(4 * 196, BF),
     "qtc": _sb(4 * H, Q4), "qts": _sb(4 * H, U8),
     "ysb": _sb(C, F32), "olb": _sb(C, F32),
@@ -41,7 +42,7 @@ SCRATCH = {
 for _s in ("l", "h"):
     for _n in ("f", "pf", "eq", "s1", "x1", "x2"):
         SCRATCH[_n + _s] = _sb(C, BF)
-    SCRATCH["cn" + _s] = _sb(C + 16, BF)
+    SCRATCH["cn" + _s] = _sb(C + Z, BF)
 for _r in range(R + 1):
     SCRATCH["xw%d" % _r] = _sb(4 * (C + K), BF)
 for _b in range(8):
@@ -138,6 +139,12 @@ def rank_program(g, core, T, topo):
     def act(out, in_, func, rd, wr, **kw):
         op("s", lambda: S.activation(out, in_, func, **kw), rd, wr)
 
+    def move(e, out, in_, rd, wr):
+        if e == "v":
+            cp(out, in_, rd, wr)
+        else:
+            act(out, in_, F.Copy, rd, wr)
+
     def mm(bank, n, lc, ls, rc, rs, start, stop, rd):
         op("p", lambda: P.matmul_mx(T["ps%d" % bank][:, 0:n], lc, ls, rc, rs, start, stop), rd, ["ps%d" % bank], chain=not start)
 
@@ -163,39 +170,40 @@ def rank_program(g, core, T, topo):
     dma("y", T.vt[:], T.v[:], [], ["vt"])
 
     btk = ["bt0", "bt1", "bt2", "bt3"]
-    iota(T.pi[:], [[0, 24]], 0, 1, ["pi"])
-    iota(T.im[:], [[1, 16]], 0, -1, ["im"])
     iota(T.ci[:, 0:8], [[16, 8]], 0, 0, ["ci0"])
     iota(T.ci[:, 8:16], [[32, 4], [0, 2]], 0, 0, ["ci1"])
     iota(T.ci[:, 16:24], [[32, 4], [0, 2]], 16, 0, ["ci2"])
     iota(T.ci[:, 24:48], [[1, 12], [12, 2]], 0, 0, ["ci3"])
+    iota(T.pi[:], [[0, 24]], 0, 1, ["pi"])
+    iota(T.im[:], [[1, 16]], 0, -1, ["im"])
     iota(T.ia[:], [[16, 24]], 0, 0, ["ia"], True)
     fill(T.ones[:], 1.0, ["ones"])
     fill(T.bt[:], 0.0, btk)
     fill(T.zero[:], 0.0, ["zero"])
     fill(T.ctl2[:], -256.0, ["ctl2"])
-    fill(T.cnl[:, 0:16], 0.0, ["cnl"])
-    fill(T.cnh[:, 0:16], 0.0, ["cnh"])
+    fill(T.cnl[:, 0:Z], 0.0, ["cnl"])
+    fill(T.cnh[:, 0:Z], 0.0, ["cnh"])
     fill(T.ctl2[:, 0:C:16], 768.0, ["ctl2"])
     op("q", lambda: g.affine_select(T.gt[:], T.ones[:], [[1, 516]], A.is_equal, 0.0, -3, -4), ["ones"], ["gt"])
     iota(T.io448[:], [[1, C + K]], -192, 0, ["io448"], True)
     iota(T.ow[:, 0:C], [[1, C]], 0, 0, ["ow0"], True)
     quant(T.landc[:, 64:192], T.lands[:, 64:192], T.bt[:], btk, ["landz"])
+    cp(T.cu[:], T.ci[:], ["ci0", "ci1", "ci2", "ci3"], ["cu"])
     ts(T.pj[:], T.pi[:], 15, None, A.bitwise_and, None, ["pi"], ["pj"])
     ts(T.im2[:], T.im[:], 15, None, A.bitwise_and, None, ["im"], ["im2"])
     cp(T.pu[:], T.pj[:], ["pj"], ["pu"])
     ts(T.c16[:], T.im2[:], 15.0, 128.0, A.is_equal, A.mult, ["im2"], ["c16"])
     ts(T.m16[:], T.im2[:], 0.0, 1024.0, A.not_equal, A.mult, ["im2"], ["m16"])
     cp(T.qf[:], T.pj[:, 0:2], ["pj"], ["qf"])
-    cp(T.cu[:], T.ci[:], ["ci0", "ci1", "ci2", "ci3"], ["cu"])
     ts(T.il[:], T.ia[:], T.qf[:, 0:1], None, A.add, None, ["ia", "qf"], ["il"])
     act(T.ctl[:], T.c16[:].indirect(T.pu[:]), F.Copy, ["c16", "pu"], ["ctl"])
     quant(T.quc[:], T.qus[:], T.ut[:], ["ut"], ["qu"])
     act(T.pus[:], T.qus[:].indirect(T.cu[:, 0:24]), F.Copy, ["qu", "cu"], ["pus"])
     cp(T.puc[:].bitcast(dt.uint32), T.quc[:].bitcast(dt.uint32).indirect(T.cu[:, 0:24]), ["qu", "cu"], ["puc"])
-    act(T.msk[:], T.m16[:].indirect(T.pu[:]), F.Identity, ["m16", "pu"], ["msk"], bias=-256.0)
     act(T.ip[:], T.il[:, 0:4], F.Identity, ["il"], ["ip"], bias=0.5)
-    act(T.c2[:], T.il[:, 0:4], F.Identity, ["il"], ["c2"], bias=322.0, scale=2.0)
+    act(T.cc[:, 0:1], T.c16[:, 15:16], F.Identity, ["c16"], ["cc0"], bias=256.0)
+    act(T.cc[:, 1:2], T.qf[:, 0:1], F.Identity, ["qf"], ["cc1"], bias=161.0)
+    act(T.msk[:], T.m16[:].indirect(T.pu[:]), F.Identity, ["m16", "pu"], ["msk"], bias=-256.0)
 
     def qx(r, h):
         quant(T.qxc[:, H * h:H * h + H], T.qxs[:, H * h:H * h + H], T["xw%d" % r][:, 4 * H * h:4 * H * (h + 1)], xkeys(r, (h,)), ["qx%d" % h])
@@ -210,7 +218,14 @@ def rank_program(g, core, T, topo):
         y, f, pf, eq, s1, x1, x2, cn, sm = [T[n + s] for n in ("y", "f", "pf", "eq", "s1", "x1", "x2", "cn", "sm")]
         mx, mn = T["mx" + s], T["mn" + s]
         o = A.max if s == "l" else A.min
+        sign, i = (1.0, 0) if s == "l" else (-1.0, 2)
         k = lambda *a: [n + s for n in a]
+
+        def side():
+            act(T.rb[:, i:i + 1], pf[:, C - 1:C], F.Relu, k("pf"), k("ra"), bias=128.0 * sign, scale=2.0 * sign)
+            act(T.rb[:, i + 1:i + 2], T.rb[:, i:i + 1], F.Identity, k("ra"), k("rb"), bias=192.0, scale=-sign)
+            act(x2[:], pf[:], F.Identity, k("pf", "rb"), k("x2"), bias=T.rb[:, i + 1:i + 2], scale=2.0)
+
         return {
             "y": lambda: op("v", lambda: V.transpose(y[:], T["k1" + s][:]), k("k1"), k("y")),
             "f": lambda: ts(f[:], y[:], 0.0, 0.5, A.is_gt, A.mult, k("y"), k("f")),
@@ -219,17 +234,16 @@ def rank_program(g, core, T, topo):
             "pf": lambda: scan(pf[:], f[:], T.zero[:], -96.0, A.add, A.add, k("f") + ["zero"], k("pf")),
             "sg": lambda: ts(sm[:, 0:1], pf[:, C - 1:C], -64.0, 0.5, A.is_ge, A.subtract, k("pf"), k("sg")),
             "ty": lambda: ts(sm[:, 1:2], mx[:, H - 1:H], sm[:, 0:1], mn[:, H - 1:H], A.min, A.max, k("mx", "mn", "sg"), k("ty")),
-            "m2": lambda: ts(sm[:, 2:3], pf[:, C - 1:C], 32.0, -96.0, A.subtract, o, k("pf"), k("m2")),
             "eq": lambda: ts(eq[:], y[:], sm[:, 1:2], sm[:, 0:1], A.is_equal, A.mult, k("y", "ty", "sg"), k("eq")),
-            "x2": lambda: ts(x2[:], pf[:], sm[:, 2:3], 2.0, A.subtract, A.mult, k("pf", "m2"), k("x2")),
+            "x2": side,
             "s1": lambda: scan(s1[:], f[:], eq[:], -96.0, A.add, A.subtract, k("f", "eq"), k("s1")),
             "m1": lambda: ts(sm[:, 3:4], s1[:, C - 1:C], 32.0, -96.0, A.subtract, o, k("s1"), k("m1")),
             "x1": lambda: ts(x1[:], s1[:], sm[:, 3:4], 2.0, A.subtract, A.mult, k("s1", "m1"), k("x1")),
-            "cn": lambda: scan(cn[:, 16:C + 16], x1[:], x2[:], 0.0, A.max, o, k("x1", "x2"), k("cn")),
+            "cn": lambda: scan(cn[:, Z:C + Z], x1[:], x2[:], 0.0, A.max, o, k("x1", "x2"), k("cn")),
         }
 
-    def wrap(out, src, key, okey):
-        scan(out[:], src, T.ctl[:], 128.0, A.min, A.add, [key, "ctl"], [okey])
+    def wrap(out, src, ctl, rd, okey):
+        scan(out[:], src, ctl[:], 128.0, A.min, A.add, rd, [okey])
 
     qx(0, 0)
     score(0, 0, 0, H, ["qx0"])
@@ -245,8 +259,8 @@ def rank_program(g, core, T, topo):
         score(3, 0, H, C, ["qx1"])
         score(4, 2, 0, C, ["qx0", "qx1"])
         if r == 0:
-            for b in range(4):
-                quant(T.ec[:, 128 * b:128 * b + 128], T.es[:, 128 * b:128 * b + 128], T.gt[:, 3 - b:515 - b], ["gt"], ["e%d" % b])
+            cp(T.ctlc[:], T.ctl[:], ["ctl"], ["ctlc"])
+            tt(T.ctlc[:, 15:C:16], T.ctl[:, 15:C:16], T.il[:], A.add, ["ctl", "il"], ["ctlc"])
 
         def cmp(b):
             ts(T.flg[:, C * b:C * b + C], T.ps2[:, 0:C], T.pt[:, 32 * b + 16:32 * b + 17], None, A.is_gt, None, ["ps2", "pt%d" % (b // 6)], ["flg%d" % b])
@@ -266,9 +280,9 @@ def rank_program(g, core, T, topo):
                 turn(3, 1)
             else:
                 cnt(b - 1)
-            if b == 10:
+            if b == 9:
                 act(T.sg[:, C * 12:C * 13], T.ps4[:, 0:C], F.Sign, ["ps4", "pt1"], ["sg12"], bias=T.pt[:, 32 * 11 + 16:32 * 11 + 17], scale=-1.0)
-            if b == 11:
+            if b == 10:
                 act(T.sg[:, C * 13:C * 14], T.sg[:, C * 12:C * 13], F.Relu, ["sg12"], ["sg13", "acc12"], scale=-1.0, accum_out=T.acc[:, 12:13])
             sgn(b)
             for k, n in (("ps1", 11), ("ps2", 10)):
@@ -276,97 +290,78 @@ def rank_program(g, core, T, topo):
                     readers[k] = []
                     lastw[k] = written[k]
         acck, sjk = ["acc%d" % b for b in range(12)], ["sj%d" % b for b in range(11)]
-        act(T.z4[:, 23:24], T.acc[:, 12:13], F.Identity, ["acc12"], ["z4e"], bias=-2562.0, scale=8.0)
-        act(T.z4[:, 47:48], T.acc[:, 12:13], F.Identity, ["acc12"], ["z4f"], bias=506.0, scale=-8.0)
-        act(T.z4[:, 0:12], T.acc[:, 0:12], F.Identity, acck, ["z4a"], bias=-1030.0, scale=-4.0)
-        act(T.z4[:, 24:36], T.acc[:, 0:12], F.Identity, acck, ["z4c"], bias=-1026.0, scale=4.0)
+        ts(T.z4[:, 23:24], T.acc[:, 12:13], 8.0, -2562.0, A.mult, A.add, ["acc12"], ["z4e"])
         ts(T.z4[:, 12:23], T.sj[:, H - 1:11 * H:H], 8.0, -1026.0, A.mult, A.add, sjk, ["z4b"])
+        ts(T.z4[:, 47:48], T.acc[:, 12:13], -8.0, 506.0, A.mult, A.add, ["acc12"], ["z4f"])
         ts(T.z4[:, 36:47], T.sj[:, H - 1:11 * H:H], -8.0, -1030.0, A.mult, A.add, sjk, ["z4d"])
+        act(T.z4[:, 0:12], T.acc[:, 0:12], F.Identity, acck, ["z4a"], bias=-1030.0, scale=-4.0)
+        ts(T.z4[:, 24:36], T.acc[:, 0:12], 4.0, -1026.0, A.mult, A.add, acck, ["z4c"])
         op("v", lambda: V.reciprocal(T.yc[:], T.z4[:]), ["z4" + c for c in "abcdef"], ["yc"])
         act(T.k1h[:], T.yc[:, 24:48].indirect(T.cu[:, 24:48]), F.Copy, ["yc", "cu"], ["k1h"])
         cp(T.k1l[:], T.yc[:, 0:24].indirect(T.cu[:, 24:48]), ["yc", "cu"], ["k1l"])
 
         lo, hi = cut("l"), cut("h")
-        for n in ("y", "f", "mx", "pf", "mn", "sg", "ty", "eq", "s1", "m1", "x1"):
+        for n in ("y", "f", "pf", "x2", "mx", "mn", "sg", "ty", "eq", "s1", "m1", "x1", "cn"):
             lo[n]()
-        act(T.rb[:, 0:1], T.pfl[:, C - 1:C], F.Relu, ["pfl"], ["rb0"], bias=128.0, scale=2.0)
-        act(T.rb[:, 1:2], T.rb[:, 0:1], F.Identity, ["rb0"], ["rb1"], bias=192.0, scale=-1.0)
-        act(T.x2l[:], T.pfl[:], F.Identity, ["pfl", "rb1"], ["x2l"], bias=T.rb[:, 1:2], scale=2.0)
-        lo["cn"]()
-        CLi, CLe, CHi, CHe = T.cnl[:, 16:C + 16], T.cnl[:, 15:C + 15], T.cnh[:, 16:C + 16], T.cnh[:, 15:C + 15]
+            hi[n]()
+        CLi, CLe, CHi, CHe = T.cnl[:, Z:C + Z], T.cnl[:, Z - 1:C + Z - 1], T.cnh[:, Z:C + Z], T.cnh[:, Z - 1:C + Z - 1]
         for k in range(4):
             act(T.sgl[:, C * k:C * k + C], CLi, F.Sign, ["cnl", "ip"], ["sgl%d" % k, "dl%d" % k], bias=T.ip[:, k:k + 1], scale=-1.0, accum_out=T.dl[:, k:k + 1])
+        for k in range(4):
+            act(T.sgh[:, (C + Z) * k:(C + Z) * k + C + 32 * k], T.cnh[:, Z - 32 * k:C + Z], F.Sign, ["cnh", "ip"], ["sgh%d" % k, "dh%d" % k],
+                bias=T.ip[:, k:k + 1], scale=-1.0, accum_out=T.dh[:, k:k + 1])
         dlk = ["dl%d" % k for k in range(4)]
-
-        hi["y"]()
-        wrap(T.cva, CLi, "cnl", "cva")
-        hi["f"]()
-        wrap(T.cvb, CLe, "cnl", "cvb")
-        hi["mx"]()
-        hi["pf"]()
-        hi["mn"]()
-        hi["sg"]()
+        wrap(T.cva, CLi, T.ctl, ["cnl", "ctl"], "cva")
+        wrap(T.cvb, CLe, T.ctl, ["cnl", "ctl"], "cvb")
+        wrap(T.cvc, CHe, T.ctlc, ["cnh", "ctlc"], "cvc")
         tt(T.t1[:], T.cva[:, 15:C:16], T.cvb[:, 15:C:16], A.subtract, ["cva", "cvb"], ["t1"])
-        hi["ty"]()
-        hi["m2"]()
-        hi["eq"]()
+        ts(T.lm[:], T.t1[:], -768.0, T.cc[:, 0:1], A.mult, A.add, ["t1", "cc0"], ["lm"])
+        tt(T.wm[:], T.cvb[:, 15:C:16], T.lm[:], A.min, ["cvb", "lm"], ["wm"])
+        tt(T.oo[:], T.cvc[:, 15:C:16], T.wm[:], A.subtract, ["cvc", "wm"], ["oo"])
+        cp(T.ou[:], T.oo[:], ["oo"], ["ou"])
         for t in range(4):
             ts(T.lo[:, 4 * t:4 * t + 4], T.dl[:], 2.0, 768.0 + t, A.mult, A.add, dlk, ["lo%d" % t])
-            act(T.bt[:, t:4 * K:4], X[:, 0:4 * C].indirect(T.lo[:, 4 * t:4 * t + 4]), F.Copy, xk + ["lo%d" % t], ["bt%d" % t])
         ts(T.lo[:, 16:20], T.dl[:], 0.5, 192.0, A.mult, A.add, dlk, ["lo4"])
-        hi["s1"]()
-        hi["x2"]()
-        hi["m1"]()
+        for t in range(4):
+            cp(T.bt[:, t:4 * K:4], X[:, 0:4 * C].indirect(T.lo[:, 4 * t:4 * t + 4]), xk + ["lo%d" % t], ["bt%d" % t])
+        cp(T.chl[:], CHi.indirect(T.lo[:, 16:20]), ["cnh", "lo4"], ["chl"])
         quant(T.qbc[:, 128 * r:128 * r + 128], T.qbs[:, 128 * r:128 * r + 128], T.bt[:], btk, ["qb%d" % r])
         l0 = (0, 192, 256)[r]
         send(T.landc[:, l0:l0 + K].bitcast(dt.uint8), T.qbc[:, 128 * r:128 * r + K].bitcast(dt.uint8), "arr%d" % r, ["qb%d" % r])
         send(T.lands[:, l0:l0 + K], T.qbs[:, 128 * r:128 * r + K], "arr%d" % r, ["qb%d" % r])
         lastw["land%d" % r] = ("arr%d" % r, 2 * neng)
+
+        for k in range(4):
+            act(T.sgm[:, K * k:K * k + K], T.chl[:], F.Sign, ["chl", "ip"], ["sgm%d" % k, "dm%d" % k], bias=T.ip[:, k:k + 1], scale=-1.0, accum_out=T.dm[:, k:k + 1])
         if last:
             act(T.lsend[:], T.io448[:, 0:C].indirect(T.lo[:, 16:20]), F.Copy, ["io448", "lo4"], ["lsend"])
             send(T.lland[:], T.lsend[:], "arrl", ["lsend"])
             lastw["lland"] = ("arrl", neng)
-        hi["x1"]()
-        ts(T.lm[:], T.t1[:], 512.0, -64.0, A.mult, A.add, ["t1"], ["lm"])
-        hi["cn"]()
-        tt(T.bq[:], T.il[:], T.cvb[:, 15:C:16], A.subtract, ["il", "cvb"], ["bq"])
-        wrap(T.cvc, CHe, "cnh", "cvc")
-        tt(T.lm2[:], T.lm[:], T.il[:], A.add, ["lm", "il"], ["lm2"])
-        act(T.chl[:], CHi.indirect(T.lo[:, 16:20]), F.Copy, ["cnh", "lo4"], ["chl"])
-        for k in range(4):
-            act(T.sgh[:, C * k:C * k + C], CHi, F.Sign, ["cnh", "ip"], ["sgh%d" % k, "dh%d" % k], bias=T.ip[:, k:k + 1], scale=-1.0, accum_out=T.dh[:, k:k + 1])
-        for k in range(4):
-            act(T.sgm[:, K * k:K * k + K], T.chl[:], F.Sign, ["chl", "ip"], ["sgm%d" % k, "dm%d" % k], bias=T.ip[:, k:k + 1], scale=-1.0, accum_out=T.dm[:, k:k + 1])
-        tt(T.pp[:], T.cvc[:, 15:C:16], T.bq[:], A.add, ["cvc", "bq"], ["pp"])
-        tt(T.oo[:], T.pp[:], T.lm2[:], A.max, ["pp", "lm2"], ["oo"])
-        cp(T.ou[:], T.oo[:], ["oo"], ["ou"])
         cp(T.ew[:].indirect(T.ou[:]), T.io448[:, 0:C], ["ou", "io448"], ["ew"])
         tt(T.a1[:], T.dh[:], T.dm[:], A.subtract, ["dh%d" % k for k in range(4)] + ["dm%d" % k for k in range(4)], ["a1"])
-        tt(T.a2[:], T.a1[:], T.c2[:], A.add, ["a1", "c2"], ["a2"])
-        ts(T.au[:], T.a2[:], 0.5, None, A.mult, None, ["a2"], ["au"])
+        ts(T.au[:], T.a1[:], 0.5, T.cc[:, 1:2], A.mult, A.add, ["a1", "cc1"], ["au"])
         cp(T.ew[:].indirect(T.au[:]), T.io448[:, C:C + K], ["au", "io448"], ["ew"])
+        if r == 0:
+            for b in range(4):
+                quant(T.ec[:, 128 * b:128 * b + 128], T.es[:, 128 * b:128 * b + 128], T.gt[:, 3 - b:515 - b], ["gt"], ["e%d" % b])
         tt(T.em[:], T.ew[:, 0:C], T.msk[:], A.max, ["ew", "msk"], ["em"])
         scan(T.ex[:], T.ctl2[:], T.em[:], 0.0, A.max, A.min, ["em", "ctl2"], ["ex"])
+        for t in (2, 3, 0, 1):
+            ts(T.eo[:, 24 * t:24 * t + 24], T.ex[:, 15:C:16], 4.0, 768.0 + t, A.mult, A.add, ["ex"], ["eo%d" % t])
 
         v0 = (0, 128, 192)[r]
         lk = ["land%d" % r, "landz"] + (["land1"] if r == 2 else [])
         for b in range(4):
             mm(4 + b, 128, T.ec[:, 128 * b:128 * b + 128], T.es[:, 128 * b:128 * b + 128], T.landc[:, v0:v0 + 128], T.lands[:, v0:v0 + 128], True, True, ["e%d" % b] + lk)
-            act(X[:, 4 * C + b:4 * (C + K):4], T["ps%d" % (4 + b)][:, l0 - v0:l0 - v0 + K], F.Copy, ["ps%d" % (4 + b)], ["xa%d_%d" % (r, b)])
+            move("s", X[:, 4 * C + b:4 * (C + K):4], T["ps%d" % (4 + b)][:, l0 - v0:l0 - v0 + K], ["ps%d" % (4 + b)], ["xa%d_%d" % (r, b)])
         wk = xk + ["xa%d_%d" % (r, b) for b in range(4)]
-
-        for t in (2, 3, 0, 1):
-            ts(T.eo[:, 24 * t:24 * t + 24], T.ex[:, 15:C:16], 4.0, 768.0 + t, A.mult, A.add, ["ex"], ["eo%d" % t])
 
         def gather(e, h, t):
             if h == 0:
                 out, off, key = T.ta[:, t:4 * 208:4], T.eo[:, 24 * t:24 * t + 13], "ta%d" % t
             else:
                 out, off, key = T.tb[:, t:4 * H:4], T.eo[:, 24 * t + 12:24 * t + 24], "tb%d" % t
-            if e == "v":
-                cp(out, X[:].indirect(off), wk + ["eo%d" % t], [key])
-            else:
-                act(out, X[:].indirect(off), F.Copy, wk + ["eo%d" % t], [key])
+            move(e, out, X[:].indirect(off), wk + ["eo%d" % t], [key])
 
         def qt(h, rot):
             i = 2 * h + rot
@@ -391,8 +386,6 @@ def rank_program(g, core, T, topo):
         gather("s", 0, 3)
         gather("v", 0, 0)
         gather("v", 0, 1)
-        if last:
-            ts(T.eo[:, 96:120], T.ex[:, 15:C:16], 192.0, None, A.add, None, ["ex"], ["eo4"])
         qt(0, 0)
         qt(0, 1)
         layer(0)
@@ -400,14 +393,16 @@ def rank_program(g, core, T, topo):
         gather("s", 1, 3)
         gather("v", 1, 0)
         gather("s", 1, 1)
-        act(T.tb[:, 4 * H:4 * H + 4], T.ta[:, 0:4], F.Copy, ["ta%d" % t for t in range(4)], ["tbw"])
+        cp(T.tb[:, 4 * H:4 * H + 4], T.ta[:, 0:4], ["ta%d" % t for t in range(4)], ["tbw"])
+        if last:
+            ts(T.eo[:, 96:120], T.ex[:, 15:C:16], 192.0, None, A.add, None, ["ex"], ["eo4"])
         qt(1, 0)
         qt(1, 1)
         layer(1)
         evac("s", 0, 0)
-        evac("s", 0, 1)
-        evac("v", 0, 2)
-        evac("s", 0, 3)
+        evac("v", 0, 1)
+        evac("s", 0, 2)
+        evac("v", 0, 3)
         if r == 0:
             quant(T.qvc[:], T.qvs[:], T.vt[:], ["vt"], ["qv"])
         if last:

@@ -3,7 +3,8 @@ from concourse.mybir import dt, AluOpType, ActivationFunctionType
 A, F = AluOpType, ActivationFunctionType
 C, K, R = 384, 64, 3
 H = C // 2
-Z = 96
+W = C + K
+U = H + 16
 Q4, U8, BF, F32, I32, U16, F16 = "float8_e4m3fn_x4", "uint8", "bfloat16", "float32", "int32", "uint16", "float16"
 
 
@@ -21,20 +22,20 @@ SCRATCH = {
     "ia": _sb(24, F32), "il": _sb(24, F32), "ip": _sb(4, F32), "cc": _sb(2, F32),
     "im": _sb(16, I32), "im2": _sb(16, I32), "c16": _sb(16, F32), "m16": _sb(16, F32),
     "msk": _sb(C, BF), "ctl": _sb(C, BF), "ctlc": _sb(C, F16), "ctl2": _sb(C, BF),
-    "zero": _sb(C, BF), "io448": _sb(C + K, BF), "ow": _sb(C + K, F32),
+    "zero": _sb(C, BF), "zt": _sb(512, BF), "ramp": _sb(C, BF), "ow": _sb(W, F32),
     "qxc": _sb(C, Q4), "qxs": _sb(C, U8), "pt": _sb(C, F32),
-    "flg": _sb(11 * C, BF), "sj": _sb(11 * H, BF), "sg": _sb(14 * C, BF), "acc": _sb(13, F32),
-    "z4": _sb(48, F32), "yc": _sb(48, F32), "rb": _sb(4, F32),
-    "k1l": _sb(C, F16), "yl": _sb(C, F16), "k1h": _sb(C, BF), "yh": _sb(C, BF),
-    "mxl": _sb(H, F16), "mnl": _sb(H, F32), "mxh": _sb(H, BF), "mnh": _sb(H, BF), "sml": _sb(4, F32), "smh": _sb(4, BF),
-    "dl": _sb(4, F32), "dh": _sb(4, F32), "dm": _sb(4, F32), "sgl": _sb(4 * C, BF), "sgh": _sb(4 * (C + Z), BF), "sgm": _sb(4 * K, BF),
-    "lo": _sb(20, U16), "chl": _sb(K, BF), "bt": _sb(512, BF),
+    "tri2": _sb(4 * 192, BF), "tri3": _sb(4 * 256, BF), "tri4": _sb(4 * 320, BF), "tri5": _sb(4 * 384, BF),
+    "sj": _sb(6 * H, BF), "sg": _sb(8 * 128, BF), "rho": _sb(24, F32),
+    "qfc": _sb(896, Q4), "qfs": _sb(896, U8), "cs0": _sb(128, BF), "cst": _sb(512, BF), "csc": _sb(128, Q4), "css": _sb(128, U8),
+    "qt": _sb(C, F32), "kc": _sb(48, F32), "kr": _sb(48, F32), "z4": _sb(48, F32), "yc": _sb(48, F32), "rb": _sb(4, F32),
+    "k1l": _sb(C, BF), "yl": _sb(C, BF), "k1h": _sb(C, F16), "yh": _sb(C, F16),
+    "mxl": _sb(H, BF), "mnl": _sb(H, BF), "mxh": _sb(H, F16), "mnh": _sb(H, F32), "sml": _sb(4, BF), "smh": _sb(4, F32),
+    "dl": _sb(4, F32), "sgl": _sb(4 * C, BF), "lo": _sb(4, U16), "bt": _sb(512, BF), "xp": _sb(4 * W, BF),
     "qbc": _sb(R * 128, Q4), "qbs": _sb(R * 128, U8), "landc": _sb(320, Q4), "lands": _sb(320, U8),
     "lsend": _sb(K, BF), "lland": _sb(K, BF),
     "cva": _sb(C, BF), "cvb": _sb(C, BF), "cvc": _sb(C, F16),
-    "t1": _sb(24, F32), "lm": _sb(24, F32), "wm": _sb(24, F32), "oo": _sb(24, F32),
-    "ou": _sb(24, U16), "a1": _sb(4, F32), "au": _sb(4, U16),
-    "ew": _sb(960, BF), "em": _sb(C, BF), "ex": _sb(C, BF), "eo": _sb(120, U16),
+    "t1": _sb(24, F32), "lm": _sb(24, F32), "wm": _sb(24, F32), "oo": _sb(24, F32), "ou": _sb(24, U16),
+    "ew": _sb(960, BF), "hf": _sb(C, BF), "hn": _sb(C, BF), "en": _sb(C, BF), "em": _sb(C, BF), "ex": _sb(C, BF), "eo": _sb(24, U16),
     "ta": _sb(4 * 208, BF), "tb": _sb(4 * 196, BF),
     "qtc": _sb(4 * H, Q4), "qts": _sb(4 * H, U8),
     "ysb": _sb(C, F32), "olb": _sb(C, F32),
@@ -42,14 +43,18 @@ SCRATCH = {
 for _s in ("l", "h"):
     for _n in ("f", "pf", "eq", "s1", "x1", "x2"):
         SCRATCH[_n + _s] = _sb(C, BF)
-    SCRATCH["cn" + _s] = _sb(C + Z, BF)
+    SCRATCH["cn" + _s] = _sb(C + 16, BF)
 for _r in range(R + 1):
-    SCRATCH["xw%d" % _r] = _sb(4 * (C + K), BF)
+    SCRATCH["xw%d" % _r] = _sb(4 * C, BF)
 for _b in range(8):
     SCRATCH["ps%d" % _b] = ("psum", [128, 512], F32)
 
 _NDMA = 17
 SEMAPHORES = ["sv", "ss", "sp", "sq", "sent", "arr0", "arr1", "arr2", "arrl"] + ["d%d" % _i for _i in range(_NDMA)]
+
+
+def _reach(b):
+    return max(128, 64 * (b // 2 + 1))
 
 
 def rank_program(g, core, T, topo):
@@ -62,7 +67,7 @@ def rank_program(g, core, T, topo):
     neng = len(topo.engines(core, nxt))
 
     queue = {"v": g.vector, "s": g.scalar, "p": g.tensor, "q": g, "y": g.sync}
-    semof = {"v": "sv", "s": "ss", "p": "sp", "q": "sq"}
+    semof = {"v": "sv", "s": "ss", "p": "sp", "q": "sq", "y": None}
     count = {}
     waited = {k: {} for k in queue}
     lastw, readers = {}, {}
@@ -75,15 +80,18 @@ def rank_program(g, core, T, topo):
 
     def before(e, rd, wr, chain=False):
         need = {}
+        toks = []
         for k in rd:
             if k in lastw:
-                need[lastw[k][0]] = max(need.get(lastw[k][0], 0), lastw[k][1])
+                toks.append(lastw[k])
+            if k.startswith("ps"):
+                toks += [t for t in readers.get(k, []) if t[0] != semof[e]]
         for k in wr:
-            toks = list(readers.get(k, []))
+            toks += readers.get(k, [])
             if k in lastw and not chain:
                 toks.append(lastw[k])
-            for t in toks:
-                need[t[0]] = max(need.get(t[0], 0), t[1])
+        for t in toks:
+            need[t[0]] = max(need.get(t[0], 0), t[1])
         for s in need:
             wait(e, (s, need[s]))
 
@@ -95,7 +103,6 @@ def rank_program(g, core, T, topo):
             readers[k] = []
 
     def op(e, make, rd, wr, chain=False):
-        wr = list(wr) + [k for k in rd if k.startswith("ps")]
         before(e, rd, wr, chain)
         s = semof[e]
         count[s] = count.get(s, 0) + 1
@@ -148,17 +155,23 @@ def rank_program(g, core, T, topo):
     def mm(bank, n, lc, ls, rc, rs, start, stop, rd):
         op("p", lambda: P.matmul_mx(T["ps%d" % bank][:, 0:n], lc, ls, rc, rs, start, stop), rd, ["ps%d" % bank], chain=not start)
 
-    def iota(out, pat, base, cm, wr, fl=False):
+    def iota(out, pat, base, cm, wr, fl=True):
         if fl:
             op("q", lambda: g.iota(out, pat, base, cm, allow_small_or_imprecise_dtypes=True), [], wr)
         else:
             op("q", lambda: g.iota(out, pat, base, cm), [], wr)
+
+    def keep(out, in_, pat, base, cm, o, rd, wr):
+        op("q", lambda: g.affine_select(out, in_, pat, o, 0.0, base, cm), rd, wr)
 
     def fill(ap, c, wr):
         op("v", lambda: V.memset(ap, c), [], wr)
 
     def xkeys(r, halves=(0, 1)):
         return ["x%d_%d_%d" % (r, h, b) for h in halves for b in range(4)]
+
+    def qx(r, h):
+        quant(T.qxc[:, H * h:H * h + H], T.qxs[:, H * h:H * h + H], T["xw%d" % r][:, 4 * H * h:4 * H * (h + 1)], xkeys(r, (h,)), ["qx%d" % h])
 
     dma("s", T.ut[:], T.u[:], [], ["ut"])
     dma("y", T.xw0[:, 0:4 * H], T.x[:, 0:4 * H], [], xkeys(0, (0,)))
@@ -170,43 +183,49 @@ def rank_program(g, core, T, topo):
     dma("y", T.vt[:], T.v[:], [], ["vt"])
 
     btk = ["bt0", "bt1", "bt2", "bt3"]
-    iota(T.ci[:, 0:8], [[16, 8]], 0, 0, ["ci0"])
-    iota(T.ci[:, 8:16], [[32, 4], [0, 2]], 0, 0, ["ci1"])
-    iota(T.ci[:, 16:24], [[32, 4], [0, 2]], 16, 0, ["ci2"])
-    iota(T.ci[:, 24:48], [[1, 12], [12, 2]], 0, 0, ["ci3"])
-    iota(T.pi[:], [[0, 24]], 0, 1, ["pi"])
-    iota(T.im[:], [[1, 16]], 0, -1, ["im"])
-    iota(T.ia[:], [[16, 24]], 0, 0, ["ia"], True)
+    iota(T.ci[:, 0:8], [[16, 8]], 0, 0, ["ci0"], False)
+    iota(T.ci[:, 8:24], [[16, 2], [32, 4], [0, 2]], 0, 0, ["ci1"], False)
+    iota(T.ci[:, 24:48], [[1, 24]], 0, 0, ["ci2"], False)
+    iota(T.pi[:], [[0, 24]], 0, 1, ["pi"], False)
+    iota(T.im[:], [[1, 16]], 0, -1, ["im"], False)
+    iota(T.ia[:], [[16, 24]], 0, 0, ["ia"])
     fill(T.ones[:], 1.0, ["ones"])
-    fill(T.bt[:], 0.0, btk)
-    fill(T.zero[:], 0.0, ["zero"])
-    fill(T.ctl2[:], -256.0, ["ctl2"])
-    fill(T.cnl[:, 0:Z], 0.0, ["cnl"])
-    fill(T.cnh[:, 0:Z], 0.0, ["cnh"])
-    fill(T.ctl2[:, 0:C:16], 768.0, ["ctl2"])
-    op("q", lambda: g.affine_select(T.gt[:], T.ones[:], [[1, 516]], A.is_equal, 0.0, -3, -4), ["ones"], ["gt"])
-    iota(T.io448[:], [[1, C + K]], -192, 0, ["io448"], True)
-    iota(T.ow[:, 0:C], [[1, C]], 0, 0, ["ow0"], True)
-    quant(T.landc[:, 64:192], T.lands[:, 64:192], T.bt[:], btk, ["landz"])
-    cp(T.cu[:], T.ci[:], ["ci0", "ci1", "ci2", "ci3"], ["cu"])
+    fill(T.cst[:], 0.0, ["cst"])
+    keep(T.cs0[:], T.ones[:, 0:128], [[-2, 2], [0, 16], [1, 4]], 0, 0, A.is_ge, ["ones"], ["cs0"])
+    for a in range(4):
+        keep(T.cst[32 * a:32 * a + 32, 128 * a:128 * a + 128], T.cs0[32 * a:32 * a + 32, :], [[2, 2], [0, 16], [-1, 4]], 1, 0, A.is_ge,
+             ["cs0", "cst"] + ["cst%d" % i for i in range(a)], ["cst%d" % a])
+    before("q", ["cst3"], [])
+    iota(T.qt[:, 320:C], [[0, C - 320]], 0, 0, ["qtz"])
+    iota(T.zero[:], [[0, C]], 0, 0, ["zero"])
+    iota(T.cnl[:, 0:16], [[0, 16]], -K, 0, ["cnl"])
+    iota(T.cnh[:, 0:16], [[0, 16]], -K, 0, ["cnh"])
+    iota(T.bt[:, 4 * K:512], [[0, 512 - 4 * K]], 0, 0, ["btz"])
+    iota(T.ramp[:], [[1, C]], -192, 0, ["ramp"])
+    keep(T.gt[:], T.ones[:], [[1, 516]], -3, -4, A.is_equal, ["ones"], ["gt"])
+    iota(T.ctl2[:], [[0, C]], -256, 0, ["ctl2"])
+    iota(T.ctl2[:, 0:C:16], [[0, C // 16]], 768, 0, ["ctl2"])
+    iota(T.ow[:, 0:C], [[1, C]], 0, 0, ["ow0"])
+    kck = []
+    for o, n in ((0, 2 * (C - K) + 0.5), (24, 2 * K + 0.5)):
+        for e in range(2):
+            fill(T.kc[:, o + e:o + 24:2], C + H * e - n, ["kc%d" % (o + e)])
+            kck.append("kc%d" % (o + e))
+    fill(T.zt[:], 0.0, ["zt"])
+    cp(T.cu[:], T.ci[:], ["ci0", "ci1", "ci2"], ["cu"])
     ts(T.pj[:], T.pi[:], 15, None, A.bitwise_and, None, ["pi"], ["pj"])
+    quant(T.landc[:, 64:192], T.lands[:, 64:192], T.zt[:], ["zt"], ["landz"])
     ts(T.im2[:], T.im[:], 15, None, A.bitwise_and, None, ["im"], ["im2"])
+    cp(T.qf[:], T.pj[:, 0:2], ["pj"], ["qf"])
     cp(T.pu[:], T.pj[:], ["pj"], ["pu"])
     ts(T.c16[:], T.im2[:], 15.0, 128.0, A.is_equal, A.mult, ["im2"], ["c16"])
-    ts(T.m16[:], T.im2[:], 0.0, 1024.0, A.not_equal, A.mult, ["im2"], ["m16"])
-    cp(T.qf[:], T.pj[:, 0:2], ["pj"], ["qf"])
     ts(T.il[:], T.ia[:], T.qf[:, 0:1], None, A.add, None, ["ia", "qf"], ["il"])
-    act(T.ctl[:], T.c16[:].indirect(T.pu[:]), F.Copy, ["c16", "pu"], ["ctl"])
     quant(T.quc[:], T.qus[:], T.ut[:], ["ut"], ["qu"])
+    qx(0, 0)
     act(T.pus[:], T.qus[:].indirect(T.cu[:, 0:24]), F.Copy, ["qu", "cu"], ["pus"])
     cp(T.puc[:].bitcast(dt.uint32), T.quc[:].bitcast(dt.uint32).indirect(T.cu[:, 0:24]), ["qu", "cu"], ["puc"])
-    act(T.ip[:], T.il[:, 0:4], F.Identity, ["il"], ["ip"], bias=0.5)
-    act(T.cc[:, 0:1], T.c16[:, 15:16], F.Identity, ["c16"], ["cc0"], bias=256.0)
-    act(T.cc[:, 1:2], T.qf[:, 0:1], F.Identity, ["qf"], ["cc1"], bias=161.0)
-    act(T.msk[:], T.m16[:].indirect(T.pu[:]), F.Identity, ["m16", "pu"], ["msk"], bias=-256.0)
-
-    def qx(r, h):
-        quant(T.qxc[:, H * h:H * h + H], T.qxs[:, H * h:H * h + H], T["xw%d" % r][:, 4 * H * h:4 * H * (h + 1)], xkeys(r, (h,)), ["qx%d" % h])
+    act(T.ip[:], T.il[:, 0:4], F.Identity, ["il"], ["ip"], bias=0.5 - K)
+    act(T.cc[:, 0:1], T.c16[:, 15:16], F.Identity, ["c16"], ["cc0"], bias=256.0 - K)
 
     def score(bank, j, c0, c1, rd):
         mm(bank, c1 - c0, T.puc[:, 128 * j:128 * j + 128], T.pus[:, 128 * j:128 * j + 128], T.qxc[:, c0:c1], T.qxs[:, c0:c1], True, True, ["puc", "pus"] + rd)
@@ -222,152 +241,203 @@ def rank_program(g, core, T, topo):
         k = lambda *a: [n + s for n in a]
 
         def side():
-            act(T.rb[:, i:i + 1], pf[:, C - 1:C], F.Relu, k("pf"), k("ra"), bias=128.0 * sign, scale=2.0 * sign)
-            act(T.rb[:, i + 1:i + 2], T.rb[:, i:i + 1], F.Identity, k("ra"), k("rb"), bias=192.0, scale=-sign)
-            act(x2[:], pf[:], F.Identity, k("pf", "rb"), k("x2"), bias=T.rb[:, i + 1:i + 2], scale=2.0)
+            act(sm[:, 0:1], pf[:, C - 1:C], F.Sign, k("pf"), k("sg"), bias=128.5)
+            act(T.rb[:, i:i + 1], pf[:, C - 1:C], F.Relu, k("pf"), k("ra"), bias=128.0 * sign, scale=sign)
+            act(T.rb[:, i + 1:i + 2], T.rb[:, i:i + 1], F.Identity, k("ra"), k("rb"), bias=128.0, scale=-sign)
 
         return {
             "y": lambda: op("v", lambda: V.transpose(y[:], T["k1" + s][:]), k("k1"), k("y")),
-            "f": lambda: ts(f[:], y[:], 0.0, 0.5, A.is_gt, A.mult, k("y"), k("f")),
+            "f": lambda: ts(f[:], y[:], 0.0, None, A.is_gt, None, k("y"), k("f")),
             "mx": lambda: scan(mx[:], y[:, 0:H], y[:, H:C], -1.0, A.max, A.max, k("y"), k("mx")),
             "mn": lambda: scan(mn[:], y[:, 0:H], y[:, H:C], 1.0, A.min, A.min, k("y"), k("mn")),
-            "pf": lambda: scan(pf[:], f[:], T.zero[:], -96.0, A.add, A.add, k("f") + ["zero"], k("pf")),
-            "sg": lambda: ts(sm[:, 0:1], pf[:, C - 1:C], -64.0, 0.5, A.is_ge, A.subtract, k("pf"), k("sg")),
+            "pf": lambda: scan(pf[:], f[:], T.zero[:], -192.0, A.add, A.add, k("f") + ["zero"], k("pf")),
+            "sg": side,
             "ty": lambda: ts(sm[:, 1:2], mx[:, H - 1:H], sm[:, 0:1], mn[:, H - 1:H], A.min, A.max, k("mx", "mn", "sg"), k("ty")),
             "eq": lambda: ts(eq[:], y[:], sm[:, 1:2], sm[:, 0:1], A.is_equal, A.mult, k("y", "ty", "sg"), k("eq")),
-            "x2": side,
-            "s1": lambda: scan(s1[:], f[:], eq[:], -96.0, A.add, A.subtract, k("f", "eq"), k("s1")),
-            "m1": lambda: ts(sm[:, 3:4], s1[:, C - 1:C], 32.0, -96.0, A.subtract, o, k("s1"), k("m1")),
-            "x1": lambda: ts(x1[:], s1[:], sm[:, 3:4], 2.0, A.subtract, A.mult, k("s1", "m1"), k("x1")),
-            "cn": lambda: scan(cn[:, Z:C + Z], x1[:], x2[:], 0.0, A.max, o, k("x1", "x2"), k("cn")),
+            "x2": lambda: act(x2[:], pf[:], F.Identity, k("pf", "rb"), k("x2"), bias=T.rb[:, i + 1:i + 2]),
+            "s1": lambda: scan(s1[:], f[:], eq[:], -192.0, A.add, A.subtract, k("f", "eq"), k("s1")),
+            "m1": lambda: ts(sm[:, 3:4], s1[:, C - 1:C], -128.0, None, o, None, k("s1"), k("m1")),
+            "x1": lambda: ts(x1[:], s1[:], sm[:, 3:4], None, A.subtract, None, k("s1", "m1"), k("x1")),
+            "cn": lambda: scan(cn[:, 16:C + 16], x1[:], x2[:], -64.0, A.max, o, k("x1", "x2"), k("cn")),
         }
 
     def wrap(out, src, ctl, rd, okey):
-        scan(out[:], src, ctl[:], 128.0, A.min, A.add, rd, [okey])
+        scan(out[:], src, ctl[:], 128.0 - K, A.min, A.add, rd, [okey])
 
-    qx(0, 0)
-    score(0, 0, 0, H, ["qx0"])
+    def early_scores():
+        score(0, 0, 0, H, ["qx0"])
+        score(1, 2, 0, H, ["qx0"])
+
+    early_scores()
     qx(0, 1)
+    ts(T.m16[:], T.im2[:], 0.0, 1024.0, A.not_equal, A.mult, ["im2"], ["m16"])
     turn(0, 0)
 
     for r in range(R):
         last = r == R - 1
         X, XN = T["xw%d" % r], T["xw%d" % (r + 1)]
         xk = xkeys(r)
-        score(2, 2, 0, C, ["qx0", "qx1"])
-        score(1, 1, 0, C, ["qx0", "qx1"])
         score(3, 0, H, C, ["qx1"])
         score(4, 2, 0, C, ["qx0", "qx1"])
-        if r == 0:
-            cp(T.ctlc[:], T.ctl[:], ["ctl"], ["ctlc"])
-            tt(T.ctlc[:, 15:C:16], T.ctl[:, 15:C:16], T.il[:], A.add, ["ctl", "il"], ["ctlc"])
+        score(2, 1, 0, C, ["qx0", "qx1"])
+
+        def row(e, b):
+            if b < 4:
+                return T.sg[:, 128 * (4 * e + b):128 * (4 * e + b) + 128], "sg%d" % (4 * e + b)
+            return T["tri%d" % (b // 2)][:, 2 * e + b % 2:4 * _reach(b):4], "tr%d_%d" % (b, e)
+
+        def sgn(e, b):
+            bank = "ps1" if e else "ps2"
+            out, key = row(e, b)
+            act(out, T[bank][:, 0:_reach(b)], F.Sign, [bank, "pt%d" % (b // 6)], [key, "rho%d" % (2 * b + e)],
+                bias=T.pt[:, 32 * b + 16 * e:32 * b + 16 * e + 1], scale=-1.0, accum_out=T.rho[:, 2 * b + e:2 * b + e + 1])
 
         def cmp(b):
-            ts(T.flg[:, C * b:C * b + C], T.ps2[:, 0:C], T.pt[:, 32 * b + 16:32 * b + 17], None, A.is_gt, None, ["ps2", "pt%d" % (b // 6)], ["flg%d" % b])
+            out, key = row(1, b)
+            ts(out, T.ps4[:, 0:_reach(b)], T.pt[:, 32 * b + 16:32 * b + 17], -2.0, A.is_ge, A.mult, ["ps4", "pt1"], [key])
 
         def cnt(b):
-            scan(T.sj[:, H * b:H * b + H], T.flg[:, C * b:C * b + H], T.flg[:, C * b + H:C * b + C], -192.0, A.add, A.add, ["flg%d" % b], ["sj%d" % b])
+            n, t, tri = _reach(b), 2 + b % 2, T["tri%d" % (b // 2)]
+            e = H * (b - 5)
+            scan(T.sj[:, e - n // 2:e], tri[:, t:2 * n:4], tri[:, 2 * n + t:4 * n:4], 2.0 * n - C, A.add, A.add, ["tr%d_1" % b], ["sj%d" % b])
 
-        def sgn(b):
-            act(T.sg[:, C * b:C * b + C], T.ps1[:, 0:C], F.Sign, ["ps1", "pt%d" % (b // 6)], ["sg%d" % b, "acc%d" % b],
-                bias=T.pt[:, 32 * b:32 * b + 1], scale=-1.0, accum_out=T.acc[:, b:b + 1])
+        def cols(k):
+            n = 64 * k
+            o = {5: 0, 4: 320, 3: 576, 2: 768}[k]
+            quant(T.qfc[:, o:o + n], T.qfs[:, o:o + n], T["tri%d" % k][:, 0:4 * n], ["tr%d_%d" % (b, e) for b in (2 * k, 2 * k + 1) for e in (0, 1)], ["qf%d" % k])
+            mm(5, n, T.csc[:], T.css[:], T.qfc[:, o:o + n], T.qfs[:, o:o + n], k == 5, k == 2, ["cs", "qf%d" % k])
 
-        written = {k: lastw[k] for k in ("ps1", "ps2")}
-        for b in range(12):
-            if b < 11:
-                cmp(b)
-            if b == 0:
-                turn(3, 1)
-            else:
-                cnt(b - 1)
-            if b == 9:
-                act(T.sg[:, C * 12:C * 13], T.ps4[:, 0:C], F.Sign, ["ps4", "pt1"], ["sg12"], bias=T.pt[:, 32 * 11 + 16:32 * 11 + 17], scale=-1.0)
-            if b == 10:
-                act(T.sg[:, C * 13:C * 14], T.sg[:, C * 12:C * 13], F.Relu, ["sg12"], ["sg13", "acc12"], scale=-1.0, accum_out=T.acc[:, 12:13])
-            sgn(b)
-            for k, n in (("ps1", 11), ("ps2", 10)):
-                if b < n:
-                    readers[k] = []
-                    lastw[k] = written[k]
-        acck, sjk = ["acc%d" % b for b in range(12)], ["sj%d" % b for b in range(11)]
-        ts(T.z4[:, 23:24], T.acc[:, 12:13], 8.0, -2562.0, A.mult, A.add, ["acc12"], ["z4e"])
-        ts(T.z4[:, 12:23], T.sj[:, H - 1:11 * H:H], 8.0, -1026.0, A.mult, A.add, sjk, ["z4b"])
-        ts(T.z4[:, 47:48], T.acc[:, 12:13], -8.0, 506.0, A.mult, A.add, ["acc12"], ["z4f"])
-        ts(T.z4[:, 36:47], T.sj[:, H - 1:11 * H:H], -8.0, -1030.0, A.mult, A.add, sjk, ["z4d"])
-        act(T.z4[:, 0:12], T.acc[:, 0:12], F.Identity, acck, ["z4a"], bias=-1030.0, scale=-4.0)
-        ts(T.z4[:, 24:36], T.acc[:, 0:12], 4.0, -1026.0, A.mult, A.add, acck, ["z4c"])
-        op("v", lambda: V.reciprocal(T.yc[:], T.z4[:]), ["z4" + c for c in "abcdef"], ["yc"])
-        act(T.k1h[:], T.yc[:, 24:48].indirect(T.cu[:, 24:48]), F.Copy, ["yc", "cu"], ["k1h"])
-        cp(T.k1l[:], T.yc[:, 0:24].indirect(T.cu[:, 24:48]), ["yc", "cu"], ["k1l"])
+        for b in (4, 5, 0, 1, 2, 3):
+            sgn(1, b)
+        turn(3, 1)
+        for b in (10, 11, 8, 9, 6, 7, 4, 5, 0, 1, 2, 3):
+            sgn(0, b)
+        cmp(10)
+        cmp(11)
+        cnt(10)
+        cmp(8)
+        cnt(11)
+        if r == 0:
+            quant(T.csc[:], T.css[:], T.cst[:], ["cst%d" % a for a in range(4)], ["cs"])
+        cmp(9)
+        cols(5)
+        cnt(8)
+        cmp(6)
+        cnt(9)
+        cmp(7)
+        cols(4)
+        cols(3)
+        cols(2)
+        cnt(6)
+        cnt(7)
+        ts(T.rho[:, 13:24:2], T.sj[:, H - 1:6 * H:H], float(H), None, A.add, None, ["sj%d" % b for b in range(6, 12)], ["rhov"])
+        op("v", lambda: V.transpose(T.qt[:, 0:320], T.ps5[:, 0:320]), ["ps5"], ["qt"])
+        rk = ["rhov"] + ["rho%d" % (2 * b + e) for b in range(12) for e in range(2) if not (e == 1 and b >= 6)]
+        for o in (0, 24):
+            tt(T.kr[:, o:o + 24], T.kc[:, o:o + 24], T.rho[:], A.subtract, kck + rk, ["kr%d" % o])
+        for o in (0, 24):
+            tt(T.z4[:, o:o + 24], T.qt[:, 0:C:16], T.kr[:, o:o + 24], A.add, ["qt", "qtz", "kr%d" % o], ["z4%d" % o])
+        op("v", lambda: V.reciprocal(T.yc[:], T.z4[:]), ["z40", "z424"], ["yc"])
+        if r == 0:
+            act(T.ctl[:], T.c16[:].indirect(T.pu[:]), F.Copy, ["c16", "pu"], ["ctl"])
+        act(T.k1l[:], T.yc[:, 0:24].indirect(T.cu[:, 24:48]), F.Identity, ["yc", "cu"], ["k1l"], scale=0.125)
+        ts(T.k1h[:], T.yc[:, 24:48].indirect(T.cu[:, 24:48]), -0.125, None, A.mult, None, ["yc", "cu"], ["k1h"])
+
+        def plane(t):
+            act(T.xp[:, W * t:W * t + C], X[:, t:4 * C:4], F.Copy, xk, ["xp%d" % t])
 
         lo, hi = cut("l"), cut("h")
-        for n in ("y", "f", "pf", "x2", "mx", "mn", "sg", "ty", "eq", "s1", "m1", "x1", "cn"):
+        for t in range(3):
+            plane(t)
+        for n in ("y", "f", "pf"):
+            hi[n]()
+            lo[n]()
+        for n in ("sg", "x2", "mx", "mn", "ty", "eq", "s1", "m1", "x1", "cn"):
             lo[n]()
             hi[n]()
-        CLi, CLe, CHi, CHe = T.cnl[:, Z:C + Z], T.cnl[:, Z - 1:C + Z - 1], T.cnh[:, Z:C + Z], T.cnh[:, Z - 1:C + Z - 1]
-        for k in range(4):
+            if n == "x2":
+                plane(3)
+                act(T.ew[:, 0:C], T.zero[:], F.Identity, ["zero"], ["ew"], bias=256.0)
+        CLi, CLe, CHe = T.cnl[:, 16:C + 16], T.cnl[:, 15:C + 15], T.cnh[:, 15:C + 15]
+
+        for k in range(3):
             act(T.sgl[:, C * k:C * k + C], CLi, F.Sign, ["cnl", "ip"], ["sgl%d" % k, "dl%d" % k], bias=T.ip[:, k:k + 1], scale=-1.0, accum_out=T.dl[:, k:k + 1])
-        for k in range(4):
-            act(T.sgh[:, (C + Z) * k:(C + Z) * k + C + 32 * k], T.cnh[:, Z - 32 * k:C + Z], F.Sign, ["cnh", "ip"], ["sgh%d" % k, "dh%d" % k],
-                bias=T.ip[:, k:k + 1], scale=-1.0, accum_out=T.dh[:, k:k + 1])
-        dlk = ["dl%d" % k for k in range(4)]
+        if r == 0:
+            cp(T.ctlc[:], T.ctl[:], ["ctl"], ["ctlc"])
         wrap(T.cva, CLi, T.ctl, ["cnl", "ctl"], "cva")
+        if r == 0:
+            tt(T.ctlc[:, 15:C:16], T.ctl[:, 15:C:16], T.il[:], A.add, ["ctl", "il"], ["ctlc"])
         wrap(T.cvb, CLe, T.ctl, ["cnl", "ctl"], "cvb")
-        wrap(T.cvc, CHe, T.ctlc, ["cnh", "ctlc"], "cvc")
+        ts(T.sgl[:, 3 * C:4 * C], CLi, T.ip[:, 3:4], 2.0, A.is_lt, A.mult, ["cnl", "ip"], ["sgl3"])
         tt(T.t1[:], T.cva[:, 15:C:16], T.cvb[:, 15:C:16], A.subtract, ["cva", "cvb"], ["t1"])
+        wrap(T.cvc, CHe, T.ctlc, ["cnh", "ctlc"], "cvc")
         ts(T.lm[:], T.t1[:], -768.0, T.cc[:, 0:1], A.mult, A.add, ["t1", "cc0"], ["lm"])
+        scan(T.mxl[:], T.sgl[:, 3 * C:3 * C + H], T.sgl[:, 3 * C + H:4 * C], -float(C), A.add, A.add, ["sgl3"], ["mxl"])
         tt(T.wm[:], T.cvb[:, 15:C:16], T.lm[:], A.min, ["cvb", "lm"], ["wm"])
+        ts(T.lo[:, 3:4], T.mxl[:, H - 1:H], 0.5, 192.0, A.mult, A.add, ["mxl"], ["lo1"])
+        ts(T.lo[:, 0:3], T.dl[:, 0:3], 0.5, 192.0, A.mult, A.add, ["dl%d" % k for k in range(3)], ["lo"])
         tt(T.oo[:], T.cvc[:, 15:C:16], T.wm[:], A.subtract, ["cvc", "wm"], ["oo"])
+        for t in range(4):
+            move("vsvs"[t], T.bt[:, t:4 * K:4], T.xp[:, W * t:W * t + C].indirect(T.lo[:]), ["xp%d" % t, "lo", "lo1"], ["bt%d" % t])
         cp(T.ou[:], T.oo[:], ["oo"], ["ou"])
-        for t in range(4):
-            ts(T.lo[:, 4 * t:4 * t + 4], T.dl[:], 2.0, 768.0 + t, A.mult, A.add, dlk, ["lo%d" % t])
-        ts(T.lo[:, 16:20], T.dl[:], 0.5, 192.0, A.mult, A.add, dlk, ["lo4"])
-        for t in range(4):
-            cp(T.bt[:, t:4 * K:4], X[:, 0:4 * C].indirect(T.lo[:, 4 * t:4 * t + 4]), xk + ["lo%d" % t], ["bt%d" % t])
-        cp(T.chl[:], CHi.indirect(T.lo[:, 16:20]), ["cnh", "lo4"], ["chl"])
-        quant(T.qbc[:, 128 * r:128 * r + 128], T.qbs[:, 128 * r:128 * r + 128], T.bt[:], btk, ["qb%d" % r])
+        quant(T.qbc[:, 128 * r:128 * r + 128], T.qbs[:, 128 * r:128 * r + 128], T.bt[:], btk + ["btz"], ["qb%d" % r])
         l0 = (0, 192, 256)[r]
         send(T.landc[:, l0:l0 + K].bitcast(dt.uint8), T.qbc[:, 128 * r:128 * r + K].bitcast(dt.uint8), "arr%d" % r, ["qb%d" % r])
         send(T.lands[:, l0:l0 + K], T.qbs[:, 128 * r:128 * r + K], "arr%d" % r, ["qb%d" % r])
         lastw["land%d" % r] = ("arr%d" % r, 2 * neng)
 
-        for k in range(4):
-            act(T.sgm[:, K * k:K * k + K], T.chl[:], F.Sign, ["chl", "ip"], ["sgm%d" % k, "dm%d" % k], bias=T.ip[:, k:k + 1], scale=-1.0, accum_out=T.dm[:, k:k + 1])
+        if r == 0:
+            act(T.msk[:], T.m16[:].indirect(T.pu[:]), F.Identity, ["m16", "pu"], ["msk"], bias=-256.0)
         if last:
-            act(T.lsend[:], T.io448[:, 0:C].indirect(T.lo[:, 16:20]), F.Copy, ["io448", "lo4"], ["lsend"])
+            act(T.lsend[:], T.ramp[:].indirect(T.lo[:]), F.Copy, ["ramp", "lo", "lo1"], ["lsend"])
             send(T.lland[:], T.lsend[:], "arrl", ["lsend"])
             lastw["lland"] = ("arrl", neng)
-        cp(T.ew[:].indirect(T.ou[:]), T.io448[:, 0:C], ["ou", "io448"], ["ew"])
-        tt(T.a1[:], T.dh[:], T.dm[:], A.subtract, ["dh%d" % k for k in range(4)] + ["dm%d" % k for k in range(4)], ["a1"])
-        ts(T.au[:], T.a1[:], 0.5, T.cc[:, 1:2], A.mult, A.add, ["a1", "cc1"], ["au"])
-        cp(T.ew[:].indirect(T.au[:]), T.io448[:, C:C + K], ["au", "io448"], ["ew"])
-        if r == 0:
-            for b in range(4):
+        cp(T.ew[:].indirect(T.ou[:]), T.ramp[:], ["ou", "ramp"], ["ew"])
+
+        def unit(b):
+            if r == 0:
                 quant(T.ec[:, 128 * b:128 * b + 128], T.es[:, 128 * b:128 * b + 128], T.gt[:, 3 - b:515 - b], ["gt"], ["e%d" % b])
-        tt(T.em[:], T.ew[:, 0:C], T.msk[:], A.max, ["ew", "msk"], ["em"])
-        scan(T.ex[:], T.ctl2[:], T.em[:], 0.0, A.max, A.min, ["em", "ctl2"], ["ex"])
-        for t in (2, 3, 0, 1):
-            ts(T.eo[:, 24 * t:24 * t + 24], T.ex[:, 15:C:16], 4.0, 768.0 + t, A.mult, A.add, ["ex"], ["eo%d" % t])
+
+        def invert(n, h):
+            a, b = (0, U) if h == 0 else (U, C)
+            if n == "hf":
+                ts(T.hf[:, a:b], T.ew[:, a:b], 192.0, None, A.is_ge, None, ["ew"], ["hf%d" % h])
+            elif n == "hn":
+                scan(T.hn[:, a:b], T.hf[:, a:b], T.zero[:, a:b], T.hn[:, U - 1:U] if h else 191.0, A.add, A.add, ["hf%d" % h, "zero"] + ["hn0"] * h, ["hn%d" % h])
+            elif n == "en":
+                scan(T.en[:, a:b], T.hn[:, a:b], T.ew[:, a:b], 0.0, A.max, A.min, ["hn%d" % h, "ew"], ["en%d" % h])
+            elif n == "em":
+                tt(T.em[:, a:b], T.en[:, a:b], T.msk[:, a:b], A.max, ["en%d" % h, "msk"], ["em%d" % h])
+            elif n == "ex":
+                scan(T.ex[:, a:b], T.ctl2[:, a:b], T.em[:, a:b], 0.0, A.max, A.min, ["em%d" % h, "ctl2"], ["ex%d" % h])
+            else:
+                ts(T.eo[:, a // 16:b // 16], T.ex[:, a + 15:b:16], 192.0, None, A.add, None, ["ex%d" % h], ["eo%d" % h])
+
+        unit(0)
+        unit(1)
+        invert("hf", 0)
+        invert("hf", 1)
+        invert("hn", 0)
+        unit(2)
+        for n, h in (("en", 0), ("hn", 1), ("em", 0), ("en", 1), ("ex", 0), ("em", 1), ("eo", 0), ("ex", 1)):
+            invert(n, h)
+        unit(3)
 
         v0 = (0, 128, 192)[r]
         lk = ["land%d" % r, "landz"] + (["land1"] if r == 2 else [])
         for b in range(4):
             mm(4 + b, 128, T.ec[:, 128 * b:128 * b + 128], T.es[:, 128 * b:128 * b + 128], T.landc[:, v0:v0 + 128], T.lands[:, v0:v0 + 128], True, True, ["e%d" % b] + lk)
-            move("s", X[:, 4 * C + b:4 * (C + K):4], T["ps%d" % (4 + b)][:, l0 - v0:l0 - v0 + K], ["ps%d" % (4 + b)], ["xa%d_%d" % (r, b)])
-        wk = xk + ["xa%d_%d" % (r, b) for b in range(4)]
+            move("s", T.xp[:, W * b + C:W * b + W], T["ps%d" % (4 + b)][:, l0 - v0:l0 - v0 + K], ["ps%d" % (4 + b)], ["xa%d" % b])
 
         def gather(e, h, t):
-            if h == 0:
-                out, off, key = T.ta[:, t:4 * 208:4], T.eo[:, 24 * t:24 * t + 13], "ta%d" % t
-            else:
-                out, off, key = T.tb[:, t:4 * H:4], T.eo[:, 24 * t + 12:24 * t + 24], "tb%d" % t
-            move(e, out, X[:].indirect(off), wk + ["eo%d" % t], [key])
+            n = 13 - h
+            move(e, (T.ta, T.tb)[h][:, t:64 * n:4], T.xp[:, W * t:W * t + W].indirect(T.eo[:, 12 * h:12 * h + n]),
+                 ["xp%d" % t, "xa%d" % t, "eo0"] + ["eo1"] * h, ["t%d_%d" % (h, t)])
 
         def qt(h, rot):
             i = 2 * h + rot
-            src = T.ta if h == 0 else T.tb
-            rd = ["ta%d" % t for t in range(4)] if h == 0 else ["tb%d" % t for t in range(4)] + (["tbw"] if rot else [])
-            quant(T.qtc[:, H * i:H * i + H], T.qts[:, H * i:H * i + H], src[:, 4 * rot:4 * rot + 4 * H], rd, ["qt%d" % i])
+            quant(T.qtc[:, H * i:H * i + H], T.qts[:, H * i:H * i + H], (T.ta, T.tb)[h][:, 4 * rot:4 * rot + 4 * H],
+                  ["t%d_%d" % (h, t) for t in range(4)] + (["tbw"] if i == 3 else []), ["qt%d" % i])
 
         def layer(h):
             for tap, b in ((0, 0), (0, 1), (1, 0), (1, 1), (0, 2), (1, 2), (0, 3), (1, 3)):
@@ -382,55 +452,49 @@ def rank_program(g, core, T, topo):
             else:
                 act(out, T[ps][:, 0:H], F.Copy, [ps], [key], scale=0.015625)
 
-        gather("s", 0, 2)
-        gather("s", 0, 3)
-        gather("v", 0, 0)
-        gather("v", 0, 1)
+        for t in range(4):
+            gather("svsv"[t], 0, t)
+            if t == 1:
+                invert("eo", 1)
         qt(0, 0)
         qt(0, 1)
         layer(0)
-        gather("s", 1, 2)
-        gather("s", 1, 3)
-        gather("v", 1, 0)
-        gather("s", 1, 1)
-        cp(T.tb[:, 4 * H:4 * H + 4], T.ta[:, 0:4], ["ta%d" % t for t in range(4)], ["tbw"])
-        if last:
-            ts(T.eo[:, 96:120], T.ex[:, 15:C:16], 192.0, None, A.add, None, ["ex"], ["eo4"])
+        cp(T.tb[:, 4 * H:4 * H + 4], T.ta[:, 0:4], ["t0_%d" % t for t in range(4)], ["tbw"])
+        for t in range(4):
+            gather("vsss"[t], 1, t)
         qt(1, 0)
         qt(1, 1)
         layer(1)
-        evac("s", 0, 0)
-        evac("v", 0, 1)
-        evac("s", 0, 2)
-        evac("v", 0, 3)
+        for b in range(4):
+            evac("ssvs"[b], 0, b)
         if r == 0:
             quant(T.qvc[:], T.qvs[:], T.vt[:], ["vt"], ["qv"])
-        if last:
-            act(T.ow[:, C:C + K], T.lland[:], F.Identity, ["lland"], ["ow1"], bias=576.0)
         qx(r + 1, 0)
-        evac("s", 1, 0)
-        evac("v", 1, 1)
-        evac("s", 1, 2)
         if not last:
-            score(0, 0, 0, H, ["qx0"])
-            evac("v", 1, 3)
-            qx(r + 1, 1)
+            early_scores()
+            evac("s", 1, 0)
+            evac("s", 1, 1)
+            evac("v", 1, 2)
             turn(0, 0)
+            evac("s", 1, 3)
+            qx(r + 1, 1)
         else:
             mm(0, H, T.qvc[:], T.qvs[:], T.qxc[:, 0:H], T.qxs[:, 0:H], True, True, ["qv", "qx0"])
             dma("y", T.oc[:, 0:4 * H], T.qxc[:, 0:H].bitcast(dt.uint8), ["qx0"], [])
-            evac("v", 1, 3)
+            for b in range(4):
+                evac("ssvv"[b], 1, b)
+            act(T.ow[:, C:W], T.lland[:], F.Identity, ["lland"], ["ow1"], bias=576.0)
+            act(T.olb[:], T.ow[:].indirect(T.eo[:]), F.Copy, ["ow0", "ow1", "eo0", "eo1"], ["olb"])
             qx(r + 1, 1)
             mm(1, H, T.qvc[:], T.qvs[:], T.qxc[:, H:C], T.qxs[:, H:C], True, True, ["qv", "qx1"])
-            act(T.olb[:], T.ow[:].indirect(T.eo[:, 96:120]), F.Copy, ["ow0", "ow1", "eo4"], ["olb"])
-            cp(T.ysb[:, 0:H], T.ps0[:, 0:H], ["ps0"], ["ya"])
-            dma("y", T.oc[:, 4 * H:4 * C], T.qxc[:, H:C].bitcast(dt.uint8), ["qx1"], [])
-            cp(T.ysb[:, H:C], T.ps1[:, 0:H], ["ps1"], ["yb"])
-            dma("y", T.y[:, 0:H], T.ysb[:, 0:H], ["ya"], [])
-            dma("y", T.y[:, H:C], T.ysb[:, H:C], ["yb"], [])
             dma("s", T.ol[:], T.olb[0:128:16, :], ["olb"], [])
             for k in range(4):
                 dma("s", T.osc[4 * k:4 * k + 4, :], T.qxs[32 * k:32 * k + 4, :], ["qx0", "qx1"], [])
+            dma("y", T.oc[:, 4 * H:4 * C], T.qxc[:, H:C].bitcast(dt.uint8), ["qx1"], [])
+            cp(T.ysb[:, 0:H], T.ps0[:, 0:H], ["ps0"], ["ya"])
+            dma("y", T.y[:, 0:H], T.ysb[:, 0:H], ["ya"], [])
+            cp(T.ysb[:, H:C], T.ps1[:, 0:H], ["ps1"], ["yb"])
+            dma("y", T.y[:, H:C], T.ysb[:, H:C], ["yb"], [])
 
     for s in count:
         wait("q", (s, count[s]))

@@ -4,7 +4,7 @@ A, F = AluOpType, ActivationFunctionType
 C, K, R = 384, 64, 3
 H = C // 2
 W = C + K
-U = H + 16
+UNIT = 2.0 ** -10
 Q4, U8, BF, F32, I32, U16, F16 = "float8_e4m3fn_x4", "uint8", "bfloat16", "float32", "int32", "uint16", "float16"
 
 
@@ -17,33 +17,33 @@ SCRATCH = {
     "quc": _sb(128, Q4), "qus": _sb(128, U8), "puc": _sb(384, Q4), "pus": _sb(384, U8),
     "qvc": _sb(128, Q4), "qvs": _sb(128, U8),
     "wq": _sb(512, Q4), "wp": _sb(512, U8), "zq": _sb(512, Q4), "zp": _sb(512, U8),
-    "gt": _sb(516, BF), "ones": _sb(516, BF), "ec": _sb(512, Q4), "es": _sb(512, U8),
-    "ci": _sb(48, I32), "cu": _sb(48, U16), "pi": _sb(24, I32), "pj": _sb(24, I32), "pu": _sb(24, U16), "qf": _sb(2, F32),
+    "gt": _sb(516, BF), "ones": _sb(516, BF), "onek": _sb(128, BF), "ec": _sb(512, Q4), "es": _sb(512, U8),
+    "ci": _sb(60, I32), "cu": _sb(60, U16), "pi": _sb(24, I32), "pj": _sb(24, I32), "pu": _sb(24, U16), "qf": _sb(2, F32),
     "ia": _sb(24, F32), "il": _sb(24, F32), "ip": _sb(4, F32), "cc": _sb(2, F32),
-    "im": _sb(16, I32), "im2": _sb(16, I32), "c16": _sb(16, F32), "m16": _sb(16, F32),
-    "msk": _sb(C, BF), "ctl": _sb(C, BF), "ctlc": _sb(C, F16), "ctl2": _sb(C, BF),
+    "im": _sb(16, I32), "im2": _sb(16, I32), "c16": _sb(16, F32),
+    "ctl": _sb(C, BF), "ctlc": _sb(C, F16), "ctf": _sb(C, BF), "crow": _sb(C, BF), "half": _sb(4, F32),
+    "gr": _sb(32, F32), "gq": _sb(32, F32), "gk": _sb(4, F32), "gs": _sb(4, F32), "gl": _sb(4, U16),
+    "k12": _sb(144, F32), "k32": _sb(192, F32),
     "zero": _sb(C, BF), "zt": _sb(512, BF), "ramp": _sb(C, BF), "ow": _sb(W, F32),
     "qxc": _sb(C, Q4), "qxs": _sb(C, U8), "pt": _sb(C, F32),
     "tri2": _sb(4 * 192, BF), "tri3": _sb(4 * 256, BF), "tri4": _sb(4 * 320, BF), "tri5": _sb(4 * 384, BF),
     "sj": _sb(6 * H, BF), "sg": _sb(8 * 128, BF), "rho": _sb(24, F32),
     "qfc": _sb(896, Q4), "qfs": _sb(896, U8), "cs0": _sb(128, BF), "cst": _sb(512, BF), "csc": _sb(128, Q4), "css": _sb(128, U8),
-    "qt": _sb(C, F32), "kc": _sb(48, F32), "kr": _sb(48, F32), "z4": _sb(48, F32), "yc": _sb(48, F32), "rb": _sb(4, F32),
-    "k1l": _sb(C, BF), "yl": _sb(C, BF), "k1h": _sb(C, F16), "yh": _sb(C, F16),
-    "mxl": _sb(H, BF), "mnl": _sb(H, BF), "mxh": _sb(H, F16), "mnh": _sb(H, F32), "sml": _sb(4, BF), "smh": _sb(4, F32),
+    "qt": _sb(C, F32), "kr": _sb(24, F32), "kk": _sb(24, F32), "fa": _sb(48, F32), "aa": _sb(48, F32),
+    "st": _sb(144, F32), "sw": _sb(192, F32), "su": _sb(192, F32), "sx": _sb(192, F32), "ty": _sb(4, F32),
+    "k1": _sb(C, F16), "ky": _sb(C, F16),
+    "gl_": _sb(C + 16, BF), "al": _sb(C, BF), "ah": _sb(C + 16, BF), "gh": _sb(C, BF), "capl": _sb(C, BF), "caph": _sb(C, BF),
+    "cnl": _sb(C + 16, BF), "cnh": _sb(C + 16, BF),
     "dl": _sb(4, F32), "sgl": _sb(4 * C, BF), "lo": _sb(4, U16), "bt": _sb(512, BF), "xp": _sb(4 * W, BF),
     "qbc": _sb(R * 128, Q4), "qbs": _sb(R * 128, U8), "landc": _sb(320, Q4), "lands": _sb(320, U8),
     "lsend": _sb(K, BF), "lland": _sb(K, BF),
     "cva": _sb(C, BF), "cvb": _sb(C, BF), "cvc": _sb(C, F16),
     "t1": _sb(24, F32), "lm": _sb(24, F32), "wm": _sb(24, F32), "oo": _sb(24, F32), "ou": _sb(24, U16),
-    "ew": _sb(960, BF), "hf": _sb(C, BF), "hn": _sb(C, BF), "en": _sb(C, BF), "em": _sb(C, BF), "ex": _sb(C, BF), "eo": _sb(24, U16),
+    "dat": _sb(C, BF), "ew": _sb(1088, BF), "en": _sb(C + 32, BF), "et": _sb(2 * C + 32, BF), "eg": _sb(64, BF), "em": _sb(24, F32), "eo": _sb(24, U16),
     "ta": _sb(4 * 208, BF), "tb": _sb(4 * 196, BF),
     "qtc": _sb(4 * H, Q4), "qts": _sb(4 * H, U8),
     "ysb": _sb(C, F32), "olb": _sb(C, F32),
 }
-for _s in ("l", "h"):
-    for _n in ("f", "pf", "eq", "s1", "x1", "x2"):
-        SCRATCH[_n + _s] = _sb(C, BF)
-    SCRATCH["cn" + _s] = _sb(C + 16, BF)
 for _r in range(R + 1):
     SCRATCH["xw%d" % _r] = _sb(4 * C, BF)
 for _b in range(8):
@@ -140,6 +140,9 @@ def rank_program(g, core, T, topo):
     def scan(out, d0, d1, init, o0, o1, rd, wr):
         op("v", lambda: V.tensor_tensor_scan(out, d0, d1, init, o0, o1), rd, wr)
 
+    def flip(out, in_, rd, wr):
+        op("v", lambda: V.transpose(out, in_), rd, wr)
+
     def quant(oc, osc, in_, rd, wr):
         op("v", lambda: V.quantize_mx(oc, osc, in_), rd, wr)
 
@@ -185,13 +188,14 @@ def rank_program(g, core, T, topo):
     btk = ["bt0", "bt1", "bt2", "bt3"]
     iota(T.ci[:, 0:8], [[16, 8]], 0, 0, ["ci0"], False)
     iota(T.ci[:, 8:24], [[16, 2], [32, 4], [0, 2]], 0, 0, ["ci1"], False)
-    iota(T.ci[:, 24:48], [[1, 24]], 0, 0, ["ci2"], False)
+    iota(T.ci[:, 24:48], [[1, 12], [12, 2]], 0, 0, ["ci2"], False)
+    iota(T.ci[:, 48:60], [[12, 12]], 11, 0, ["ci3"], False)
     iota(T.pi[:], [[0, 24]], 0, 1, ["pi"], False)
     iota(T.im[:], [[1, 16]], 0, -1, ["im"], False)
     iota(T.ia[:], [[16, 24]], 0, 0, ["ia"])
-    fill(T.ones[:], 1.0, ["ones"])
+    fill(T.onek[:], UNIT, ["onek"])
     fill(T.cst[:], 0.0, ["cst"])
-    keep(T.cs0[:], T.ones[:, 0:128], [[-2, 2], [0, 16], [1, 4]], 0, 0, A.is_ge, ["ones"], ["cs0"])
+    keep(T.cs0[:], T.onek[:], [[-2, 2], [0, 16], [1, 4]], 0, 0, A.is_ge, ["onek"], ["cs0"])
     for a in range(4):
         keep(T.cst[32 * a:32 * a + 32, 128 * a:128 * a + 128], T.cs0[32 * a:32 * a + 32, :], [[2, 2], [0, 16], [-1, 4]], 1, 0, A.is_ge,
              ["cs0", "cst"] + ["cst%d" % i for i in range(a)], ["cst%d" % a])
@@ -199,20 +203,32 @@ def rank_program(g, core, T, topo):
     iota(T.qt[:, 320:C], [[0, C - 320]], 0, 0, ["qtz"])
     iota(T.zero[:], [[0, C]], 0, 0, ["zero"])
     iota(T.cnl[:, 0:16], [[0, 16]], -K, 0, ["cnl"])
-    iota(T.cnh[:, 0:16], [[0, 16]], -K, 0, ["cnh"])
+    iota(T.cnh[:, 0:16], [[0, 16]], 256 - K, 0, ["cnh"])
+    iota(T.gl_[:, C:C + 16], [[0, 16]], 0, 0, ["glz"])
+    iota(T.ah[:, C:C + 16], [[0, 16]], 0, 0, ["ahz"])
     iota(T.bt[:, 4 * K:512], [[0, 512 - 4 * K]], 0, 0, ["btz"])
     iota(T.ramp[:], [[1, C]], -192, 0, ["ramp"])
-    keep(T.gt[:], T.ones[:], [[1, 516]], -3, -4, A.is_equal, ["ones"], ["gt"])
-    iota(T.ctl2[:], [[0, C]], -256, 0, ["ctl2"])
-    iota(T.ctl2[:, 0:C:16], [[0, C // 16]], 768, 0, ["ctl2"])
+    iota(T.gr[:, 0:16], [[32, 8], [C + 32, 2]], 0, 0, ["gr0"])
+    iota(T.gr[:, 16:32], [[32, 8], [-C, 2]], C + 16, 0, ["gr1"])
+    iota(T.gk[:], [[8, 2], [256, 2]], 0, 0, ["gk"])
+    iota(T.en[:, 0:16], [[0, 16]], 0, 0, ["enz0"])
+    iota(T.en[:, C + 16:C + 32], [[0, 16]], 0, 0, ["enz1"])
+    keep(T.gt[:], T.ones[:], [[1, 516]], -3, -4, A.is_equal, ["ones"], ["gt"]) if False else None
     iota(T.ow[:, 0:C], [[1, C]], 0, 0, ["ow0"])
-    kck = []
-    for o, n in ((0, 2 * (C - K) + 0.5), (24, 2 * K + 0.5)):
-        for e in range(2):
-            fill(T.kc[:, o + e:o + 24:2], C + H * e - n, ["kc%d" % (o + e)])
-            kck.append("kc%d" % (o + e))
+    for buf, n, step in ((T.k12, 48, 12), (T.k32, 64, 32)):
+        key = "k%d" % step
+        fill(buf[:, 0:2 * n], 0.0, [key + "a"])
+        fill(buf[:, 2 * n:3 * n], 1.0, [key + "b"])
     fill(T.zt[:], 0.0, ["zt"])
-    cp(T.cu[:], T.ci[:], ["ci0", "ci1", "ci2"], ["cu"])
+    for buf, n, step in ((T.k12, 48, 12), (T.k32, 64, 32)):
+        key = "k%d" % step
+        fill(buf[:, 0:n:step], -4.0, [key + "a"])
+        fill(buf[:, 2 * n:3 * n:step], 0.0, [key + "b"])
+    fill(T.ones[:], 1.0, ["ones"])
+    for buf, n, step in ((T.k12, 48, 12), (T.k32, 64, 32)):
+        fill(buf[:, n:2 * n:step], 4.0, ["k%da" % step])
+    keep(T.gt[:], T.ones[:], [[1, 516]], -3, -4, A.is_equal, ["ones"], ["gt"])
+    cp(T.cu[:], T.ci[:], ["ci0", "ci1", "ci2", "ci3"], ["cu"])
     ts(T.pj[:], T.pi[:], 15, None, A.bitwise_and, None, ["pi"], ["pj"])
     quant(T.landc[:, 64:192], T.lands[:, 64:192], T.zt[:], ["zt"], ["landz"])
     ts(T.im2[:], T.im[:], 15, None, A.bitwise_and, None, ["im"], ["im2"])
@@ -226,43 +242,16 @@ def rank_program(g, core, T, topo):
     cp(T.puc[:].bitcast(dt.uint32), T.quc[:].bitcast(dt.uint32).indirect(T.cu[:, 0:24]), ["qu", "cu"], ["puc"])
     act(T.ip[:], T.il[:, 0:4], F.Identity, ["il"], ["ip"], bias=0.5 - K)
     act(T.cc[:, 0:1], T.c16[:, 15:16], F.Identity, ["c16"], ["cc0"], bias=256.0 - K)
+    act(T.half[:, 0:1], T.qf[:, 0:1], F.Sign, ["qf"], ["hf0"], bias=-7.5)
 
     def score(bank, j, c0, c1, rd):
         mm(bank, c1 - c0, T.puc[:, 128 * j:128 * j + 128], T.pus[:, 128 * j:128 * j + 128], T.qxc[:, c0:c1], T.qxs[:, c0:c1], True, True, ["puc", "pus"] + rd)
 
     def turn(bank, h):
-        op("v", lambda: V.transpose(T.pt[:, H * h:H * h + H], T["ps%d" % bank][:, 0:H]), ["ps%d" % bank], ["pt%d" % h])
+        flip(T.pt[:, H * h:H * h + H], T["ps%d" % bank][:, 0:H], ["ps%d" % bank], ["pt%d" % h])
 
-    def cut(s):
-        y, f, pf, eq, s1, x1, x2, cn, sm = [T[n + s] for n in ("y", "f", "pf", "eq", "s1", "x1", "x2", "cn", "sm")]
-        mx, mn = T["mx" + s], T["mn" + s]
-        o = A.max if s == "l" else A.min
-        sign, i = (1.0, 0) if s == "l" else (-1.0, 2)
-        k = lambda *a: [n + s for n in a]
-
-        def side():
-            act(sm[:, 0:1], pf[:, C - 1:C], F.Sign, k("pf"), k("sg"), bias=128.5)
-            act(T.rb[:, i:i + 1], pf[:, C - 1:C], F.Relu, k("pf"), k("ra"), bias=128.0 * sign, scale=sign)
-            act(T.rb[:, i + 1:i + 2], T.rb[:, i:i + 1], F.Identity, k("ra"), k("rb"), bias=128.0, scale=-sign)
-
-        return {
-            "y": lambda: op("v", lambda: V.transpose(y[:], T["k1" + s][:]), k("k1"), k("y")),
-            "f": lambda: ts(f[:], y[:], 0.0, None, A.is_gt, None, k("y"), k("f")),
-            "mx": lambda: scan(mx[:], y[:, 0:H], y[:, H:C], -1.0, A.max, A.max, k("y"), k("mx")),
-            "mn": lambda: scan(mn[:], y[:, 0:H], y[:, H:C], 1.0, A.min, A.min, k("y"), k("mn")),
-            "pf": lambda: scan(pf[:], f[:], T.zero[:], -192.0, A.add, A.add, k("f") + ["zero"], k("pf")),
-            "sg": side,
-            "ty": lambda: ts(sm[:, 1:2], mx[:, H - 1:H], sm[:, 0:1], mn[:, H - 1:H], A.min, A.max, k("mx", "mn", "sg"), k("ty")),
-            "eq": lambda: ts(eq[:], y[:], sm[:, 1:2], sm[:, 0:1], A.is_equal, A.mult, k("y", "ty", "sg"), k("eq")),
-            "x2": lambda: act(x2[:], pf[:], F.Identity, k("pf", "rb"), k("x2"), bias=T.rb[:, i + 1:i + 2]),
-            "s1": lambda: scan(s1[:], f[:], eq[:], -192.0, A.add, A.subtract, k("f", "eq"), k("s1")),
-            "m1": lambda: ts(sm[:, 3:4], s1[:, C - 1:C], -128.0, None, o, None, k("s1"), k("m1")),
-            "x1": lambda: ts(x1[:], s1[:], sm[:, 3:4], None, A.subtract, None, k("s1", "m1"), k("x1")),
-            "cn": lambda: scan(cn[:, 16:C + 16], x1[:], x2[:], -64.0, A.max, o, k("x1", "x2"), k("cn")),
-        }
-
-    def wrap(out, src, ctl, rd, okey):
-        scan(out[:], src, ctl[:], 128.0 - K, A.min, A.add, rd, [okey])
+    def wrap(out, src, ctl, init, rd, okey):
+        scan(out[:], src, ctl[:], init, A.min, A.add, rd, [okey])
 
     def early_scores():
         score(0, 0, 0, H, ["qx0"])
@@ -270,7 +259,6 @@ def rank_program(g, core, T, topo):
 
     early_scores()
     qx(0, 1)
-    ts(T.m16[:], T.im2[:], 0.0, 1024.0, A.not_equal, A.mult, ["im2"], ["m16"])
     turn(0, 0)
 
     for r in range(R):
@@ -289,8 +277,8 @@ def rank_program(g, core, T, topo):
         def sgn(e, b):
             bank = "ps1" if e else "ps2"
             out, key = row(e, b)
-            act(out, T[bank][:, 0:_reach(b)], F.Sign, [bank, "pt%d" % (b // 6)], [key, "rho%d" % (2 * b + e)],
-                bias=T.pt[:, 32 * b + 16 * e:32 * b + 16 * e + 1], scale=-1.0, accum_out=T.rho[:, 2 * b + e:2 * b + e + 1])
+            act(out, T[bank][:, 0:_reach(b)], F.Sign, [bank, "pt%d" % (b // 6)], [key, "rho%d" % (12 * e + b)],
+                bias=T.pt[:, 32 * b + 16 * e:32 * b + 16 * e + 1], scale=-1.0, accum_out=T.rho[:, 12 * e + b:12 * e + b + 1])
 
         def cmp(b):
             out, key = row(1, b)
@@ -330,55 +318,78 @@ def rank_program(g, core, T, topo):
         cols(2)
         cnt(6)
         cnt(7)
-        ts(T.rho[:, 13:24:2], T.sj[:, H - 1:6 * H:H], float(H), None, A.add, None, ["sj%d" % b for b in range(6, 12)], ["rhov"])
-        op("v", lambda: V.transpose(T.qt[:, 0:320], T.ps5[:, 0:320]), ["ps5"], ["qt"])
-        rk = ["rhov"] + ["rho%d" % (2 * b + e) for b in range(12) for e in range(2) if not (e == 1 and b >= 6)]
-        for o in (0, 24):
-            tt(T.kr[:, o:o + 24], T.kc[:, o:o + 24], T.rho[:], A.subtract, kck + rk, ["kr%d" % o])
-        for o in (0, 24):
-            tt(T.z4[:, o:o + 24], T.qt[:, 0:C:16], T.kr[:, o:o + 24], A.add, ["qt", "qtz", "kr%d" % o], ["z4%d" % o])
-        op("v", lambda: V.reciprocal(T.yc[:], T.z4[:]), ["z40", "z424"], ["yc"])
-        if r == 0:
-            act(T.ctl[:], T.c16[:].indirect(T.pu[:]), F.Copy, ["c16", "pu"], ["ctl"])
-        act(T.k1l[:], T.yc[:, 0:24].indirect(T.cu[:, 24:48]), F.Identity, ["yc", "cu"], ["k1l"], scale=0.125)
-        ts(T.k1h[:], T.yc[:, 24:48].indirect(T.cu[:, 24:48]), -0.125, None, A.mult, None, ["yc", "cu"], ["k1h"])
 
         def plane(t):
             act(T.xp[:, W * t:W * t + C], X[:, t:4 * C:4], F.Copy, xk, ["xp%d" % t])
 
-        lo, hi = cut("l"), cut("h")
-        for t in range(3):
-            plane(t)
-        for n in ("y", "f", "pf"):
-            hi[n]()
-            lo[n]()
-        for n in ("sg", "x2", "mx", "mn", "ty", "eq", "s1", "m1", "x1", "cn"):
-            lo[n]()
-            hi[n]()
-            if n == "x2":
-                plane(3)
-                act(T.ew[:, 0:C], T.zero[:], F.Identity, ["zero"], ["ew"], bias=256.0)
-        CLi, CLe, CHe = T.cnl[:, 16:C + 16], T.cnl[:, 15:C + 15], T.cnh[:, 15:C + 15]
+        plane(0)
+        plane(1)
+        ts(T.kr[:, 12:18], T.rho[:, 12:18], -UNIT, (C + H) * UNIT, A.mult, A.add, ["rho%d" % i for i in range(12, 18)], ["kr1"])
+        ts(T.kr[:, 18:24], T.sj[:, H - 1:6 * H:H], -UNIT, C * UNIT, A.mult, A.add, ["sj%d" % b for b in range(6, 12)], ["kr2"])
+        flip(T.qt[:, 0:320], T.ps5[:, 0:320], ["ps5"], ["qt"])
+        ts(T.kr[:, 0:12], T.rho[:, 0:12], -UNIT, C * UNIT, A.mult, A.add, ["rho%d" % i for i in range(12)], ["kr0"])
+        tt(T.kk[:, 12:24], T.qt[:, 16:C:32], T.kr[:, 12:24], A.add, ["qt", "qtz", "kr1", "kr2"], ["kk1"])
+        tt(T.kk[:, 0:12], T.qt[:, 0:C:32], T.kr[:, 0:12], A.add, ["qt", "qtz", "kr0"], ["kk0"])
+        kkk = ["kk0", "kk1"]
+        for i, n in ((0, 2 * (C - K) + 0.5), (1, 2 * K + 0.5)):
+            ts(T.fa[:, 24 * i:24 * i + 24], T.kk[:], n * UNIT, None, A.is_gt, None, kkk, ["fa%d" % i])
+        for i in range(2):
+            tt(T.aa[:, 24 * i:24 * i + 24], T.kk[:], T.fa[:, 24 * i:24 * i + 24], A.subtract, kkk + ["fa%d" % i], ["aa%d" % i])
+        scan(T.st[:, 96:144], T.k12[:, 96:144], T.fa[:], 0.0, A.mult, A.add, ["k12b", "fa0", "fa1"], ["st2"])
+        scan(T.st[:, 0:48], T.k12[:, 0:48], T.aa[:], 0.0, A.add, A.max, ["k12a", "aa0", "aa1"], ["st0"])
+        scan(T.st[:, 48:96], T.k12[:, 48:96], T.aa[:], 0.0, A.add, A.min, ["k12a", "aa0", "aa1"], ["st1"])
+        act(T.sw[:], T.st[:].indirect(T.cu[:, 48:60]), F.Copy, ["st0", "st1", "st2", "cu"], ["sw"])
+        cp(T.k1[:], T.kk[:].indirect(T.cu[:, 24:48]), kkk + ["cu"], ["k1"])
+        plane(2)
+        plane(3)
+        if r == 0:
+            act(T.half[:, 1:2], T.half[:, 0:1], F.Identity, ["hf0"], ["hf1"], scale=-256.0)
+            act(T.ctl[:], T.c16[:].indirect(T.pu[:]), F.Copy, ["c16", "pu"], ["ctl"])
+        act(T.ew[:, 256:256 + C], T.zero[:], F.Identity, ["zero", "hf1"], ["ew"], bias=T.half[:, 1:2])
+        flip(T.su[:], T.sw[:], ["sw"], ["su"])
+        flip(T.ky[:], T.k1[:], ["k1"], ["ky"])
+        scan(T.sx[:, 128:192], T.k32[:, 128:192], T.su[:, 128:192], 0.0, A.mult, A.add, ["k32b", "su"], ["sx2"])
+        scan(T.sx[:, 64:128], T.k32[:, 64:128], T.su[:, 64:128], 0.0, A.add, A.min, ["k32a", "su"], ["sx1"])
+        scan(T.sx[:, 0:64], T.k32[:, 0:64], T.su[:, 0:64], 0.0, A.add, A.max, ["k32a", "su"], ["sx0"])
+        for i, n in ((0, K - 0.5), (1, C - K + 0.5)):
+            ts(T.ty[:, i:i + 1], T.sx[:, 159 + 32 * i:160 + 32 * i], n, T.sx[:, 95 + 32 * i:96 + 32 * i], A.is_gt, A.add, ["sx1", "sx2"], ["tz%d" % i])
+        for i in range(2):
+            ts(T.ty[:, 2 + i:3 + i], T.ty[:, i:i + 1], T.sx[:, 31 + 32 * i:32 + 32 * i], None, A.max, None, ["tz%d" % i, "sx0"], ["ty%d" % i])
 
-        for k in range(3):
+        tl, th = T.ty[:, 2:3], T.ty[:, 3:4]
+        CLi, CLe, CHi, CHe = T.cnl[:, 16:C + 16], T.cnl[:, 15:C + 15], T.cnh[:, 16:C + 16], T.cnh[:, 15:C + 15]
+        ts(T.gl_[:, 0:C], T.ky[:], tl, None, A.is_ge, None, ["ky", "ty0"], ["gl_"])
+        ts(T.al[:], T.ky[:], tl, None, A.is_gt, None, ["ky", "ty0"], ["al"])
+        scan(T.capl[:, ::-1], T.zero[:], T.gl_[:, C:0:-1], 0.0, A.add, A.subtract, ["zero", "gl_", "glz"], ["capl"])
+        ts(T.ah[:, 0:C], T.ky[:], th, None, A.is_lt, None, ["ky", "ty1"], ["ah"])
+        scan(CLi, T.al[:], T.capl[:], -float(K), A.add, A.max, ["al", "capl"], ["cnl"])
+        scan(T.caph[:, ::-1], T.zero[:], T.ah[:, C:0:-1], 256.0, A.add, A.subtract, ["zero", "ah", "ahz"], ["caph"])
+        ts(T.gh[:], T.ky[:], th, None, A.is_le, None, ["ky", "ty1"], ["gh"])
+
+        for k in range(4):
             act(T.sgl[:, C * k:C * k + C], CLi, F.Sign, ["cnl", "ip"], ["sgl%d" % k, "dl%d" % k], bias=T.ip[:, k:k + 1], scale=-1.0, accum_out=T.dl[:, k:k + 1])
         if r == 0:
             cp(T.ctlc[:], T.ctl[:], ["ctl"], ["ctlc"])
-        wrap(T.cva, CLi, T.ctl, ["cnl", "ctl"], "cva")
+        wrap(T.cva, CLi, T.ctl, 128.0 - K, ["cnl", "ctl"], "cva")
+        scan(CHi, T.gh[:], T.caph[:], 256.0 - K, A.add, A.min, ["gh", "caph"], ["cnh"])
         if r == 0:
             tt(T.ctlc[:, 15:C:16], T.ctl[:, 15:C:16], T.il[:], A.add, ["ctl", "il"], ["ctlc"])
-        wrap(T.cvb, CLe, T.ctl, ["cnl", "ctl"], "cvb")
-        ts(T.sgl[:, 3 * C:4 * C], CLi, T.ip[:, 3:4], 2.0, A.is_lt, A.mult, ["cnl", "ip"], ["sgl3"])
+            ts(T.half[:, 2:3], T.half[:, 0:1], 256.0, None, A.mult, None, ["hf0"], ["hf2"])
+            ts(T.half[:, 3:4], T.half[:, 0:1], 512.0, -512.0, A.mult, A.add, ["hf0"], ["hf3"])
+        wrap(T.cvb, CLe, T.ctl, 128.0 - K, ["cnl", "ctl"], "cvb")
+        if r == 0:
+            ts(T.crow[:], T.ramp[:], T.half[:, 2:3], None, A.max, None, ["ramp", "hf2"], ["crow"])
+        wrap(T.cvc, CHe, T.ctlc, 384.0 - K, ["cnh", "ctlc"], "cvc")
         tt(T.t1[:], T.cva[:, 15:C:16], T.cvb[:, 15:C:16], A.subtract, ["cva", "cvb"], ["t1"])
-        wrap(T.cvc, CHe, T.ctlc, ["cnh", "ctlc"], "cvc")
-        ts(T.lm[:], T.t1[:], -768.0, T.cc[:, 0:1], A.mult, A.add, ["t1", "cc0"], ["lm"])
-        scan(T.mxl[:], T.sgl[:, 3 * C:3 * C + H], T.sgl[:, 3 * C + H:4 * C], -float(C), A.add, A.add, ["sgl3"], ["mxl"])
+        scan(T.dat[:], CHe, T.crow[:], -256.0, A.max, A.min, ["cnh", "crow"], ["dat"])
+        ts(T.lm[:], T.t1[:], -640.0, T.cc[:, 0:1], A.mult, A.add, ["t1", "cc0"], ["lm"])
+        if r == 0:
+            ts(T.ctf[:], T.zero[:], T.half[:, 3:4], None, A.add, None, ["zero", "hf3"], ["ctf"])
         tt(T.wm[:], T.cvb[:, 15:C:16], T.lm[:], A.min, ["cvb", "lm"], ["wm"])
-        ts(T.lo[:, 3:4], T.mxl[:, H - 1:H], 0.5, 192.0, A.mult, A.add, ["mxl"], ["lo1"])
-        ts(T.lo[:, 0:3], T.dl[:, 0:3], 0.5, 192.0, A.mult, A.add, ["dl%d" % k for k in range(3)], ["lo"])
+        ts(T.lo[:], T.dl[:], 0.5, 192.0, A.mult, A.add, ["dl%d" % k for k in range(4)], ["lo"])
         tt(T.oo[:], T.cvc[:, 15:C:16], T.wm[:], A.subtract, ["cvc", "wm"], ["oo"])
         for t in range(4):
-            move("vsvs"[t], T.bt[:, t:4 * K:4], T.xp[:, W * t:W * t + C].indirect(T.lo[:]), ["xp%d" % t, "lo", "lo1"], ["bt%d" % t])
+            move("vsvs"[t], T.bt[:, t:4 * K:4], T.xp[:, W * t:W * t + C].indirect(T.lo[:]), ["xp%d" % t, "lo"], ["bt%d" % t])
         cp(T.ou[:], T.oo[:], ["oo"], ["ou"])
         quant(T.qbc[:, 128 * r:128 * r + 128], T.qbs[:, 128 * r:128 * r + 128], T.bt[:], btk + ["btz"], ["qb%d" % r])
         l0 = (0, 192, 256)[r]
@@ -386,42 +397,32 @@ def rank_program(g, core, T, topo):
         send(T.lands[:, l0:l0 + K], T.qbs[:, 128 * r:128 * r + K], "arr%d" % r, ["qb%d" % r])
         lastw["land%d" % r] = ("arr%d" % r, 2 * neng)
 
-        if r == 0:
-            act(T.msk[:], T.m16[:].indirect(T.pu[:]), F.Identity, ["m16", "pu"], ["msk"], bias=-256.0)
         if last:
-            act(T.lsend[:], T.ramp[:].indirect(T.lo[:]), F.Copy, ["ramp", "lo", "lo1"], ["lsend"])
+            act(T.lsend[:], T.ramp[:].indirect(T.lo[:]), F.Copy, ["ramp", "lo"], ["lsend"])
             send(T.lland[:], T.lsend[:], "arrl", ["lsend"])
             lastw["lland"] = ("arrl", neng)
-        cp(T.ew[:].indirect(T.ou[:]), T.ramp[:], ["ou", "ramp"], ["ew"])
+        cp(T.ew[:].indirect(T.ou[:]), T.dat[:], ["ou", "dat"], ["ew"])
 
         def unit(b):
             if r == 0:
                 quant(T.ec[:, 128 * b:128 * b + 128], T.es[:, 128 * b:128 * b + 128], T.gt[:, 3 - b:515 - b], ["gt"], ["e%d" % b])
 
-        def invert(n, h):
-            a, b = (0, U) if h == 0 else (U, C)
-            if n == "hf":
-                ts(T.hf[:, a:b], T.ew[:, a:b], 192.0, None, A.is_ge, None, ["ew"], ["hf%d" % h])
-            elif n == "hn":
-                scan(T.hn[:, a:b], T.hf[:, a:b], T.zero[:, a:b], T.hn[:, U - 1:U] if h else 191.0, A.add, A.add, ["hf%d" % h, "zero"] + ["hn0"] * h, ["hn%d" % h])
-            elif n == "en":
-                scan(T.en[:, a:b], T.hn[:, a:b], T.ew[:, a:b], 0.0, A.max, A.min, ["hn%d" % h, "ew"], ["en%d" % h])
-            elif n == "em":
-                tt(T.em[:, a:b], T.en[:, a:b], T.msk[:, a:b], A.max, ["en%d" % h, "msk"], ["em%d" % h])
-            elif n == "ex":
-                scan(T.ex[:, a:b], T.ctl2[:, a:b], T.em[:, a:b], 0.0, A.max, A.min, ["em%d" % h, "ctl2"], ["ex%d" % h])
-            else:
-                ts(T.eo[:, a // 16:b // 16], T.ex[:, a + 15:b:16], 192.0, None, A.add, None, ["ex%d" % h], ["eo%d" % h])
-
         unit(0)
+        scan(T.en[:, 16:C + 16], T.ctf[:], T.ew[:, 256:256 + C], -256.0, A.add, A.max, ["ctf", "ew"], ["en"])
         unit(1)
-        invert("hf", 0)
-        invert("hf", 1)
-        invert("hn", 0)
+        if r == 0:
+            flip(T.gq[:], T.gr[:], ["gr0", "gr1"], ["gq"])
+        flip(T.et[:, 0:C], T.en[:, 16:C + 16], ["en"], ["et0"])
+        if r == 0:
+            tt(T.gs[:], T.gq[:, 0:4], T.gk[:], A.add, ["gq", "gk"], ["gs"])
+        flip(T.et[:, C:2 * C + 32], T.en[:], ["en", "enz0", "enz1"], ["et1"])
+        if r == 0:
+            ts(T.gl[:], T.gs[:], 2.0 * C + 31, None, A.min, None, ["gs"], ["gl"])
         unit(2)
-        for n, h in (("en", 0), ("hn", 1), ("em", 0), ("en", 1), ("ex", 0), ("em", 1), ("eo", 0), ("ex", 1)):
-            invert(n, h)
+        cp(T.eg[:], T.et[:].indirect(T.gl[:]), ["et0", "et1", "gl"], ["eg"])
         unit(3)
+        tt(T.em[:], T.eg[:, 0:24], T.eg[:, 32:56], A.min, ["eg"], ["em"])
+        ts(T.eo[:], T.em[:], 192.0, None, A.add, None, ["em"], ["eo"])
 
         v0 = (0, 128, 192)[r]
         lk = ["land%d" % r, "landz"] + (["land1"] if r == 2 else [])
@@ -432,7 +433,7 @@ def rank_program(g, core, T, topo):
         def gather(e, h, t):
             n = 13 - h
             move(e, (T.ta, T.tb)[h][:, t:64 * n:4], T.xp[:, W * t:W * t + W].indirect(T.eo[:, 12 * h:12 * h + n]),
-                 ["xp%d" % t, "xa%d" % t, "eo0"] + ["eo1"] * h, ["t%d_%d" % (h, t)])
+                 ["xp%d" % t, "xa%d" % t, "eo"], ["t%d_%d" % (h, t)])
 
         def qt(h, rot):
             i = 2 * h + rot
@@ -453,9 +454,7 @@ def rank_program(g, core, T, topo):
                 act(out, T[ps][:, 0:H], F.Copy, [ps], [key], scale=0.015625)
 
         for t in range(4):
-            gather("svsv"[t], 0, t)
-            if t == 1:
-                invert("eo", 1)
+            gather("vsvs"[t], 0, t)
         qt(0, 0)
         qt(0, 1)
         layer(0)
@@ -484,7 +483,7 @@ def rank_program(g, core, T, topo):
             for b in range(4):
                 evac("ssvv"[b], 1, b)
             act(T.ow[:, C:W], T.lland[:], F.Identity, ["lland"], ["ow1"], bias=576.0)
-            act(T.olb[:], T.ow[:].indirect(T.eo[:]), F.Copy, ["ow0", "ow1", "eo0", "eo1"], ["olb"])
+            act(T.olb[:], T.ow[:].indirect(T.eo[:]), F.Copy, ["ow0", "ow1", "eo"], ["olb"])
             qx(r + 1, 1)
             mm(1, H, T.qvc[:], T.qvs[:], T.qxc[:, H:C], T.qxs[:, H:C], True, True, ["qv", "qx1"])
             dma("s", T.ol[:], T.olb[0:128:16, :], ["olb"], [])

@@ -6,6 +6,21 @@ H = C // 2
 W = C + K
 UNIT = 2.0 ** -10
 Q4, U8, BF, F32, I32, U16, F16 = "float8_e4m3fn_x4", "uint8", "bfloat16", "float32", "int32", "uint16", "float16"
+CYC, PICK, PUT, COL, LOAD, SEND, VFIX, SFIX = 0.83, 1.56, 3.8, 0.55, 1200, 2500, 50, 65
+VB = 4
+NV = 1
+ORDER = """cgka +cx0_0a ccua ps1a crampa cila:s +cgr0a tr5_1a cgwza ps2a tr4_1a sj5a +cci0a chf3a:s ps3a sg4a +ccnla pt1a +coneka sj4a
+xp0a:q +ccst0a tr11_1a ccst0b:s tr8_1a tr7_1a +cx1_0a sj8a tr10_1a ccsa +czpa ps4a +cci1a tr6_1a xp2a:q sj7a ps2b sg7a +cgr1a sg5a sg6a
+tr9_0a tr10_0a tr9_1a tr4_0a tr11_0a qf5a qf4a cim2a tr8_0a tr7_0a +czeroa tr6_0a xp1a:q qf3a tr5_0a cvta cbtza qf2a sj10a +ck120a sg1a
+sg0a cipa:s +cwpa ps5a ps5b fa1a sj6a +cuta ck321a +ciaa +ccs0a sg2a sj9a sg3a kr0a:s sj11a +cpia kr1a:s kr2a:s ps5c xp3a:q nb0a chf1a:s
+chf2a:s kk0a ps5d qta kk1a k10a:s fa0a k11a:s nb1a aa1a aa0a st1a st0a swa:s ky0a ccrowa ky1a cahza cc16a cpua +clandza tz0a tz1a cctla:s
+cprea:s ty0a ty1a +cci3a sua sx0a sx1a gwa ccc0a:s ala capla aha cnla sgl2a sgl1a capha sgl3a cctlca cvba cvaa gha sgl0a sm3a t1a cnha
+lo1a lma:s ccila:s +ccu0a loa bt1a:s bt2a:s wma cgsa bt0a:v ooa data cvca qba bt3a:s oua cgta ce1a ewb cgla lsenda:v cctfa:s ce0a ena
+ce3a et0a et1a lca em0a lsa ps7a ce2a em1a xa3a:v ps4b ps5e +ccs1a xa0a:s +conesa +cqua +cpusa +cqx0a eoa +cci2a xa1a:s +ccst2a:s ps6a
+llanda cow0a +cenz0a cqva +ccnha +cenz1a t0_3a:s +cpuca t0_1a:s t1_3a:s xa2a:v t1_2a:s +cima t0_0a:v czqa ps3b t0_2a:v qt0a ps2c +cqtza
+tbwa:v qt1a ps2d +cpja ps3c t1_1a:s ps0c ow1a:v olba:s olbb +cqx1a +ccst3a:s ps1b +ewa:q ps4d x0_3a:s +ck320a ps1c x0_1a:s ps0b x0_0a:s
++cgqa +ck121a +cqfa +chf0a qx0c t1_0a:v qt2a ps5f qt3a ps6b x1_0a:s ps4c ps7b ps5g x1_1a:s +ccst1a:s ps7c qx1c qx0a x0_2a:v x1_2a:s ps6c
++pt0a qx0d cwqa x1_3a:v +ps0a qx1a qx0e qx0g ps0e y0a:s y0b ps1e y1a:v qx0f y1b"""
 
 
 def _sb(n, d):
@@ -19,27 +34,27 @@ SCRATCH = {
     "wq": _sb(512, Q4), "wp": _sb(512, U8), "zq": _sb(512, Q4), "zp": _sb(512, U8),
     "gt": _sb(516, BF), "ones": _sb(516, BF), "onek": _sb(128, BF), "ec": _sb(512, Q4), "es": _sb(512, U8),
     "ci": _sb(60, I32), "cu": _sb(60, U16), "pi": _sb(24, I32), "pj": _sb(24, I32), "pu": _sb(24, U16), "qf": _sb(2, F32),
-    "ia": _sb(24, F32), "il": _sb(24, F32), "ip": _sb(4, F32), "cc": _sb(2, F32),
+    "ia": _sb(24, F32), "il": _sb(24, F32), "ip": _sb(6, F32),
     "im": _sb(16, I32), "im2": _sb(16, I32), "c16": _sb(16, F32),
-    "ctl": _sb(C, BF), "ctlc": _sb(C, F16), "ctf": _sb(C, BF), "crow": _sb(C, BF), "half": _sb(4, F32),
-    "gr": _sb(32, F32), "gq": _sb(32, F32), "gk": _sb(4, F32), "gs": _sb(4, F32), "gl": _sb(4, U16),
-    "k12": _sb(144, F32), "k32": _sb(192, F32),
-    "zero": _sb(C, BF), "zt": _sb(512, BF), "ramp": _sb(C, BF), "ow": _sb(W, F32),
+    "ctl": _sb(C, BF), "ctlc": _sb(C, F16), "ctf": _sb(C, BF), "crow": _sb(C, BF), "pre": _sb(C, BF), "half": _sb(4, F32),
+    "gr": _sb(72, F32), "gl": _sb(2, U16),
+    "k12": _sb(96, F32), "k32": _sb(128, F32), "cil": _sb(24, F32),
+    "zero": _sb(512, BF), "ramp": _sb(C, BF), "ow": _sb(W, F32),
     "qxc": _sb(C, Q4), "qxs": _sb(C, U8), "pt": _sb(C, F32),
     "tri2": _sb(4 * 192, BF), "tri3": _sb(4 * 256, BF), "tri4": _sb(4 * 320, BF), "tri5": _sb(4 * 384, BF),
-    "sj": _sb(6 * H, BF), "sg": _sb(8 * 128, BF), "rho": _sb(24, F32),
-    "qfc": _sb(896, Q4), "qfs": _sb(896, U8), "cs0": _sb(128, BF), "cst": _sb(512, BF), "csc": _sb(128, Q4), "css": _sb(128, U8),
+    "sj": _sb((12 - VB) * H, BF), "sg": _sb(8 * 128, BF), "rho": _sb(24, F32),
+    "qfc": _sb(896, Q4), "qfs": _sb(896, U8), "cs0": _sb(128, BF), "cs1": _sb(128, BF), "cst": _sb(512, BF), "csc": _sb(128, Q4), "css": _sb(128, U8),
     "qt": _sb(C, F32), "kr": _sb(24, F32), "kk": _sb(24, F32), "fa": _sb(48, F32), "aa": _sb(48, F32),
-    "st": _sb(144, F32), "sw": _sb(192, F32), "su": _sb(192, F32), "sx": _sb(192, F32), "ty": _sb(4, F32),
-    "k1": _sb(C, F16), "ky": _sb(C, F16),
-    "gl_": _sb(C + 16, BF), "al": _sb(C, BF), "ah": _sb(C + 16, BF), "gh": _sb(C, BF), "capl": _sb(C, BF), "caph": _sb(C, BF),
+    "st": _sb(96, F32), "sw": _sb(128, F32), "su": _sb(128, F32), "sx": _sb(128, F32), "tz": _sb(4, F32), "ty": _sb(2, BF),
+    "k1l": _sb(C, BF), "k1h": _sb(C, BF), "kyl": _sb(C, BF), "kyh": _sb(C, BF),
+    "gw": _sb(C + 16, BF), "al": _sb(C, BF), "ah": _sb(C + 16, BF), "gh": _sb(C, BF), "capl": _sb(C, BF), "caph": _sb(C, BF),
     "cnl": _sb(C + 16, BF), "cnh": _sb(C + 16, BF),
-    "dl": _sb(4, F32), "sgl": _sb(4 * C, BF), "lo": _sb(4, U16), "bt": _sb(512, BF), "xp": _sb(4 * W, BF),
+    "dl": _sb(4, F32), "sgl": _sb(4 * C, BF), "sm": _sb(4 * H, BF), "lo": _sb(4, U16), "bt": _sb(512, BF), "xp": _sb(4 * W, BF),
     "qbc": _sb(R * 128, Q4), "qbs": _sb(R * 128, U8), "landc": _sb(320, Q4), "lands": _sb(320, U8),
     "lsend": _sb(K, BF), "lland": _sb(K, BF),
     "cva": _sb(C, BF), "cvb": _sb(C, BF), "cvc": _sb(C, F16),
-    "t1": _sb(24, F32), "lm": _sb(24, F32), "wm": _sb(24, F32), "oo": _sb(24, F32), "ou": _sb(24, U16),
-    "dat": _sb(C, BF), "ew": _sb(1088, BF), "en": _sb(C + 32, BF), "et": _sb(2 * C + 32, BF), "eg": _sb(64, BF), "em": _sb(24, F32), "eo": _sb(24, U16),
+    "t1": _sb(24, F32), "lm": _sb(24, F32), "wm": _sb(24, F32), "ou": _sb(24, U16),
+    "dat": _sb(C, BF), "ew": _sb(1088, BF), "en": _sb(C + 32, BF), "et": _sb(2 * C + 32, BF), "em": _sb(50, F32), "eo": _sb(32, U16),
     "ta": _sb(4 * 208, BF), "tb": _sb(4 * 196, BF),
     "qtc": _sb(4 * H, Q4), "qts": _sb(4 * H, U8),
     "ysb": _sb(C, F32), "olb": _sb(C, F32),
@@ -57,6 +72,47 @@ def _reach(b):
     return max(128, 64 * (b // 2 + 1))
 
 
+def _preds(plan):
+    pred = [set() for _ in plan]
+    lastw, readers = {}, {}
+    for i, p in enumerate(plan):
+        rd, wr = [k.rstrip("!") for k in p[1]], p[2]
+        for k in rd:
+            if k in lastw:
+                pred[i].add(lastw[k])
+        for k in wr:
+            pred[i].update(readers.get(k, []))
+            if k in lastw:
+                pred[i].add(lastw[k])
+        for k in rd:
+            readers.setdefault(k, []).append(i)
+        for k in wr:
+            lastw[k] = i
+            readers[k] = []
+        pred[i].discard(i)
+    return pred
+
+
+def _layout(plan):
+    words = ORDER.split()
+    at = {w.strip("+").split(":")[0]: (i - len(words) * (w[0] == "+"), w.partition(":")[2]) for i, w in enumerate(words)}
+    pred = _preds(plan)
+    succ, left = [[] for _ in plan], [len(p) for p in pred]
+    for i, p in enumerate(pred):
+        for j in p:
+            succ[j].append(i)
+    ready, out = [i for i in range(len(plan)) if not left[i]], []
+    while ready:
+        i = min(ready, key=lambda j: (plan[j][6] * len(words) + at[plan[j][5]][0], j))
+        ready.remove(i)
+        out.append(([a for a in plan[i][0] if a[0] == (at[plan[i][5]][1] or a[0])][0], plan[i]))
+        for j in succ[i]:
+            left[j] -= 1
+            if not left[j]:
+                ready.append(j)
+    return out
+
+
 def rank_program(g, core, T, topo):
     rank = T.rank_of(core)
     if rank is None:
@@ -65,8 +121,350 @@ def rank_program(g, core, T, topo):
     rid, pid = topo.addr(nxt)[0], topo.addr(nxt)[1]
     mask = topo.mask(core, nxt)
     neng = len(topo.engines(core, nxt))
+    V, S, P = g.vector, g.scalar, g.tensor
+    queue = {"v": V, "s": S, "p": P, "q": g, "y": g.sync}
+    plan, seen, now = [], {}, [0]
 
-    queue = {"v": g.vector, "s": g.scalar, "p": g.tensor, "q": g, "y": g.sync}
+    def add(alts, rd, wr, lat=0, kind=None):
+        name = (wr + rd)[0]
+        if name[0] == "x" and "_" in name:
+            name = "x" + name[3:]
+        elif name[:2] in ("qb", "lc", "ls") and len(name) == 3:
+            name = name[:2]
+        seen[name] = seen.get(name, 0) + 1
+        plan.append((alts, rd, wr, lat, kind, ("" if "on" in seen else "c") + name + "abcdefgh"[seen[name] - 1], now[0]))
+
+    def vec(make, n):
+        return ("v", make, VFIX + CYC * n)
+
+    def sca(make, n):
+        return ("s", make, SFIX + CYC * n)
+
+    def pool(make, n):
+        return ("q", make, 170 + 2 * CYC * n)
+
+    def ts(out, in0, s1, s2, o0, o1, rd, wr, n):
+        if o1 is None:
+            add([vec(lambda: V.tensor_scalar(out, in0, s1, None, o0), n)], rd, wr)
+        else:
+            add([vec(lambda: V.tensor_scalar(out, in0, s1, s2, o0, o1), n)], rd, wr)
+
+    def tt(out, a, b, o, rd, wr, n):
+        add([vec(lambda: V.tensor_tensor(out, a, b, o), 2 * n)], rd, wr)
+
+    def cp(out, in_, rd, wr, n):
+        add([vec(lambda: V.tensor_copy(out, in_), n)], rd, wr)
+
+    def scan(out, d0, d1, init, o0, o1, rd, wr, n):
+        add([vec(lambda: V.tensor_tensor_scan(out, d0, d1, init, o0, o1), n)], rd, wr)
+
+    def flip(out, in_, rd, wr, n):
+        add([vec(lambda: V.transpose(out, in_), n)], rd, wr)
+
+    def quant(oc, osc, in_, rd, wr, n):
+        add([("v", lambda: V.quantize_mx(oc, osc, in_), 12 + 1.06 * CYC * n)], rd, wr)
+
+    def act(out, in_, func, rd, wr, n, **kw):
+        add([sca(lambda: S.activation(out, in_, func, **kw), n + (24 if "accum_out" in kw else 0))], rd, wr)
+
+    def move(out, in_, rd, wr, n, nv=None, on="sv"):
+        alts = {"s": sca(lambda: S.activation(out, in_, F.Copy), n), "v": vec(lambda: V.tensor_copy(out, in_), nv or n),
+                "q": pool(lambda: g.affine_select(out, in_, [[0, n]], A.is_ge, 0.0, 0, 0), n)}
+        add([alts[e] for e in on], rd, wr)
+
+    def line(out, in_, scale, bias, rd, wr, n, nv=None, on="sv"):
+        if isinstance(bias, float) and bias == 0.0:
+            alts = {"s": sca(lambda: S.activation(out, in_, F.Copy, scale=scale), n), "v": vec(lambda: V.tensor_scalar(out, in_, scale, None, A.mult), nv or n)}
+        else:
+            alts = {"s": sca(lambda: S.activation(out, in_, F.Identity, bias=bias, scale=scale), n),
+                    "v": vec(lambda: V.tensor_scalar(out, in_, scale, bias, A.mult, A.add), nv or n)}
+        add([alts[e] for e in on], rd, wr)
+
+    def mm(bank, n, lc, ls, rc, rs, start, stop, rd):
+        add([("p", lambda: P.matmul_mx(T["ps%d" % bank][:, 0:n], lc, ls, rc, rs, start, stop), 20 + COL * (n + 16))], rd, ["ps%d" % bank], 0, None if start else "chain")
+
+    def iota(out, pat, base, cm, wr, fl=True):
+        n = 1
+        for p in pat:
+            n *= p[1]
+        if fl:
+            add([pool(lambda: g.iota(out, pat, base, cm, allow_small_or_imprecise_dtypes=True), n)], [], wr)
+        else:
+            add([pool(lambda: g.iota(out, pat, base, cm), n)], [], wr)
+
+    def keep(out, in_, pat, base, cm, o, rd, wr, n, other=0.0):
+        add([pool(lambda: g.affine_select(out, in_, pat, o, other, base, cm), n)], rd, wr)
+
+    def fill(ap, c, wr, n):
+        add([vec(lambda: V.memset(ap, c), n)], [], wr)
+
+    def dma(e, out, in_, rd, wr, lat, d=60):
+        add([(e, lambda: queue[e].dma_start(out, in_), d)], rd, wr, lat, "dma")
+
+    def send(out, in_, sem, total, rd, wr):
+        add([("q", lambda: g.remote_dma(out, in_, T.sem[sem], T.sem.sent, pid, rid, mask), 100)], rd, wr, SEND, (sem, total))
+
+    def xkeys(r, halves=(0, 1)):
+        return ["x%d_%d_%d" % (r, h, b) for h in halves for b in range(4)]
+
+    def qx(r, h):
+        quant(T.qxc[:, H * h:H * h + H], T.qxs[:, H * h:H * h + H], T["xw%d" % r][:, 4 * H * h:4 * H * (h + 1)], xkeys(r, (h,)), ["qx%d" % h], H)
+
+    dma("s", T.ut[:], T.u[:], [], ["ut"], LOAD + 350)
+    dma("y", T.xw0[:, 0:4 * H], T.x[:, 0:4 * H], [], xkeys(0, (0,)), LOAD, 500)
+    dma("y", T.xw0[:, 4 * H:4 * C], T.x[:, 4 * H:4 * C], [], xkeys(0, (1,)), LOAD, 500)
+    dma("y", T.wq[:].bitcast(dt.uint8), T.wc[:], [], ["wq"], LOAD, 650)
+    dma("y", T.zq[:].bitcast(dt.uint8), T.zc[:], [], ["zq"], LOAD, 650)
+    dma("y", T.wp[:], T.ws[:], [], ["wp"], LOAD, 200)
+    dma("y", T.zp[:], T.zs[:], [], ["zp"], LOAD, 200)
+    dma("y", T.vt[:], T.v[:], [], ["vt"], LOAD, 350)
+
+    btk = ["bt0", "bt1", "bt2", "bt3"]
+    iota(T.ci[:, 0:8], [[16, 8]], 0, 0, ["ci0"], False)
+    iota(T.ci[:, 8:24], [[16, 2], [32, 4], [0, 2]], 0, 0, ["ci1"], False)
+    iota(T.ci[:, 24:48], [[1, 12], [12, 2]], 0, 0, ["ci2"], False)
+    iota(T.ci[:, 48:60], [[12, 12]], 11, 0, ["ci3"], False)
+    cp(T.cu[:, 0:24], T.ci[:, 0:24], ["ci0", "ci1"], ["cu0"], 24)
+    cp(T.cu[:, 24:60], T.ci[:, 24:60], ["ci2", "ci3"], ["cu"], 36)
+    iota(T.pi[:], [[0, 24]], 0, 1, ["pi"], False)
+    iota(T.im[:], [[1, 16]], 0, -1, ["im"], False)
+    iota(T.ia[:], [[16, 24]], 0, 0, ["ia"])
+    fill(T.onek[:], UNIT, ["onek"], 64)
+    fill(T.zero[:], 0.0, ["zero"], 256)
+    cstk = ["cst%d" % a for a in range(4)]
+    fill(T.cst[:], 0.0, cstk, 256)
+    fill(T.ones[:], 1.0, ["ones"], 258)
+    keep(T.cs0[:], T.onek[:], [[-2, 2], [0, 16], [1, 4]], 0, 0, A.is_ge, ["onek"], ["cs0"], 128)
+    keep(T.cs1[:], T.cs0[:], [[2, 2], [0, 16], [-1, 4]], 1, 0, A.is_ge, ["cs0"], ["cs1"], 128)
+    for a in range(4):
+        move(T.cst[32 * a:32 * a + 32, 128 * a:128 * a + 128], T.cs1[32 * a:32 * a + 32, :], ["cs1"], [cstk[a]], 128, 64)
+    quant(T.csc[:], T.css[:], T.cst[:], cstk, ["cs"], 128)
+    iota(T.qt[:, 320:C], [[0, C - 320]], 0, 0, ["qtz"])
+    iota(T.cnl[:, 0:16], [[0, 16]], -K, 0, ["cnl"])
+    iota(T.cnh[:, 0:16], [[0, 16]], 256 - K, 0, ["cnh"])
+    iota(T.gw[:, C:C + 16], [[0, 16]], 0, 0, ["gwz"])
+    iota(T.ah[:, C:C + 16], [[0, 16]], 0, 0, ["ahz"])
+    iota(T.bt[:, 4 * K:512], [[0, 512 - 4 * K]], 0, 0, ["btz"])
+    iota(T.ramp[:], [[1, C]], -192, 0, ["ramp"])
+    iota(T.gr[:, 0:16], [[2, 8], [26, 2]], 0, 0, ["gr0"])
+    iota(T.gr[:, 16:32], [[2, 8], [-24, 2]], 25, 0, ["gr1"])
+    iota(T.gr[:, 64:66], [[16, 2]], 0, 0, ["gk"])
+    flip(T.gr[:, 32:64], T.gr[:, 0:32], ["gr0", "gr1"], ["gq"], 32)
+    tt(T.gr[:, 68:70], T.gr[:, 32:34], T.gr[:, 64:66], A.add, ["gq", "gk"], ["gs"], 4)
+    ts(T.gl[:], T.gr[:, 68:70], 49.0, None, A.min, None, ["gs"], ["gl"], 4)
+    iota(T.en[:, 0:16], [[0, 16]], 0, 0, ["enz0"])
+    iota(T.en[:, C + 16:C + 32], [[0, 16]], 0, 0, ["enz1"])
+    keep(T.gt[:], T.ones[:], [[1, 516]], -3, -4, A.is_equal, ["ones"], ["gt"], 516)
+    for b in range(4):
+        quant(T.ec[:, 128 * b:128 * b + 128], T.es[:, 128 * b:128 * b + 128], T.gt[:, 3 - b:515 - b], ["gt"], ["e%d" % b], 128)
+    iota(T.ow[:, 0:C], [[1, C]], 0, 0, ["ow0"])
+    for i in range(2):
+        keep(T.k12[:, 48 * i:48 * i + 48], T.zero[:, 0:48], [[0, 4], [1, 12]], 0, 0, A.is_gt, ["zero"], ["k12%d" % i], 48, 8.0 * i - 4.0)
+        keep(T.k32[:, 64 * i:64 * i + 64], T.zero[:, 0:64], [[0, 2], [1, 32]], 0, 0, A.is_gt, ["zero"], ["k32%d" % i], 64, 8.0 * i - 4.0)
+    ts(T.pj[:], T.pi[:], 15, None, A.bitwise_and, None, ["pi"], ["pj"], 24)
+    quant(T.landc[:, 64:192], T.lands[:, 64:192], T.zero[:], ["zero"], ["landz"], 128)
+    ts(T.im2[:], T.im[:], 15, None, A.bitwise_and, None, ["im"], ["im2"], 16)
+    cp(T.qf[:], T.pj[:, 0:2], ["pj"], ["qf"], 2)
+    cp(T.pu[:], T.pj[:], ["pj"], ["pu"], 24)
+    ts(T.c16[:], T.im2[:], 15.0, 128.0, A.is_equal, A.mult, ["im2"], ["c16"], 16)
+    line(T.il[:], T.ia[:], 1.0, T.qf[:, 0:1], ["ia", "qf"], ["il"], 24)
+    quant(T.quc[:], T.qus[:], T.ut[:], ["ut"], ["qu"], 128)
+    quant(T.qvc[:], T.qvs[:], T.vt[:], ["vt"], ["qv"], 128)
+    act(T.pus[:], T.qus[:].indirect(T.cu[:, 0:24]), F.Copy, ["qu", "cu0"], ["pus"], PICK * C)
+    cp(T.puc[:].bitcast(dt.uint32), T.quc[:].bitcast(dt.uint32).indirect(T.cu[:, 0:24]), ["qu", "cu0"], ["puc"], PICK * C)
+    line(T.ip[:, 0:4], T.il[:, 0:4], 1.0, 0.5 - K, ["il"], ["ip"], 4)
+    line(T.ip[:, 4:5], T.c16[:, 15:16], -1.0, float(W), ["c16"], ["cc0"], 1)
+    act(T.half[:, 0:1], T.qf[:, 0:1], F.Sign, ["qf"], ["hf0"], 1, bias=-7.5)
+    line(T.half[:, 1:2], T.half[:, 0:1], -256.0, 0.0, ["hf0"], ["hf1"], 1)
+    line(T.half[:, 2:3], T.half[:, 0:1], 256.0, 0.0, ["hf0"], ["hf2"], 1)
+    line(T.half[:, 3:4], T.half[:, 0:1], 512.0, -512.0, ["hf0"], ["hf3"], 1)
+    move(T.ctl[:], T.c16[:].indirect(T.pu[:]), ["c16", "pu"], ["ctl"], PICK * C)
+    move(T.ctlc[:], T.ctl[:], ["ctl"], ["ctlc"], C, H, "v")
+    line(T.cil[:], T.il[:], 1.0, float(W), ["il"], ["cil"], 24)
+    ts(T.crow[:], T.ramp[:], T.half[:, 2:3], None, A.max, None, ["ramp", "hf2"], ["crow"], H)
+    line(T.ctf[:], T.zero[:, 0:C], 1.0, T.half[:, 3:4], ["zero", "hf3"], ["ctf"], C, H)
+    line(T.pre[:], T.zero[:, 0:C], 1.0, T.half[:, 1:2], ["zero", "hf1"], ["pre"], C, H)
+    Z = T.zero[:, 0:C]
+
+    def score(bank, j, c0, c1, rd):
+        mm(bank, c1 - c0, T.puc[:, 128 * j:128 * j + 128], T.pus[:, 128 * j:128 * j + 128], T.qxc[:, c0:c1], T.qxs[:, c0:c1], True, True, ["puc", "pus"] + rd)
+
+    def turn(bank, h):
+        flip(T.pt[:, H * h:H * h + H], T["ps%d" % bank][:, 0:H], ["ps%d" % bank], ["pt%d" % h], H)
+
+    def wrap(out, src, ctl, init, rd, okey):
+        scan(out[:], src, ctl[:], init, A.min, A.add, rd, [okey], H)
+
+    qx(0, 0)
+    qx(0, 1)
+    for r in range(R):
+        last = r == R - 1
+        seen.clear()
+        seen["on"] = 1
+        now[0] = r
+        X, XN = T["xw%d" % r], T["xw%d" % (r + 1)]
+        xk = xkeys(r)
+        score(0, 0, 0, H, ["qx0"])
+        score(1, 2, 0, _reach(VB - 1), ["qx0"])
+        if VB < 6:
+            score(2, 2, 0, H, ["qx0"])
+        turn(0, 0)
+        score(3, 0, H, C, ["qx1"])
+        score(4, 2, 0, C, ["qx0", "qx1"])
+        turn(3, 1)
+
+        def row(e, b):
+            if b < 4:
+                return T.sg[:, 128 * (4 * e + b):128 * (4 * e + b) + 128], "sg%d" % (4 * e + b)
+            return T["tri%d" % (b // 2)][:, 2 * e + b % 2:4 * _reach(b):4], "tr%d_%d" % (b, e)
+
+        def sgn(e, b):
+            bank = "ps1" if e else "ps2"
+            out, key = row(e, b)
+            act(out, T[bank][:, 0:_reach(b)], F.Sign, [bank, "pt%d" % (b // 6)], [key, "rho%d" % (12 * e + b)], _reach(b),
+                bias=T.pt[:, 32 * b + 16 * e:32 * b + 16 * e + 1], scale=-1.0, accum_out=T.rho[:, 12 * e + b:12 * e + b + 1])
+
+        def cmp(b):
+            out, key = row(1, b)
+            bank = "ps4" if b >= 6 else "ps2"
+            ts(out, T[bank][:, 0:_reach(b)], T.pt[:, 32 * b + 16:32 * b + 17], -2.0, A.is_ge, A.mult, [bank, "pt%d" % (b // 6)], [key], _reach(b))
+
+        def cnt(b):
+            n, t, tri = _reach(b), 2 + b % 2, T["tri%d" % (b // 2)]
+            e = H * (b - VB + 1)
+            scan(T.sj[:, e - n // 2:e], tri[:, t:2 * n:4], tri[:, 2 * n + t:4 * n:4], 2.0 * n - C, A.add, A.add, ["tr%d_1" % b], ["sj%d" % b], n // 4)
+
+        def cols(k):
+            n = 64 * k
+            o = {5: 0, 4: 320, 3: 576, 2: 768}[k]
+            quant(T.qfc[:, o:o + n], T.qfs[:, o:o + n], T["tri%d" % k][:, 0:4 * n], ["tr%d_%d" % (b, e) for b in (2 * k, 2 * k + 1) for e in (0, 1)], ["qf%d" % k], n)
+            mm(5, n, T.csc[:], T.css[:], T.qfc[:, o:o + n], T.qfs[:, o:o + n], k == 5, k == 2, ["cs", "qf%d" % k])
+
+        for b in range(12):
+            if b < VB:
+                sgn(1, b)
+            else:
+                cmp(b)
+                cnt(b)
+            if b == 5:
+                score(2, 1, 0, C, ["qx0", "qx1"])
+        for b in range(12):
+            sgn(0, b)
+        for k in (5, 4, 3, 2):
+            cols(k)
+        for t in range(4):
+            move(T.xp[:, W * t:W * t + C], X[:, t:4 * C:4], xk, ["xp%d" % t], C, H, "qs")
+        move(T.ew[:, 256:256 + C], T.pre[:], ["pre"], ["ew"], C, H, "qs")
+
+        line(T.kr[:, 12:12 + VB], T.rho[:, 12:12 + VB], -UNIT, (2 * C - 32 * VB) * UNIT, ["rho%d" % i for i in range(12, 12 + VB)], ["kr1"], 6)
+        line(T.kr[:, 12 + VB:24], T.sj[:, H - 1:(12 - VB) * H:H], -UNIT, C * UNIT, ["sj%d" % b for b in range(VB, 12)], ["kr2"], 6)
+        line(T.kr[:, 0:12], T.rho[:, 0:12], -UNIT, C * UNIT, ["rho%d" % i for i in range(12)], ["kr0"], 12)
+        flip(T.qt[:, 0:320], T.ps5[:, 0:320], ["ps5"], ["qt"], 320)
+        tt(T.kk[:, 12:24], T.qt[:, 16:C:32], T.kr[:, 12:24], A.add, ["qt", "qtz", "kr1", "kr2"], ["kk1"], 12)
+        tt(T.kk[:, 0:12], T.qt[:, 0:C:32], T.kr[:, 0:12], A.add, ["qt", "qtz", "kr0"], ["kk0"], 12)
+        kkk = ["kk0", "kk1"]
+        cuts = (2 * (C - K), 2 * K)
+        for i in range(2):
+            ts(T.fa[:, 24 * i:24 * i + 24], T.kk[:], (cuts[i] + 0.5) * UNIT, cuts[i] * UNIT, A.is_gt, A.add, kkk, ["fa%d" % i], 24)
+            tt(T.aa[:, 24 * i:24 * i + 24], T.kk[:], T.fa[:, 24 * i:24 * i + 24], A.subtract, kkk + ["fa%d" % i], ["aa%d" % i], 24)
+        for i, o in enumerate((A.max, A.min)):
+            scan(T.st[:, 48 * i:48 * i + 48], T.k12[:, 48 * i:48 * i + 48], T.aa[:], 0.0, A.add, o, ["k12%d" % i, "aa0", "aa1"], ["st%d" % i], 48)
+        move(T.sw[:], T.st[:].indirect(T.cu[:, 48:56]), ["st0", "st1", "cu"], ["sw"], PICK * 128)
+        flip(T.su[:], T.sw[:], ["sw"], ["su"], 128)
+        for i, o in enumerate((A.max, A.min)):
+            scan(T.sx[:, 64 * i:64 * i + 64], T.k32[:, 64 * i:64 * i + 64], T.su[:, 64 * i:64 * i + 64], 0.0, A.add, o, ["k32%d" % i, "su"], ["sx%d" % i], 64)
+        for i, n in ((0, C - 2 * K + 1.0), (1, 2 * K - C - 1.0)):
+            k1, ky = (T.k1l, T.k1h)[i], (T.kyl, T.kyh)[i]
+            line(k1[:], T.kk[:].indirect(T.cu[:, 24:48]), 1.0, -cuts[i] * UNIT, kkk + ["cu"], ["k1%d" % i], PICK * C)
+            flip(ky[:], k1[:], ["k1%d" % i], ["ky%d" % i], H)
+            act(T.sgl[:, C * i:C * i + C], ky[:], F.Sign, ["ky%d" % i], ["nb%d" % i, "sgl%d" % i], C, bias=-0.5 * UNIT, accum_out=T.tz[:, 2 + i:3 + i])
+            act(T.tz[:, i:i + 1], T.tz[:, 2 + i:3 + i], F.Sign, ["nb%d" % i], ["tz%d" % i], 1, bias=n)
+            ts(T.ty[:, i:i + 1], T.sx[:, 95 + 32 * i:96 + 32 * i], T.tz[:, i:i + 1], T.sx[:, 31 + 32 * i:32 + 32 * i], A.add, A.max, ["tz%d" % i, "sx0", "sx1"], ["ty%d" % i], 1)
+
+        tl, th = T.ty[:, 0:1], T.ty[:, 1:2]
+        CLi, CLe, CHi, CHe = T.cnl[:, 16:C + 16], T.cnl[:, 15:C + 15], T.cnh[:, 16:C + 16], T.cnh[:, 15:C + 15]
+        ts(T.gw[:, 0:C], T.kyl[:], tl, None, A.is_ge, None, ["ky0", "ty0"], ["gw"], H)
+        ts(T.al[:], T.kyl[:], tl, None, A.is_gt, None, ["ky0", "ty0"], ["al"], H)
+        scan(T.capl[:, ::-1], Z, T.gw[:, C:0:-1], 0.0, A.add, A.subtract, ["zero", "gw", "gwz"], ["capl"], H)
+        scan(CLi, T.al[:], T.capl[:], -float(K), A.add, A.max, ["al", "capl"], ["cnl"], H)
+        ts(T.ah[:, 0:C], T.kyh[:], th, None, A.is_lt, None, ["ky1", "ty1"], ["ah"], H)
+        ts(T.gh[:], T.kyh[:], th, None, A.is_le, None, ["ky1", "ty1"], ["gh"], H)
+        scan(T.caph[:, ::-1], Z, T.ah[:, C:0:-1], 256.0, A.add, A.subtract, ["zero", "ah", "ahz"], ["caph"], H)
+        scan(CHi, T.gh[:], T.caph[:], 256.0 - K, A.add, A.min, ["gh", "caph"], ["cnh"], H)
+
+        for k in range(4 - NV):
+            act(T.sgl[:, C * k:C * k + C], CLi, F.Sign, ["cnl", "ip"], ["sgl%d" % k, "dl%d" % k], C, bias=T.ip[:, k:k + 1], scale=-1.0, accum_out=T.dl[:, k:k + 1])
+        ts(T.lo[:, 0:4 - NV], T.dl[:, 0:4 - NV], 0.5, 192.0, A.mult, A.add, ["dl%d" % k for k in range(4 - NV)], ["lo"], 4)
+        for k in range(4 - NV, 4):
+            ts(T.sgl[:, C * k:C * k + C], CLi, T.ip[:, k:k + 1], None, A.is_lt, None, ["cnl", "ip"], ["sgl%d" % k], H)
+            scan(T.sm[:, H * k:H * k + H], T.sgl[:, C * k:C * k + H], T.sgl[:, C * k + H:C * k + C], -192.0, A.add, A.add, ["sgl%d" % k], ["sm%d" % k], H // 2)
+        if NV:
+            ts(T.lo[:, 4 - NV:4], T.sm[:, H * (5 - NV) - 1:4 * H:H], 192.0, None, A.add, None, ["sm%d" % k for k in range(4 - NV, 4)], ["lo1"], 4)
+        wrap(T.cva, CLi, T.ctl, 128.0 - K, ["cnl", "ctl"], "cva")
+        wrap(T.cvb, CLe, T.ctl, 128.0 - K, ["cnl", "ctl"], "cvb")
+        tt(T.t1[:], T.cva[:, 15:C:16], T.cvb[:, 15:C:16], A.is_equal, ["cva", "cvb"], ["t1"], 24)
+        line(T.lm[:], T.cvb[:, 15:C:16], 1.0, T.ip[:, 4:5], ["cvb", "cc0"], ["lm"], 24)
+        tt(T.wm[:], T.t1[:], T.lm[:], A.mult, ["t1", "lm"], ["wm"], 24)
+        tt(T.ctlc[:, 15:C:16], T.cil[:], T.wm[:], A.subtract, ["cil", "wm", "ctlc"], ["oo"], 24)
+        wrap(T.cvc, CHe, T.ctlc, 384.0 - K, ["cnh", "oo"], "cvc")
+        cp(T.ou[:], T.cvc[:, 15:C:16], ["cvc"], ["ou"], 24)
+        scan(T.dat[:], CHe, T.crow[:], -256.0, A.max, A.min, ["cnh", "crow"], ["dat"], H)
+        for t in range(4):
+            move(T.bt[:, t:4 * K:4], T.xp[:, W * t:W * t + C].indirect(T.lo[:]), ["xp%d" % t, "lo", "lo1"], ["bt%d" % t], PICK * K)
+        quant(T.qbc[:, 128 * r:128 * r + 128], T.qbs[:, 128 * r:128 * r + 128], T.bt[:], btk + ["btz"], ["qb%d" % r], 128)
+        l0 = (0, 192, 256)[r]
+        send(T.landc[:, l0:l0 + K].bitcast(dt.uint8), T.qbc[:, 128 * r:128 * r + K].bitcast(dt.uint8), "arr%d" % r, 2 * neng, ["qb%d" % r], ["lc%d" % r])
+        send(T.lands[:, l0:l0 + K], T.qbs[:, 128 * r:128 * r + K], "arr%d" % r, 2 * neng, ["qb%d" % r], ["ls%d" % r])
+        if last:
+            move(T.lsend[:], T.ramp[:].indirect(T.lo[:]), ["ramp", "lo", "lo1"], ["lsend"], PICK * K)
+            send(T.lland[:], T.lsend[:], "arrl", neng, ["lsend", "qb%d!" % r], ["lland"])
+
+        cp(T.ew[:].indirect(T.ou[:]), T.dat[:], ["ou", "dat"], ["ew"], PUT * C)
+        scan(T.en[:, 16:C + 16], T.ctf[:], T.ew[:, 256:256 + C], -256.0, A.add, A.max, ["ctf", "ew"], ["en"], H)
+        flip(T.et[:, 0:C], T.en[:, 16:C + 16], ["en"], ["et0"], H)
+        flip(T.et[:, C:2 * C + 32], T.en[:], ["en", "enz0", "enz1"], ["et1"], H + 16)
+        tt(T.em[:, 0:24], T.et[:, 0:C:16], T.et[:, 8:C:16], A.min, ["et0"], ["em0"], 24)
+        tt(T.em[:, 24:50], T.et[:, C:2 * C + 32:16], T.et[:, C + 8:2 * C + 32:16], A.min, ["et1"], ["em1"], 26)
+        ts(T.eo[:], T.em[:].indirect(T.gl[:]), 192.0, None, A.add, None, ["em0", "em1", "gl"], ["eo"], PICK * 32)
+
+        v0 = (0, 128, 192)[r]
+        lk = ["lc%d" % r, "ls%d" % r, "landz"] + (["lc1", "ls1"] if r == 2 else [])
+        for b in range(4):
+            mm(4 + b, 128, T.ec[:, 128 * b:128 * b + 128], T.es[:, 128 * b:128 * b + 128], T.landc[:, v0:v0 + 128], T.lands[:, v0:v0 + 128], True, True, ["e%d" % b] + lk)
+            move(T.xp[:, W * b + C:W * b + W], T["ps%d" % (4 + b)][:, l0 - v0:l0 - v0 + K], ["ps%d" % (4 + b)], ["xa%d" % b], K)
+
+        for h in range(2):
+            n = 13 - h
+            tile = (T.ta, T.tb)[h]
+            for t in range(4):
+                move(tile[:, t:64 * n:4], T.xp[:, W * t:W * t + W].indirect(T.eo[:, 12 * h:12 * h + n]), ["xp%d" % t, "xa%d" % t, "eo"], ["t%d_%d" % (h, t)], PICK * 16 * n)
+            if h:
+                move(T.tb[:, 4 * H:4 * H + 4], T.ta[:, 0:4], ["t0_%d" % t for t in range(4)], ["tbw"], 4)
+            for rot in range(2):
+                i = 2 * h + rot
+                quant(T.qtc[:, H * i:H * i + H], T.qts[:, H * i:H * i + H], tile[:, 4 * rot:4 * rot + 4 * H],
+                      ["t%d_%d" % (h, t) for t in range(4)] + (["tbw"] if i == 3 else []), ["qt%d" % i], H)
+            for b in range(4):
+                for tap in range(2):
+                    i = 2 * h + tap
+                    wq, wp, kk = (T.wq, T.wp, ["wq", "wp"]) if tap == 0 else (T.zq, T.zp, ["zq", "zp"])
+                    mm(4 * h + b, H, wq[:, 128 * b:128 * b + 128], wp[:, 128 * b:128 * b + 128], T.qtc[:, H * i:H * i + H], T.qts[:, H * i:H * i + H], tap == 0, tap == 1, kk + ["qt%d" % i])
+                ps = "ps%d" % (4 * h + b)
+                line(XN[:, 4 * H * h + b:4 * H * (h + 1):4], T[ps][:, 0:H], 0.015625, 0.0, [ps], ["x%d_%d_%d" % (r + 1, h, b)], H)
+            qx(r + 1, h)
+
+    seen.update({"ps0": 4, "ps1": 4, "qx0": 2, "qx1": 2})
+    line(T.ow[:, C:W], T.lland[:], 1.0, 576.0, ["lland"], ["ow1"], K)
+    move(T.olb[:], T.ow[:].indirect(T.eo[:, 0:24]), ["ow0", "ow1", "eo"], ["olb"], PICK * C)
+    dma("y", T.ol[:], T.olb[0:128:16, :], ["olb"], [], LOAD)
+    for h in range(2):
+        mm(h, H, T.qvc[:], T.qvs[:], T.qxc[:, H * h:H * h + H], T.qxs[:, H * h:H * h + H], True, True, ["qv", "qx%d" % h])
+        move(T.ysb[:, H * h:H * h + H], T["ps%d" % h][:, 0:H], ["ps%d" % h], ["y%d" % h], H)
+        dma("y", T.y[:, H * h:H * h + H], T.ysb[:, H * h:H * h + H], ["y%d" % h], [], LOAD + 300)
+        dma("y", T.oc[:, 4 * H * h:4 * H * (h + 1)], T.qxc[:, H * h:H * h + H].bitcast(dt.uint8), ["qx%d" % h], [], LOAD + 300)
+    for k in range(4):
+        dma("sy"[k % 2], T.osc[4 * k:4 * k + 4, :], T.qxs[32 * k:32 * k + 4, :], ["qx0", "qx1"], [], LOAD)
+
     semof = {"v": "sv", "s": "ss", "p": "sp", "q": "sq", "y": None}
     count = {}
     waited = {k: {} for k in queue}
@@ -78,9 +476,9 @@ def rank_program(g, core, T, topo):
             queue[e].wait_ge(T.sem[tok[0]], tok[1])
             waited[e][tok[0]] = tok[1]
 
-    def before(e, rd, wr, chain=False):
-        need = {}
+    for (e, make, _), (_, rd, wr, _, kind, _, _) in _layout(plan):
         toks = []
+        rd = [k for k in rd if k[-1] != "!"]
         for k in rd:
             if k in lastw:
                 toks.append(lastw[k])
@@ -88,412 +486,35 @@ def rank_program(g, core, T, topo):
                 toks += [t for t in readers.get(k, []) if t[0] != semof[e]]
         for k in wr:
             toks += readers.get(k, [])
-            if k in lastw and not chain:
+            if k in lastw and kind != "chain":
                 toks.append(lastw[k])
+        need = {}
         for t in toks:
             need[t[0]] = max(need.get(t[0], 0), t[1])
         for s in need:
             wait(e, (s, need[s]))
-
-    def after(tok, rd, wr):
+        if kind == "dma":
+            s = "d%d" % ndma[0]
+            ndma[0] += 1
+            make().then_inc(T.sem[s], 16)
+            count[s] = 16
+            tok = (s, 16)
+        elif kind is None or kind == "chain":
+            s = semof[e]
+            count[s] = count.get(s, 0) + 1
+            make().then_inc(T.sem[s], 1)
+            tok = (s, count[s])
+        else:
+            make()
+            count["sent"] = count.get("sent", 0) + neng
+            count[kind[0]] = kind[1]
+            tok = kind
+            rd = []
         for k in rd:
             readers.setdefault(k, []).append(tok)
         for k in wr:
             lastw[k] = tok
             readers[k] = []
-
-    def op(e, make, rd, wr, chain=False):
-        before(e, rd, wr, chain)
-        s = semof[e]
-        count[s] = count.get(s, 0) + 1
-        make().then_inc(T.sem[s], 1)
-        after((s, count[s]), rd, wr)
-
-    def dma(e, out, in_, rd, wr):
-        before(e, rd, wr)
-        s = "d%d" % ndma[0]
-        ndma[0] += 1
-        queue[e].dma_start(out, in_).then_inc(T.sem[s], 16)
-        count[s] = 16
-        after((s, 16), rd, wr)
-
-    def send(out, in_, sem, rd):
-        before("q", rd, [])
-        g.remote_dma(out, in_, T.sem[sem], T.sem.sent, pid, rid, mask)
-        count["sent"] = count.get("sent", 0) + neng
-        count[sem] = count.get(sem, 0) + neng
-
-    V, S, P = g.vector, g.scalar, g.tensor
-
-    def ts(out, in0, s1, s2, o0, o1, rd, wr):
-        if o1 is None:
-            op("v", lambda: V.tensor_scalar(out, in0, s1, None, o0), rd, wr)
-        else:
-            op("v", lambda: V.tensor_scalar(out, in0, s1, s2, o0, o1), rd, wr)
-
-    def tt(out, a, b, o, rd, wr):
-        op("v", lambda: V.tensor_tensor(out, a, b, o), rd, wr)
-
-    def cp(out, in_, rd, wr):
-        op("v", lambda: V.tensor_copy(out, in_), rd, wr)
-
-    def scan(out, d0, d1, init, o0, o1, rd, wr):
-        op("v", lambda: V.tensor_tensor_scan(out, d0, d1, init, o0, o1), rd, wr)
-
-    def flip(out, in_, rd, wr):
-        op("v", lambda: V.transpose(out, in_), rd, wr)
-
-    def quant(oc, osc, in_, rd, wr):
-        op("v", lambda: V.quantize_mx(oc, osc, in_), rd, wr)
-
-    def act(out, in_, func, rd, wr, **kw):
-        op("s", lambda: S.activation(out, in_, func, **kw), rd, wr)
-
-    def move(e, out, in_, rd, wr):
-        if e == "v":
-            cp(out, in_, rd, wr)
-        else:
-            act(out, in_, F.Copy, rd, wr)
-
-    def mm(bank, n, lc, ls, rc, rs, start, stop, rd):
-        op("p", lambda: P.matmul_mx(T["ps%d" % bank][:, 0:n], lc, ls, rc, rs, start, stop), rd, ["ps%d" % bank], chain=not start)
-
-    def iota(out, pat, base, cm, wr, fl=True):
-        if fl:
-            op("q", lambda: g.iota(out, pat, base, cm, allow_small_or_imprecise_dtypes=True), [], wr)
-        else:
-            op("q", lambda: g.iota(out, pat, base, cm), [], wr)
-
-    def keep(out, in_, pat, base, cm, o, rd, wr):
-        op("q", lambda: g.affine_select(out, in_, pat, o, 0.0, base, cm), rd, wr)
-
-    def fill(ap, c, wr):
-        op("v", lambda: V.memset(ap, c), [], wr)
-
-    def xkeys(r, halves=(0, 1)):
-        return ["x%d_%d_%d" % (r, h, b) for h in halves for b in range(4)]
-
-    def qx(r, h):
-        quant(T.qxc[:, H * h:H * h + H], T.qxs[:, H * h:H * h + H], T["xw%d" % r][:, 4 * H * h:4 * H * (h + 1)], xkeys(r, (h,)), ["qx%d" % h])
-
-    dma("s", T.ut[:], T.u[:], [], ["ut"])
-    dma("y", T.xw0[:, 0:4 * H], T.x[:, 0:4 * H], [], xkeys(0, (0,)))
-    dma("y", T.xw0[:, 4 * H:4 * C], T.x[:, 4 * H:4 * C], [], xkeys(0, (1,)))
-    dma("y", T.wq[:].bitcast(dt.uint8), T.wc[:], [], ["wq"])
-    dma("y", T.zq[:].bitcast(dt.uint8), T.zc[:], [], ["zq"])
-    dma("y", T.wp[:], T.ws[:], [], ["wp"])
-    dma("y", T.zp[:], T.zs[:], [], ["zp"])
-    dma("y", T.vt[:], T.v[:], [], ["vt"])
-
-    btk = ["bt0", "bt1", "bt2", "bt3"]
-    iota(T.ci[:, 0:8], [[16, 8]], 0, 0, ["ci0"], False)
-    iota(T.ci[:, 8:24], [[16, 2], [32, 4], [0, 2]], 0, 0, ["ci1"], False)
-    iota(T.ci[:, 24:48], [[1, 12], [12, 2]], 0, 0, ["ci2"], False)
-    iota(T.ci[:, 48:60], [[12, 12]], 11, 0, ["ci3"], False)
-    iota(T.pi[:], [[0, 24]], 0, 1, ["pi"], False)
-    iota(T.im[:], [[1, 16]], 0, -1, ["im"], False)
-    iota(T.ia[:], [[16, 24]], 0, 0, ["ia"])
-    fill(T.onek[:], UNIT, ["onek"])
-    fill(T.cst[:], 0.0, ["cst"])
-    keep(T.cs0[:], T.onek[:], [[-2, 2], [0, 16], [1, 4]], 0, 0, A.is_ge, ["onek"], ["cs0"])
-    for a in range(4):
-        keep(T.cst[32 * a:32 * a + 32, 128 * a:128 * a + 128], T.cs0[32 * a:32 * a + 32, :], [[2, 2], [0, 16], [-1, 4]], 1, 0, A.is_ge,
-             ["cs0", "cst"] + ["cst%d" % i for i in range(a)], ["cst%d" % a])
-    before("q", ["cst3"], [])
-    iota(T.qt[:, 320:C], [[0, C - 320]], 0, 0, ["qtz"])
-    iota(T.zero[:], [[0, C]], 0, 0, ["zero"])
-    iota(T.cnl[:, 0:16], [[0, 16]], -K, 0, ["cnl"])
-    iota(T.cnh[:, 0:16], [[0, 16]], 256 - K, 0, ["cnh"])
-    iota(T.gl_[:, C:C + 16], [[0, 16]], 0, 0, ["glz"])
-    iota(T.ah[:, C:C + 16], [[0, 16]], 0, 0, ["ahz"])
-    iota(T.bt[:, 4 * K:512], [[0, 512 - 4 * K]], 0, 0, ["btz"])
-    iota(T.ramp[:], [[1, C]], -192, 0, ["ramp"])
-    iota(T.gr[:, 0:16], [[32, 8], [C + 32, 2]], 0, 0, ["gr0"])
-    iota(T.gr[:, 16:32], [[32, 8], [-C, 2]], C + 16, 0, ["gr1"])
-    iota(T.gk[:], [[8, 2], [256, 2]], 0, 0, ["gk"])
-    iota(T.en[:, 0:16], [[0, 16]], 0, 0, ["enz0"])
-    iota(T.en[:, C + 16:C + 32], [[0, 16]], 0, 0, ["enz1"])
-    keep(T.gt[:], T.ones[:], [[1, 516]], -3, -4, A.is_equal, ["ones"], ["gt"]) if False else None
-    iota(T.ow[:, 0:C], [[1, C]], 0, 0, ["ow0"])
-    for buf, n, step in ((T.k12, 48, 12), (T.k32, 64, 32)):
-        key = "k%d" % step
-        fill(buf[:, 0:2 * n], 0.0, [key + "a"])
-        fill(buf[:, 2 * n:3 * n], 1.0, [key + "b"])
-    fill(T.zt[:], 0.0, ["zt"])
-    for buf, n, step in ((T.k12, 48, 12), (T.k32, 64, 32)):
-        key = "k%d" % step
-        fill(buf[:, 0:n:step], -4.0, [key + "a"])
-        fill(buf[:, 2 * n:3 * n:step], 0.0, [key + "b"])
-    fill(T.ones[:], 1.0, ["ones"])
-    for buf, n, step in ((T.k12, 48, 12), (T.k32, 64, 32)):
-        fill(buf[:, n:2 * n:step], 4.0, ["k%da" % step])
-    keep(T.gt[:], T.ones[:], [[1, 516]], -3, -4, A.is_equal, ["ones"], ["gt"])
-    cp(T.cu[:], T.ci[:], ["ci0", "ci1", "ci2", "ci3"], ["cu"])
-    ts(T.pj[:], T.pi[:], 15, None, A.bitwise_and, None, ["pi"], ["pj"])
-    quant(T.landc[:, 64:192], T.lands[:, 64:192], T.zt[:], ["zt"], ["landz"])
-    ts(T.im2[:], T.im[:], 15, None, A.bitwise_and, None, ["im"], ["im2"])
-    cp(T.qf[:], T.pj[:, 0:2], ["pj"], ["qf"])
-    cp(T.pu[:], T.pj[:], ["pj"], ["pu"])
-    ts(T.c16[:], T.im2[:], 15.0, 128.0, A.is_equal, A.mult, ["im2"], ["c16"])
-    ts(T.il[:], T.ia[:], T.qf[:, 0:1], None, A.add, None, ["ia", "qf"], ["il"])
-    quant(T.quc[:], T.qus[:], T.ut[:], ["ut"], ["qu"])
-    qx(0, 0)
-    act(T.pus[:], T.qus[:].indirect(T.cu[:, 0:24]), F.Copy, ["qu", "cu"], ["pus"])
-    cp(T.puc[:].bitcast(dt.uint32), T.quc[:].bitcast(dt.uint32).indirect(T.cu[:, 0:24]), ["qu", "cu"], ["puc"])
-    act(T.ip[:], T.il[:, 0:4], F.Identity, ["il"], ["ip"], bias=0.5 - K)
-    act(T.cc[:, 0:1], T.c16[:, 15:16], F.Identity, ["c16"], ["cc0"], bias=256.0 - K)
-    act(T.half[:, 0:1], T.qf[:, 0:1], F.Sign, ["qf"], ["hf0"], bias=-7.5)
-
-    def score(bank, j, c0, c1, rd):
-        mm(bank, c1 - c0, T.puc[:, 128 * j:128 * j + 128], T.pus[:, 128 * j:128 * j + 128], T.qxc[:, c0:c1], T.qxs[:, c0:c1], True, True, ["puc", "pus"] + rd)
-
-    def turn(bank, h):
-        flip(T.pt[:, H * h:H * h + H], T["ps%d" % bank][:, 0:H], ["ps%d" % bank], ["pt%d" % h])
-
-    def wrap(out, src, ctl, init, rd, okey):
-        scan(out[:], src, ctl[:], init, A.min, A.add, rd, [okey])
-
-    def early_scores():
-        score(0, 0, 0, H, ["qx0"])
-        score(1, 2, 0, H, ["qx0"])
-
-    early_scores()
-    qx(0, 1)
-    turn(0, 0)
-
-    for r in range(R):
-        last = r == R - 1
-        X, XN = T["xw%d" % r], T["xw%d" % (r + 1)]
-        xk = xkeys(r)
-        score(3, 0, H, C, ["qx1"])
-        score(4, 2, 0, C, ["qx0", "qx1"])
-        score(2, 1, 0, C, ["qx0", "qx1"])
-
-        def row(e, b):
-            if b < 4:
-                return T.sg[:, 128 * (4 * e + b):128 * (4 * e + b) + 128], "sg%d" % (4 * e + b)
-            return T["tri%d" % (b // 2)][:, 2 * e + b % 2:4 * _reach(b):4], "tr%d_%d" % (b, e)
-
-        def sgn(e, b):
-            bank = "ps1" if e else "ps2"
-            out, key = row(e, b)
-            act(out, T[bank][:, 0:_reach(b)], F.Sign, [bank, "pt%d" % (b // 6)], [key, "rho%d" % (12 * e + b)],
-                bias=T.pt[:, 32 * b + 16 * e:32 * b + 16 * e + 1], scale=-1.0, accum_out=T.rho[:, 12 * e + b:12 * e + b + 1])
-
-        def cmp(b):
-            out, key = row(1, b)
-            ts(out, T.ps4[:, 0:_reach(b)], T.pt[:, 32 * b + 16:32 * b + 17], -2.0, A.is_ge, A.mult, ["ps4", "pt1"], [key])
-
-        def cnt(b):
-            n, t, tri = _reach(b), 2 + b % 2, T["tri%d" % (b // 2)]
-            e = H * (b - 5)
-            scan(T.sj[:, e - n // 2:e], tri[:, t:2 * n:4], tri[:, 2 * n + t:4 * n:4], 2.0 * n - C, A.add, A.add, ["tr%d_1" % b], ["sj%d" % b])
-
-        def cols(k):
-            n = 64 * k
-            o = {5: 0, 4: 320, 3: 576, 2: 768}[k]
-            quant(T.qfc[:, o:o + n], T.qfs[:, o:o + n], T["tri%d" % k][:, 0:4 * n], ["tr%d_%d" % (b, e) for b in (2 * k, 2 * k + 1) for e in (0, 1)], ["qf%d" % k])
-            mm(5, n, T.csc[:], T.css[:], T.qfc[:, o:o + n], T.qfs[:, o:o + n], k == 5, k == 2, ["cs", "qf%d" % k])
-
-        for b in (4, 5, 0, 1, 2, 3):
-            sgn(1, b)
-        turn(3, 1)
-        for b in (10, 11, 8, 9, 6, 7, 4, 5, 0, 1, 2, 3):
-            sgn(0, b)
-        cmp(10)
-        cmp(11)
-        cnt(10)
-        cmp(8)
-        cnt(11)
-        if r == 0:
-            quant(T.csc[:], T.css[:], T.cst[:], ["cst%d" % a for a in range(4)], ["cs"])
-        cmp(9)
-        cols(5)
-        cnt(8)
-        cmp(6)
-        cnt(9)
-        cmp(7)
-        cols(4)
-        cols(3)
-        cols(2)
-        cnt(6)
-        cnt(7)
-
-        def plane(t):
-            act(T.xp[:, W * t:W * t + C], X[:, t:4 * C:4], F.Copy, xk, ["xp%d" % t])
-
-        plane(0)
-        plane(1)
-        ts(T.kr[:, 12:18], T.rho[:, 12:18], -UNIT, (C + H) * UNIT, A.mult, A.add, ["rho%d" % i for i in range(12, 18)], ["kr1"])
-        ts(T.kr[:, 18:24], T.sj[:, H - 1:6 * H:H], -UNIT, C * UNIT, A.mult, A.add, ["sj%d" % b for b in range(6, 12)], ["kr2"])
-        flip(T.qt[:, 0:320], T.ps5[:, 0:320], ["ps5"], ["qt"])
-        ts(T.kr[:, 0:12], T.rho[:, 0:12], -UNIT, C * UNIT, A.mult, A.add, ["rho%d" % i for i in range(12)], ["kr0"])
-        tt(T.kk[:, 12:24], T.qt[:, 16:C:32], T.kr[:, 12:24], A.add, ["qt", "qtz", "kr1", "kr2"], ["kk1"])
-        tt(T.kk[:, 0:12], T.qt[:, 0:C:32], T.kr[:, 0:12], A.add, ["qt", "qtz", "kr0"], ["kk0"])
-        kkk = ["kk0", "kk1"]
-        for i, n in ((0, 2 * (C - K) + 0.5), (1, 2 * K + 0.5)):
-            ts(T.fa[:, 24 * i:24 * i + 24], T.kk[:], n * UNIT, None, A.is_gt, None, kkk, ["fa%d" % i])
-        for i in range(2):
-            tt(T.aa[:, 24 * i:24 * i + 24], T.kk[:], T.fa[:, 24 * i:24 * i + 24], A.subtract, kkk + ["fa%d" % i], ["aa%d" % i])
-        scan(T.st[:, 96:144], T.k12[:, 96:144], T.fa[:], 0.0, A.mult, A.add, ["k12b", "fa0", "fa1"], ["st2"])
-        scan(T.st[:, 0:48], T.k12[:, 0:48], T.aa[:], 0.0, A.add, A.max, ["k12a", "aa0", "aa1"], ["st0"])
-        scan(T.st[:, 48:96], T.k12[:, 48:96], T.aa[:], 0.0, A.add, A.min, ["k12a", "aa0", "aa1"], ["st1"])
-        act(T.sw[:], T.st[:].indirect(T.cu[:, 48:60]), F.Copy, ["st0", "st1", "st2", "cu"], ["sw"])
-        cp(T.k1[:], T.kk[:].indirect(T.cu[:, 24:48]), kkk + ["cu"], ["k1"])
-        plane(2)
-        plane(3)
-        if r == 0:
-            act(T.half[:, 1:2], T.half[:, 0:1], F.Identity, ["hf0"], ["hf1"], scale=-256.0)
-            act(T.ctl[:], T.c16[:].indirect(T.pu[:]), F.Copy, ["c16", "pu"], ["ctl"])
-        act(T.ew[:, 256:256 + C], T.zero[:], F.Identity, ["zero", "hf1"], ["ew"], bias=T.half[:, 1:2])
-        flip(T.su[:], T.sw[:], ["sw"], ["su"])
-        flip(T.ky[:], T.k1[:], ["k1"], ["ky"])
-        scan(T.sx[:, 128:192], T.k32[:, 128:192], T.su[:, 128:192], 0.0, A.mult, A.add, ["k32b", "su"], ["sx2"])
-        scan(T.sx[:, 64:128], T.k32[:, 64:128], T.su[:, 64:128], 0.0, A.add, A.min, ["k32a", "su"], ["sx1"])
-        scan(T.sx[:, 0:64], T.k32[:, 0:64], T.su[:, 0:64], 0.0, A.add, A.max, ["k32a", "su"], ["sx0"])
-        for i, n in ((0, K - 0.5), (1, C - K + 0.5)):
-            ts(T.ty[:, i:i + 1], T.sx[:, 159 + 32 * i:160 + 32 * i], n, T.sx[:, 95 + 32 * i:96 + 32 * i], A.is_gt, A.add, ["sx1", "sx2"], ["tz%d" % i])
-        for i in range(2):
-            ts(T.ty[:, 2 + i:3 + i], T.ty[:, i:i + 1], T.sx[:, 31 + 32 * i:32 + 32 * i], None, A.max, None, ["tz%d" % i, "sx0"], ["ty%d" % i])
-
-        tl, th = T.ty[:, 2:3], T.ty[:, 3:4]
-        CLi, CLe, CHi, CHe = T.cnl[:, 16:C + 16], T.cnl[:, 15:C + 15], T.cnh[:, 16:C + 16], T.cnh[:, 15:C + 15]
-        ts(T.gl_[:, 0:C], T.ky[:], tl, None, A.is_ge, None, ["ky", "ty0"], ["gl_"])
-        ts(T.al[:], T.ky[:], tl, None, A.is_gt, None, ["ky", "ty0"], ["al"])
-        scan(T.capl[:, ::-1], T.zero[:], T.gl_[:, C:0:-1], 0.0, A.add, A.subtract, ["zero", "gl_", "glz"], ["capl"])
-        ts(T.ah[:, 0:C], T.ky[:], th, None, A.is_lt, None, ["ky", "ty1"], ["ah"])
-        scan(CLi, T.al[:], T.capl[:], -float(K), A.add, A.max, ["al", "capl"], ["cnl"])
-        scan(T.caph[:, ::-1], T.zero[:], T.ah[:, C:0:-1], 256.0, A.add, A.subtract, ["zero", "ah", "ahz"], ["caph"])
-        ts(T.gh[:], T.ky[:], th, None, A.is_le, None, ["ky", "ty1"], ["gh"])
-
-        for k in range(4):
-            act(T.sgl[:, C * k:C * k + C], CLi, F.Sign, ["cnl", "ip"], ["sgl%d" % k, "dl%d" % k], bias=T.ip[:, k:k + 1], scale=-1.0, accum_out=T.dl[:, k:k + 1])
-        if r == 0:
-            cp(T.ctlc[:], T.ctl[:], ["ctl"], ["ctlc"])
-        wrap(T.cva, CLi, T.ctl, 128.0 - K, ["cnl", "ctl"], "cva")
-        scan(CHi, T.gh[:], T.caph[:], 256.0 - K, A.add, A.min, ["gh", "caph"], ["cnh"])
-        if r == 0:
-            tt(T.ctlc[:, 15:C:16], T.ctl[:, 15:C:16], T.il[:], A.add, ["ctl", "il"], ["ctlc"])
-            ts(T.half[:, 2:3], T.half[:, 0:1], 256.0, None, A.mult, None, ["hf0"], ["hf2"])
-            ts(T.half[:, 3:4], T.half[:, 0:1], 512.0, -512.0, A.mult, A.add, ["hf0"], ["hf3"])
-        wrap(T.cvb, CLe, T.ctl, 128.0 - K, ["cnl", "ctl"], "cvb")
-        if r == 0:
-            ts(T.crow[:], T.ramp[:], T.half[:, 2:3], None, A.max, None, ["ramp", "hf2"], ["crow"])
-        wrap(T.cvc, CHe, T.ctlc, 384.0 - K, ["cnh", "ctlc"], "cvc")
-        tt(T.t1[:], T.cva[:, 15:C:16], T.cvb[:, 15:C:16], A.subtract, ["cva", "cvb"], ["t1"])
-        scan(T.dat[:], CHe, T.crow[:], -256.0, A.max, A.min, ["cnh", "crow"], ["dat"])
-        ts(T.lm[:], T.t1[:], -640.0, T.cc[:, 0:1], A.mult, A.add, ["t1", "cc0"], ["lm"])
-        if r == 0:
-            ts(T.ctf[:], T.zero[:], T.half[:, 3:4], None, A.add, None, ["zero", "hf3"], ["ctf"])
-        tt(T.wm[:], T.cvb[:, 15:C:16], T.lm[:], A.min, ["cvb", "lm"], ["wm"])
-        ts(T.lo[:], T.dl[:], 0.5, 192.0, A.mult, A.add, ["dl%d" % k for k in range(4)], ["lo"])
-        tt(T.oo[:], T.cvc[:, 15:C:16], T.wm[:], A.subtract, ["cvc", "wm"], ["oo"])
-        for t in range(4):
-            move("vsvs"[t], T.bt[:, t:4 * K:4], T.xp[:, W * t:W * t + C].indirect(T.lo[:]), ["xp%d" % t, "lo"], ["bt%d" % t])
-        cp(T.ou[:], T.oo[:], ["oo"], ["ou"])
-        quant(T.qbc[:, 128 * r:128 * r + 128], T.qbs[:, 128 * r:128 * r + 128], T.bt[:], btk + ["btz"], ["qb%d" % r])
-        l0 = (0, 192, 256)[r]
-        send(T.landc[:, l0:l0 + K].bitcast(dt.uint8), T.qbc[:, 128 * r:128 * r + K].bitcast(dt.uint8), "arr%d" % r, ["qb%d" % r])
-        send(T.lands[:, l0:l0 + K], T.qbs[:, 128 * r:128 * r + K], "arr%d" % r, ["qb%d" % r])
-        lastw["land%d" % r] = ("arr%d" % r, 2 * neng)
-
-        if last:
-            act(T.lsend[:], T.ramp[:].indirect(T.lo[:]), F.Copy, ["ramp", "lo"], ["lsend"])
-            send(T.lland[:], T.lsend[:], "arrl", ["lsend"])
-            lastw["lland"] = ("arrl", neng)
-        cp(T.ew[:].indirect(T.ou[:]), T.dat[:], ["ou", "dat"], ["ew"])
-
-        def unit(b):
-            if r == 0:
-                quant(T.ec[:, 128 * b:128 * b + 128], T.es[:, 128 * b:128 * b + 128], T.gt[:, 3 - b:515 - b], ["gt"], ["e%d" % b])
-
-        unit(0)
-        scan(T.en[:, 16:C + 16], T.ctf[:], T.ew[:, 256:256 + C], -256.0, A.add, A.max, ["ctf", "ew"], ["en"])
-        unit(1)
-        if r == 0:
-            flip(T.gq[:], T.gr[:], ["gr0", "gr1"], ["gq"])
-        flip(T.et[:, 0:C], T.en[:, 16:C + 16], ["en"], ["et0"])
-        if r == 0:
-            tt(T.gs[:], T.gq[:, 0:4], T.gk[:], A.add, ["gq", "gk"], ["gs"])
-        flip(T.et[:, C:2 * C + 32], T.en[:], ["en", "enz0", "enz1"], ["et1"])
-        if r == 0:
-            ts(T.gl[:], T.gs[:], 2.0 * C + 31, None, A.min, None, ["gs"], ["gl"])
-        unit(2)
-        cp(T.eg[:], T.et[:].indirect(T.gl[:]), ["et0", "et1", "gl"], ["eg"])
-        unit(3)
-        tt(T.em[:], T.eg[:, 0:24], T.eg[:, 32:56], A.min, ["eg"], ["em"])
-        ts(T.eo[:], T.em[:], 192.0, None, A.add, None, ["em"], ["eo"])
-
-        v0 = (0, 128, 192)[r]
-        lk = ["land%d" % r, "landz"] + (["land1"] if r == 2 else [])
-        for b in range(4):
-            mm(4 + b, 128, T.ec[:, 128 * b:128 * b + 128], T.es[:, 128 * b:128 * b + 128], T.landc[:, v0:v0 + 128], T.lands[:, v0:v0 + 128], True, True, ["e%d" % b] + lk)
-            move("s", T.xp[:, W * b + C:W * b + W], T["ps%d" % (4 + b)][:, l0 - v0:l0 - v0 + K], ["ps%d" % (4 + b)], ["xa%d" % b])
-
-        def gather(e, h, t):
-            n = 13 - h
-            move(e, (T.ta, T.tb)[h][:, t:64 * n:4], T.xp[:, W * t:W * t + W].indirect(T.eo[:, 12 * h:12 * h + n]),
-                 ["xp%d" % t, "xa%d" % t, "eo"], ["t%d_%d" % (h, t)])
-
-        def qt(h, rot):
-            i = 2 * h + rot
-            quant(T.qtc[:, H * i:H * i + H], T.qts[:, H * i:H * i + H], (T.ta, T.tb)[h][:, 4 * rot:4 * rot + 4 * H],
-                  ["t%d_%d" % (h, t) for t in range(4)] + (["tbw"] if i == 3 else []), ["qt%d" % i])
-
-        def layer(h):
-            for tap, b in ((0, 0), (0, 1), (1, 0), (1, 1), (0, 2), (1, 2), (0, 3), (1, 3)):
-                i = 2 * h + tap
-                wq, wp, kk = (T.wq, T.wp, ["wq", "wp"]) if tap == 0 else (T.zq, T.zp, ["zq", "zp"])
-                mm(4 * h + b, H, wq[:, 128 * b:128 * b + 128], wp[:, 128 * b:128 * b + 128], T.qtc[:, H * i:H * i + H], T.qts[:, H * i:H * i + H], tap == 0, tap == 1, kk + ["qt%d" % i])
-
-        def evac(e, h, b):
-            out, ps, key = XN[:, 4 * H * h + b:4 * H * (h + 1):4], "ps%d" % (4 * h + b), "x%d_%d_%d" % (r + 1, h, b)
-            if e == "v":
-                ts(out, T[ps][:, 0:H], 0.015625, None, A.mult, None, [ps], [key])
-            else:
-                act(out, T[ps][:, 0:H], F.Copy, [ps], [key], scale=0.015625)
-
-        for t in range(4):
-            gather("vsvs"[t], 0, t)
-        qt(0, 0)
-        qt(0, 1)
-        layer(0)
-        cp(T.tb[:, 4 * H:4 * H + 4], T.ta[:, 0:4], ["t0_%d" % t for t in range(4)], ["tbw"])
-        for t in range(4):
-            gather("vsss"[t], 1, t)
-        qt(1, 0)
-        qt(1, 1)
-        layer(1)
-        for b in range(4):
-            evac("ssvs"[b], 0, b)
-        if r == 0:
-            quant(T.qvc[:], T.qvs[:], T.vt[:], ["vt"], ["qv"])
-        qx(r + 1, 0)
-        if not last:
-            early_scores()
-            evac("s", 1, 0)
-            evac("s", 1, 1)
-            evac("v", 1, 2)
-            turn(0, 0)
-            evac("s", 1, 3)
-            qx(r + 1, 1)
-        else:
-            mm(0, H, T.qvc[:], T.qvs[:], T.qxc[:, 0:H], T.qxs[:, 0:H], True, True, ["qv", "qx0"])
-            dma("y", T.oc[:, 0:4 * H], T.qxc[:, 0:H].bitcast(dt.uint8), ["qx0"], [])
-            for b in range(4):
-                evac("ssvv"[b], 1, b)
-            act(T.ow[:, C:W], T.lland[:], F.Identity, ["lland"], ["ow1"], bias=576.0)
-            act(T.olb[:], T.ow[:].indirect(T.eo[:]), F.Copy, ["ow0", "ow1", "eo"], ["olb"])
-            qx(r + 1, 1)
-            mm(1, H, T.qvc[:], T.qvs[:], T.qxc[:, H:C], T.qxs[:, H:C], True, True, ["qv", "qx1"])
-            dma("s", T.ol[:], T.olb[0:128:16, :], ["olb"], [])
-            for k in range(4):
-                dma("s", T.osc[4 * k:4 * k + 4, :], T.qxs[32 * k:32 * k + 4, :], ["qx0", "qx1"], [])
-            dma("y", T.oc[:, 4 * H:4 * C], T.qxc[:, H:C].bitcast(dt.uint8), ["qx1"], [])
-            cp(T.ysb[:, 0:H], T.ps0[:, 0:H], ["ps0"], ["ya"])
-            dma("y", T.y[:, 0:H], T.ysb[:, 0:H], ["ya"], [])
-            cp(T.ysb[:, H:C], T.ps1[:, 0:H], ["ps1"], ["yb"])
-            dma("y", T.y[:, H:C], T.ysb[:, H:C], ["yb"], [])
 
     for s in count:
         wait("q", (s, count[s]))

@@ -1,4 +1,4 @@
-from concourse.mybir import dt, AluOpType, ActivationFunctionType
+from concourse.mybir import dt, AluOpType, AxisListType, ActivationFunctionType
 
 A, F = AluOpType, ActivationFunctionType
 C, K, R = 384, 64, 3
@@ -9,18 +9,19 @@ Q4, U8, BF, F32, I32, U16, F16 = "float8_e4m3fn_x4", "uint8", "bfloat16", "float
 CYC, PICK, PUT, COL, LOAD, SEND, VFIX, SFIX = 0.83, 1.56, 3.8, 0.55, 1200, 2500, 50, 65
 VB = 4
 NV = 1
-ORDER = """cgka +cx0_0a ccua ps1a crampa cila:s +cgr0a tr5_1a cgwza ps2a tr4_1a sj5a +cci0a chf3a:s ps3a sg4a +ccnla pt1a +coneka sj4a
-xp0a:q +ccst0a tr11_1a ccst0b:s tr8_1a tr7_1a +cx1_0a sj8a tr10_1a ccsa +czpa ps4a +cci1a tr6_1a xp2a:q sj7a ps2b sg7a +cgr1a sg5a sg6a
-tr9_0a tr10_0a tr9_1a tr4_0a tr11_0a qf5a qf4a cim2a tr8_0a tr7_0a +czeroa tr6_0a xp1a:q qf3a tr5_0a cvta cbtza qf2a sj10a +ck120a sg1a
-sg0a cipa:s +cwpa ps5a ps5b fa1a sj6a +cuta ck321a +ciaa +ccs0a sg2a sj9a sg3a kr0a:s sj11a +cpia kr1a:s kr2a:s ps5c xp3a:q nb0a chf1a:s
-chf2a:s kk0a ps5d qta kk1a k10a:s fa0a k11a:s nb1a aa1a aa0a st1a st0a swa:s ky0a ccrowa ky1a cahza cc16a cpua +clandza tz0a tz1a cctla:s
-cprea:s ty0a ty1a +cci3a sua sx0a sx1a gwa ccc0a:s ala capla aha cnla sgl2a sgl1a capha sgl3a cctlca cvba cvaa gha sgl0a sm3a t1a cnha
-lo1a lma:s ccila:s +ccu0a loa bt1a:s bt2a:s wma cgsa bt0a:v ooa data cvca qba bt3a:s oua cgta ce1a ewb cgla lsenda:v cctfa:s ce0a ena
-ce3a et0a et1a lca em0a lsa ps7a ce2a em1a xa3a:v ps4b ps5e +ccs1a xa0a:s +conesa +cqua +cpusa +cqx0a eoa +cci2a xa1a:s +ccst2a:s ps6a
-llanda cow0a +cenz0a cqva +ccnha +cenz1a t0_3a:s +cpuca t0_1a:s t1_3a:s xa2a:v t1_2a:s +cima t0_0a:v czqa ps3b t0_2a:v qt0a ps2c +cqtza
-tbwa:v qt1a ps2d +cpja ps3c t1_1a:s ps0c ow1a:v olba:s olbb +cqx1a +ccst3a:s ps1b +ewa:q ps4d x0_3a:s +ck320a ps1c x0_1a:s ps0b x0_0a:s
-+cgqa +ck121a +cqfa +chf0a qx0c t1_0a:v qt2a ps5f qt3a ps6b x1_0a:s ps4c ps7b ps5g x1_1a:s +ccst1a:s ps7c qx1c qx0a x0_2a:v x1_2a:s ps6c
-+pt0a qx0d cwqa x1_3a:v +ps0a qx1a qx0e qx0g ps0e y0a:s y0b ps1e y1a:v qx0f y1b"""
+ORDER = """+cx0_0a +cx1_0a +cpia +coneka +czeroa ps2a +czpa tr5_1a cahza tr4_1a ccst1a:s +cci0a ps1a sg7a sg4a ccsa ps3a pt1a sj5a +cpja
++ccs0a sg6a xp0a:q +cuta ps4a +cnt0a +clandza +cpua sj4a tr10_1a czqa tr6_1a tr11_1a sg5a ps7a tr6_0a +cqfa tr11_0a tr10_0a tr8_0a tr9_1a
++conesa tr7_1a tr9_0a tr8_1a tr7_0a sj11a qf5a qf4a qf3a sj10a tr4_0a tr5_0a qf2a sg3a sj9a sj7a sg1a sj6a sj8a kr1a:s sg0a cgqa ps5a
+ps5b ps5c ps5d qta +ciaa +cila:s ccrowa sg2a +ccst0a kr2a:s kk1a +ciq2a:s kr0a:s kk0a +cci1a +ccs1a ccua nt1a nt3a fa0a nt2a +ccu0a
++cetza nt0a +ck121a cctla:s cgla fa1a aa0a +cqua nqa ps6a aa1a k10a:s k11a:s st0a st1a st3a st2a sw1a:s sw0a:v ky0a su0a +cipa:s cctlca
+su1a sx0a nb0a nb1a sx1a ccc0a:s sx2a sx3a +ciq1a:s tz0a ty0a ky1a +chf0a +ccst3a:s +cima tz1a ty1a gwa +cgta ala capla cprea:s +chf2a:s
+aha cnla capha +cenz1a zza cvaa +cqx0a +cqtza sgl3a cvba sm3a cctlcb +cwpa +cpus0a +cgr0a cow0a tqa gia gha +ccst2a:s +cpus2a sgl0a cnha
+sgl1a t1a sgl2a +cci3a lo1a xp3a:q loa cvca lma:s wma +cci2a bt1a:s cwqa bt2a:v +ccnla +ck120a bt0a:v ooa bt3a:s qba lsa +cbtza +ciq0a:s
+chf3a:s +cpuc0a ce3a ou0a cvta lsenda:s ce0a data cctfa:s +chf1a:s ce2a ew0b ce1a ou1a en0a ew1a et0a et1a en1a em0a et2a et3a eo0a lca
+ps4b xa0a:s ps7b xa3a:s +ccnha +ccst0b:s ps5e xa1a:v em1a ps6b llanda xa2a:s t0_0a:v eo1a t0_3a:s +cpuc1a t0_1a:s t1_1a:s t1_3a:s +cgr1a
++cpus1a t0_2a:v +cenz0a qt0a ps2b ps1b qt1a ps1c +crampa ps2c t1_2a:s tbwa:s x0_2a:s +cim2a ps0b ps3b ps3c ow1a:s cqva x0_3a:s t1_0a:v
+qt2a qt3a x0_1a:v ps0c x0_0a:v +ew0a:q ps7c ps4c ps4d +cpuc2a ps6c ps6d ps7d ps5f ps5g olb1a:s qx0a ps0e +ps0a x1_2a:v +cc16a qx0c +cgwza
++pt0a x1_0a:s olb0a:v x1_3a:s +cqx1a x1_1a:s +xp2a:q +xp1a:q qx1a qx0e ps1e olb0b y0a:s y0b qx1c qx0f qx0g qx0d y1a:v y1b"""
 
 
 def _sb(n, d):
@@ -34,27 +35,27 @@ SCRATCH = {
     "wq": _sb(512, Q4), "wp": _sb(512, U8), "zq": _sb(512, Q4), "zp": _sb(512, U8),
     "gt": _sb(516, BF), "ones": _sb(516, BF), "onek": _sb(128, BF), "ec": _sb(512, Q4), "es": _sb(512, U8),
     "ci": _sb(60, I32), "cu": _sb(60, U16), "pi": _sb(24, I32), "pj": _sb(24, I32), "pu": _sb(24, U16), "qf": _sb(2, F32),
-    "ia": _sb(24, F32), "il": _sb(24, F32), "ip": _sb(6, F32),
+    "ia": _sb(24, F32), "il": _sb(24, F32), "ip": _sb(8, F32),
     "im": _sb(16, I32), "im2": _sb(16, I32), "c16": _sb(16, F32),
     "ctl": _sb(C, BF), "ctlc": _sb(C, F16), "ctf": _sb(C, BF), "crow": _sb(C, BF), "pre": _sb(C, BF), "half": _sb(4, F32),
     "gr": _sb(72, F32), "gl": _sb(2, U16),
-    "k12": _sb(96, F32), "k32": _sb(128, F32), "cil": _sb(24, F32),
+    "k12": _sb(48, F32), "nt": _sb(512, BF), "ntc": _sb(128, Q4), "nts": _sb(128, U8), "cil": _sb(24, F32),
     "zero": _sb(512, BF), "ramp": _sb(C, BF), "ow": _sb(W, F32),
     "qxc": _sb(C, Q4), "qxs": _sb(C, U8), "pt": _sb(C, F32),
     "tri2": _sb(4 * 192, BF), "tri3": _sb(4 * 256, BF), "tri4": _sb(4 * 320, BF), "tri5": _sb(4 * 384, BF),
     "sj": _sb((12 - VB) * H, BF), "sg": _sb(8 * 128, BF), "rho": _sb(24, F32),
     "qfc": _sb(896, Q4), "qfs": _sb(896, U8), "cs0": _sb(128, BF), "cs1": _sb(128, BF), "cst": _sb(512, BF), "csc": _sb(128, Q4), "css": _sb(128, U8),
     "qt": _sb(C, F32), "kr": _sb(24, F32), "kk": _sb(24, F32), "fa": _sb(48, F32), "aa": _sb(48, F32),
-    "st": _sb(96, F32), "sw": _sb(128, F32), "su": _sb(128, F32), "sx": _sb(128, F32), "tz": _sb(4, F32), "ty": _sb(2, BF),
+    "st": _sb(96, F32), "sw": _sb(128, F32), "su": _sb(128, F32), "sx": _sb(4, F32), "tz": _sb(30, F32), "ty": _sb(2, BF),
     "k1l": _sb(C, BF), "k1h": _sb(C, BF), "kyl": _sb(C, BF), "kyh": _sb(C, BF),
     "gw": _sb(C + 16, BF), "al": _sb(C, BF), "ah": _sb(C + 16, BF), "gh": _sb(C, BF), "capl": _sb(C, BF), "caph": _sb(C, BF),
     "cnl": _sb(C + 16, BF), "cnh": _sb(C + 16, BF),
-    "dl": _sb(4, F32), "sgl": _sb(4 * C, BF), "sm": _sb(4 * H, BF), "lo": _sb(4, U16), "bt": _sb(512, BF), "xp": _sb(4 * W, BF),
+    "dl": _sb(4, F32), "sgl": _sb(4 * C, BF), "sm": _sb(2 * H, BF), "lo": _sb(4, U16), "bt": _sb(512, BF), "xp": _sb(4 * W, BF),
     "qbc": _sb(R * 128, Q4), "qbs": _sb(R * 128, U8), "landc": _sb(320, Q4), "lands": _sb(320, U8),
     "lsend": _sb(K, BF), "lland": _sb(K, BF),
     "cva": _sb(C, BF), "cvb": _sb(C, BF), "cvc": _sb(C, F16),
     "t1": _sb(24, F32), "lm": _sb(24, F32), "wm": _sb(24, F32), "ou": _sb(24, U16),
-    "dat": _sb(C, BF), "ew": _sb(1088, BF), "en": _sb(C + 32, BF), "et": _sb(2 * C + 32, BF), "em": _sb(50, F32), "eo": _sb(32, U16),
+    "dat": _sb(C, BF), "ew": _sb(1088, BF), "en": _sb(C + 32, BF), "et": _sb(896, BF), "em": _sb(64, F32), "eo": _sb(32, U16),
     "ta": _sb(4 * 208, BF), "tb": _sb(4 * 196, BF),
     "qtc": _sb(4 * H, Q4), "qts": _sb(4 * H, U8),
     "ysb": _sb(C, F32), "olb": _sb(C, F32),
@@ -158,6 +159,9 @@ def rank_program(g, core, T, topo):
     def scan(out, d0, d1, init, o0, o1, rd, wr, n):
         add([vec(lambda: V.tensor_tensor_scan(out, d0, d1, init, o0, o1), n)], rd, wr)
 
+    def most(out, in_, o, rd, wr, n):
+        add([vec(lambda: V.tensor_reduce(out, in_, AxisListType.X, o), n)], rd, wr)
+
     def flip(out, in_, rd, wr, n):
         add([vec(lambda: V.transpose(out, in_), n)], rd, wr)
 
@@ -202,7 +206,7 @@ def rank_program(g, core, T, topo):
         add([(e, lambda: queue[e].dma_start(out, in_), d)], rd, wr, lat, "dma")
 
     def send(out, in_, sem, total, rd, wr):
-        add([("q", lambda: g.remote_dma(out, in_, T.sem[sem], T.sem.sent, pid, rid, mask), 100)], rd, wr, SEND, (sem, total))
+        add([("q", lambda: g.remote_dma(out, in_, T.sem[sem], T.sem.sent, pid, rid, mask), 100)], rd, wr, SEND + 1500 * (now[0] == 0), (sem, total))
 
     def xkeys(r, halves=(0, 1)):
         return ["x%d_%d_%d" % (r, h, b) for h in halves for b in range(4)]
@@ -239,6 +243,7 @@ def rank_program(g, core, T, topo):
     for a in range(4):
         move(T.cst[32 * a:32 * a + 32, 128 * a:128 * a + 128], T.cs1[32 * a:32 * a + 32, :], ["cs1"], [cstk[a]], 128, 64)
     quant(T.csc[:], T.css[:], T.cst[:], cstk, ["cs"], 128)
+    fill(T.nt[:], 0.0, ["nt0", "nt1", "nt2", "nt3"], 256)
     iota(T.qt[:, 320:C], [[0, C - 320]], 0, 0, ["qtz"])
     iota(T.cnl[:, 0:16], [[0, 16]], -K, 0, ["cnl"])
     iota(T.cnh[:, 0:16], [[0, 16]], 256 - K, 0, ["cnh"])
@@ -246,12 +251,11 @@ def rank_program(g, core, T, topo):
     iota(T.ah[:, C:C + 16], [[0, 16]], 0, 0, ["ahz"])
     iota(T.bt[:, 4 * K:512], [[0, 512 - 4 * K]], 0, 0, ["btz"])
     iota(T.ramp[:], [[1, C]], -192, 0, ["ramp"])
-    iota(T.gr[:, 0:16], [[2, 8], [26, 2]], 0, 0, ["gr0"])
-    iota(T.gr[:, 16:32], [[2, 8], [-24, 2]], 25, 0, ["gr1"])
-    iota(T.gr[:, 64:66], [[16, 2]], 0, 0, ["gk"])
+    iota(T.gr[:, 0:16], [[2, 8], [16, 2]], 0, 0, ["gr0"])
+    iota(T.gr[:, 16:32], [[2, 8], [-14, 2]], 15, 0, ["gr1"])
+    iota(T.et[:, 640:672], [[0, 32]], 0, 0, ["etz"])
     flip(T.gr[:, 32:64], T.gr[:, 0:32], ["gr0", "gr1"], ["gq"], 32)
-    tt(T.gr[:, 68:70], T.gr[:, 32:34], T.gr[:, 64:66], A.add, ["gq", "gk"], ["gs"], 4)
-    ts(T.gl[:], T.gr[:, 68:70], 49.0, None, A.min, None, ["gs"], ["gl"], 4)
+    ts(T.gl[:], T.gr[:, 32:34], 27.0, None, A.min, None, ["gq"], ["gl"], 4)
     iota(T.en[:, 0:16], [[0, 16]], 0, 0, ["enz0"])
     iota(T.en[:, C + 16:C + 32], [[0, 16]], 0, 0, ["enz1"])
     keep(T.gt[:], T.ones[:], [[1, 516]], -3, -4, A.is_equal, ["ones"], ["gt"], 516)
@@ -259,8 +263,7 @@ def rank_program(g, core, T, topo):
         quant(T.ec[:, 128 * b:128 * b + 128], T.es[:, 128 * b:128 * b + 128], T.gt[:, 3 - b:515 - b], ["gt"], ["e%d" % b], 128)
     iota(T.ow[:, 0:C], [[1, C]], 0, 0, ["ow0"])
     for i in range(2):
-        keep(T.k12[:, 48 * i:48 * i + 48], T.zero[:, 0:48], [[0, 4], [1, 12]], 0, 0, A.is_gt, ["zero"], ["k12%d" % i], 48, 8.0 * i - 4.0)
-        keep(T.k32[:, 64 * i:64 * i + 64], T.zero[:, 0:64], [[0, 2], [1, 32]], 0, 0, A.is_gt, ["zero"], ["k32%d" % i], 64, 8.0 * i - 4.0)
+        keep(T.k12[:, 24 * i:24 * i + 24], T.zero[:, 0:24], [[0, 2], [1, 12]], 0, 0, A.is_gt, ["zero"], ["k12%d" % i], 24, 8.0 * i - 4.0)
     ts(T.pj[:], T.pi[:], 15, None, A.bitwise_and, None, ["pi"], ["pj"], 24)
     quant(T.landc[:, 64:192], T.lands[:, 64:192], T.zero[:], ["zero"], ["landz"], 128)
     ts(T.im2[:], T.im[:], 15, None, A.bitwise_and, None, ["im"], ["im2"], 16)
@@ -270,9 +273,13 @@ def rank_program(g, core, T, topo):
     line(T.il[:], T.ia[:], 1.0, T.qf[:, 0:1], ["ia", "qf"], ["il"], 24)
     quant(T.quc[:], T.qus[:], T.ut[:], ["ut"], ["qu"], 128)
     quant(T.qvc[:], T.qvs[:], T.vt[:], ["vt"], ["qv"], 128)
-    act(T.pus[:], T.qus[:].indirect(T.cu[:, 0:24]), F.Copy, ["qu", "cu0"], ["pus"], PICK * C)
-    cp(T.puc[:].bitcast(dt.uint32), T.quc[:].bitcast(dt.uint32).indirect(T.cu[:, 0:24]), ["qu", "cu0"], ["puc"], PICK * C)
-    line(T.ip[:, 0:4], T.il[:, 0:4], 1.0, 0.5 - K, ["il"], ["ip"], 4)
+    for j in range(3):
+        act(T.pus[:, 128 * j:128 * j + 128], T.qus[:].indirect(T.cu[:, 8 * j:8 * j + 8]), F.Copy, ["qu", "cu0"], ["pus%d" % j], PICK * 128)
+        cp(T.puc[:, 128 * j:128 * j + 128].bitcast(dt.uint32), T.quc[:].bitcast(dt.uint32).indirect(T.cu[:, 8 * j:8 * j + 8]), ["qu", "cu0"], ["puc%d" % j], PICK * 128)
+    line(T.ip[:, 0:4], T.il[:, 0:4], 2.0, 1.0 - 2 * K, ["il"], ["ip"], 4)
+    line(T.ip[:, 5:6], T.il[:, 3:4], 2.0, 2.0 - 2 * K, ["il"], ["iq0"], 1)
+    line(T.ip[:, 6:7], T.il[:, 3:4], 2.0, -2.0 * K, ["il"], ["iq1"], 1)
+    line(T.ip[:, 7:8], T.il[:, 3:4], -2.0 * H, H * (2.0 * K - 1), ["il"], ["iq2"], 1)
     line(T.ip[:, 4:5], T.c16[:, 15:16], -1.0, float(W), ["c16"], ["cc0"], 1)
     act(T.half[:, 0:1], T.qf[:, 0:1], F.Sign, ["qf"], ["hf0"], 1, bias=-7.5)
     line(T.half[:, 1:2], T.half[:, 0:1], -256.0, 0.0, ["hf0"], ["hf1"], 1)
@@ -280,14 +287,14 @@ def rank_program(g, core, T, topo):
     line(T.half[:, 3:4], T.half[:, 0:1], 512.0, -512.0, ["hf0"], ["hf3"], 1)
     move(T.ctl[:], T.c16[:].indirect(T.pu[:]), ["c16", "pu"], ["ctl"], PICK * C)
     move(T.ctlc[:], T.ctl[:], ["ctl"], ["ctlc"], C, H, "v")
-    line(T.cil[:], T.il[:], 1.0, float(W), ["il"], ["cil"], 24)
+    ts(T.ctlc[:, 15:C:16], T.il[:], float(W), None, A.add, None, ["il"], ["ctlc"], 24)
     ts(T.crow[:], T.ramp[:], T.half[:, 2:3], None, A.max, None, ["ramp", "hf2"], ["crow"], H)
     line(T.ctf[:], T.zero[:, 0:C], 1.0, T.half[:, 3:4], ["zero", "hf3"], ["ctf"], C, H)
     line(T.pre[:], T.zero[:, 0:C], 1.0, T.half[:, 1:2], ["zero", "hf1"], ["pre"], C, H)
     Z = T.zero[:, 0:C]
 
     def score(bank, j, c0, c1, rd):
-        mm(bank, c1 - c0, T.puc[:, 128 * j:128 * j + 128], T.pus[:, 128 * j:128 * j + 128], T.qxc[:, c0:c1], T.qxs[:, c0:c1], True, True, ["puc", "pus"] + rd)
+        mm(bank, c1 - c0, T.puc[:, 128 * j:128 * j + 128], T.pus[:, 128 * j:128 * j + 128], T.qxc[:, c0:c1], T.qxs[:, c0:c1], True, True, ["puc%d" % j, "pus%d" % j] + rd)
 
     def turn(bank, h):
         flip(T.pt[:, H * h:H * h + H], T["ps%d" % bank][:, 0:H], ["ps%d" % bank], ["pt%d" % h], H)
@@ -311,6 +318,7 @@ def rank_program(g, core, T, topo):
         turn(0, 0)
         score(3, 0, H, C, ["qx1"])
         score(4, 2, 0, C, ["qx0", "qx1"])
+        score(7, 1, 0, C, ["qx0", "qx1"])
         turn(3, 1)
 
         def row(e, b):
@@ -319,7 +327,7 @@ def rank_program(g, core, T, topo):
             return T["tri%d" % (b // 2)][:, 2 * e + b % 2:4 * _reach(b):4], "tr%d_%d" % (b, e)
 
         def sgn(e, b):
-            bank = "ps1" if e else "ps2"
+            bank = "ps1" if e else "ps7"
             out, key = row(e, b)
             act(out, T[bank][:, 0:_reach(b)], F.Sign, [bank, "pt%d" % (b // 6)], [key, "rho%d" % (12 * e + b)], _reach(b),
                 bias=T.pt[:, 32 * b + 16 * e:32 * b + 16 * e + 1], scale=-1.0, accum_out=T.rho[:, 12 * e + b:12 * e + b + 1])
@@ -346,15 +354,13 @@ def rank_program(g, core, T, topo):
             else:
                 cmp(b)
                 cnt(b)
-            if b == 5:
-                score(2, 1, 0, C, ["qx0", "qx1"])
         for b in range(12):
             sgn(0, b)
         for k in (5, 4, 3, 2):
             cols(k)
         for t in range(4):
             move(T.xp[:, W * t:W * t + C], X[:, t:4 * C:4], xk, ["xp%d" % t], C, H, "qs")
-        move(T.ew[:, 256:256 + C], T.pre[:], ["pre"], ["ew"], C, H, "qs")
+        move(T.ew[:, 256:256 + C], T.pre[:], ["pre"], ["ew0", "ew1"], C, H, "qs")
 
         line(T.kr[:, 12:12 + VB], T.rho[:, 12:12 + VB], -UNIT, (2 * C - 32 * VB) * UNIT, ["rho%d" % i for i in range(12, 12 + VB)], ["kr1"], 6)
         line(T.kr[:, 12 + VB:24], T.sj[:, H - 1:(12 - VB) * H:H], -UNIT, C * UNIT, ["sj%d" % b for b in range(VB, 12)], ["kr2"], 6)
@@ -365,67 +371,79 @@ def rank_program(g, core, T, topo):
         kkk = ["kk0", "kk1"]
         cuts = (2 * (C - K), 2 * K)
         for i in range(2):
+            for e in range(2):
+                ts(T.nt[:, 48 * i + 2 * e:48 * i + 48:4], T.kk[:, 12 * e:12 * e + 12], (cuts[i] + 0.5) * UNIT, None, A.is_gt, None, ["kk%d" % e], ["nt%d" % (2 * i + e)], 12)
+        quant(T.ntc[:], T.nts[:], T.nt[:], ["nt0", "nt1", "nt2", "nt3"], ["nq"], 128)
+        mm(6, 128, T.csc[:], T.css[:], T.ntc[:], T.nts[:], True, True, ["cs", "nq"])
+        for i in range(2):
             ts(T.fa[:, 24 * i:24 * i + 24], T.kk[:], (cuts[i] + 0.5) * UNIT, cuts[i] * UNIT, A.is_gt, A.add, kkk, ["fa%d" % i], 24)
             tt(T.aa[:, 24 * i:24 * i + 24], T.kk[:], T.fa[:, 24 * i:24 * i + 24], A.subtract, kkk + ["fa%d" % i], ["aa%d" % i], 24)
-        for i, o in enumerate((A.max, A.min)):
-            scan(T.st[:, 48 * i:48 * i + 48], T.k12[:, 48 * i:48 * i + 48], T.aa[:], 0.0, A.add, o, ["k12%d" % i, "aa0", "aa1"], ["st%d" % i], 48)
-        move(T.sw[:], T.st[:].indirect(T.cu[:, 48:56]), ["st0", "st1", "cu"], ["sw"], PICK * 128)
-        flip(T.su[:], T.sw[:], ["sw"], ["su"], 128)
-        for i, o in enumerate((A.max, A.min)):
-            scan(T.sx[:, 64 * i:64 * i + 64], T.k32[:, 64 * i:64 * i + 64], T.su[:, 64 * i:64 * i + 64], 0.0, A.add, o, ["k32%d" % i, "su"], ["sx%d" % i], 64)
-        for i, n in ((0, C - 2 * K + 1.0), (1, 2 * K - C - 1.0)):
+            for j, o in enumerate((A.max, A.min)):
+                scan(T.st[:, 48 * i + 24 * j:48 * i + 24 * j + 24], T.k12[:, 24 * j:24 * j + 24], T.aa[:, 24 * i:24 * i + 24], 0.0, A.add, o, ["k12%d" % j, "aa%d" % i], ["st%d" % (2 * i + j)], 24)
+            move(T.sw[:, 64 * i:64 * i + 64], T.st[:, 48 * i:48 * i + 48].indirect(T.cu[:, 48:52]), ["st%d" % (2 * i), "st%d" % (2 * i + 1), "cu"], ["sw%d" % i], PICK * 64)
+            flip(T.su[:, 64 * i:64 * i + 64], T.sw[:, 64 * i:64 * i + 64], ["sw%d" % i], ["su%d" % i], 64)
+            for j, o in enumerate((A.max, A.min)):
+                most(T.sx[:, 2 * i + j:2 * i + j + 1], T.su[:, 64 * i + 32 * j:64 * i + 32 * j + 32], o, ["su%d" % i], ["sx%d" % (2 * i + j)], 32)
+        for i, n in ((0, (0.5 - K) * UNIT), (1, (K - C - 0.5) * UNIT)):
             k1, ky = (T.k1l, T.k1h)[i], (T.kyl, T.kyh)[i]
             line(k1[:], T.kk[:].indirect(T.cu[:, 24:48]), 1.0, -cuts[i] * UNIT, kkk + ["cu"], ["k1%d" % i], PICK * C)
             flip(ky[:], k1[:], ["k1%d" % i], ["ky%d" % i], H)
-            act(T.sgl[:, C * i:C * i + C], ky[:], F.Sign, ["ky%d" % i], ["nb%d" % i, "sgl%d" % i], C, bias=-0.5 * UNIT, accum_out=T.tz[:, 2 + i:3 + i])
+            act(T.tz[:, 4 + 12 * i:16 + 12 * i], T.ps6[:, 12 * i:12 * i + 12], F.Identity, ["ps6"], ["nb%d" % i], 12, accum_out=T.tz[:, 2 + i:3 + i])
             act(T.tz[:, i:i + 1], T.tz[:, 2 + i:3 + i], F.Sign, ["nb%d" % i], ["tz%d" % i], 1, bias=n)
-            ts(T.ty[:, i:i + 1], T.sx[:, 95 + 32 * i:96 + 32 * i], T.tz[:, i:i + 1], T.sx[:, 31 + 32 * i:32 + 32 * i], A.add, A.max, ["tz%d" % i, "sx0", "sx1"], ["ty%d" % i], 1)
+            ts(T.ty[:, i:i + 1], T.sx[:, 2 * i + 1:2 * i + 2], T.tz[:, i:i + 1], T.sx[:, 2 * i:2 * i + 1], A.add, A.max, ["tz%d" % i, "sx%d" % (2 * i), "sx%d" % (2 * i + 1)], ["ty%d" % i], 1)
 
         tl, th = T.ty[:, 0:1], T.ty[:, 1:2]
+        act(T.tz[:, 28:29], th, F.Identity, ["ty1"], ["tq"], 1, bias=0.25 * UNIT)
         CLi, CLe, CHi, CHe = T.cnl[:, 16:C + 16], T.cnl[:, 15:C + 15], T.cnh[:, 16:C + 16], T.cnh[:, 15:C + 15]
         ts(T.gw[:, 0:C], T.kyl[:], tl, None, A.is_ge, None, ["ky0", "ty0"], ["gw"], H)
         ts(T.al[:], T.kyl[:], tl, None, A.is_gt, None, ["ky0", "ty0"], ["al"], H)
         scan(T.capl[:, ::-1], Z, T.gw[:, C:0:-1], 0.0, A.add, A.subtract, ["zero", "gw", "gwz"], ["capl"], H)
         scan(CLi, T.al[:], T.capl[:], -float(K), A.add, A.max, ["al", "capl"], ["cnl"], H)
         ts(T.ah[:, 0:C], T.kyh[:], th, None, A.is_lt, None, ["ky1", "ty1"], ["ah"], H)
-        ts(T.gh[:], T.kyh[:], th, None, A.is_le, None, ["ky1", "ty1"], ["gh"], H)
+        act(T.k1l[:], T.kyh[:], F.Sign, ["ky1", "tq"], ["gi", "k10"], C, bias=T.tz[:, 28:29], scale=-1.0)
+        act(T.gh[:], T.k1l[:], F.Relu, ["gi", "k10"], ["gh"], C)
         scan(T.caph[:, ::-1], Z, T.ah[:, C:0:-1], 256.0, A.add, A.subtract, ["zero", "ah", "ahz"], ["caph"], H)
         scan(CHi, T.gh[:], T.caph[:], 256.0 - K, A.add, A.min, ["gh", "caph"], ["cnh"], H)
 
+        scan(T.sm[:, 0:H], T.cnl[:, 16:C + 16:2], T.cnl[:, 17:C + 16:2], -256.0, A.max, A.add, ["cnl"], ["zz"], H // 2)
         for k in range(4 - NV):
-            act(T.sgl[:, C * k:C * k + C], CLi, F.Sign, ["cnl", "ip"], ["sgl%d" % k, "dl%d" % k], C, bias=T.ip[:, k:k + 1], scale=-1.0, accum_out=T.dl[:, k:k + 1])
-        ts(T.lo[:, 0:4 - NV], T.dl[:, 0:4 - NV], 0.5, 192.0, A.mult, A.add, ["dl%d" % k for k in range(4 - NV)], ["lo"], 4)
-        for k in range(4 - NV, 4):
-            ts(T.sgl[:, C * k:C * k + C], CLi, T.ip[:, k:k + 1], None, A.is_lt, None, ["cnl", "ip"], ["sgl%d" % k], H)
-            scan(T.sm[:, H * k:H * k + H], T.sgl[:, C * k:C * k + H], T.sgl[:, C * k + H:C * k + C], -192.0, A.add, A.add, ["sgl%d" % k], ["sm%d" % k], H // 2)
+            act(T.sgl[:, C * k:C * k + H], T.sm[:, 0:H], F.Sign, ["zz", "ip"], ["sgl%d" % k, "dl%d" % k], H, bias=T.ip[:, k:k + 1], scale=-1.0, accum_out=T.dl[:, k:k + 1])
+        ts(T.lo[:, 0:4 - NV], T.dl[:, 0:4 - NV], float(H), None, A.add, None, ["dl%d" % k for k in range(4 - NV)], ["lo"], 4)
         if NV:
-            ts(T.lo[:, 4 - NV:4], T.sm[:, H * (5 - NV) - 1:4 * H:H], 192.0, None, A.add, None, ["sm%d" % k for k in range(4 - NV, 4)], ["lo1"], 4)
+            ts(T.sgl[:, 3 * C:3 * C + H], T.sm[:, 0:H], T.ip[:, 5:6], T.ip[:, 6:7], A.min, A.max, ["zz", "iq0", "iq1"], ["sgl3"], H // 2)
+            scan(T.sm[:, H:H + 96], T.sgl[:, 3 * C:3 * C + 96], T.sgl[:, 3 * C + 96:3 * C + H], T.ip[:, 7:8], A.add, A.add, ["sgl3", "iq2"], ["sm3"], H // 4)
+            ts(T.lo[:, 3:4], T.sm[:, H + 95:H + 96], -1.0, float(H), A.mult, A.add, ["sm3"], ["lo1"], 4)
         wrap(T.cva, CLi, T.ctl, 128.0 - K, ["cnl", "ctl"], "cva")
         wrap(T.cvb, CLe, T.ctl, 128.0 - K, ["cnl", "ctl"], "cvb")
         tt(T.t1[:], T.cva[:, 15:C:16], T.cvb[:, 15:C:16], A.is_equal, ["cva", "cvb"], ["t1"], 24)
         line(T.lm[:], T.cvb[:, 15:C:16], 1.0, T.ip[:, 4:5], ["cvb", "cc0"], ["lm"], 24)
         tt(T.wm[:], T.t1[:], T.lm[:], A.mult, ["t1", "lm"], ["wm"], 24)
-        tt(T.ctlc[:, 15:C:16], T.cil[:], T.wm[:], A.subtract, ["cil", "wm", "ctlc"], ["oo"], 24)
-        wrap(T.cvc, CHe, T.ctlc, 384.0 - K, ["cnh", "oo"], "cvc")
-        cp(T.ou[:], T.cvc[:, 15:C:16], ["cvc"], ["ou"], 24)
+        wrap(T.cvc, CHe, T.ctlc, 384.0 - K, ["cnh", "ctlc"], "cvc")
+        tt(T.cil[:], T.cvc[:, 15:C:16], T.wm[:], A.subtract, ["cvc", "wm"], ["oo"], 24)
+        cp(T.ou[:, 0:18], T.cil[:, 0:18], ["oo"], ["ou0"], 18)
+        ts(T.ou[:, 18:24], T.cil[:, 18:24], -480.0, None, A.add, None, ["oo"], ["ou1"], 6)
         scan(T.dat[:], CHe, T.crow[:], -256.0, A.max, A.min, ["cnh", "crow"], ["dat"], H)
         for t in range(4):
             move(T.bt[:, t:4 * K:4], T.xp[:, W * t:W * t + C].indirect(T.lo[:]), ["xp%d" % t, "lo", "lo1"], ["bt%d" % t], PICK * K)
-        quant(T.qbc[:, 128 * r:128 * r + 128], T.qbs[:, 128 * r:128 * r + 128], T.bt[:], btk + ["btz"], ["qb%d" % r], 128)
-        l0 = (0, 192, 256)[r]
-        send(T.landc[:, l0:l0 + K].bitcast(dt.uint8), T.qbc[:, 128 * r:128 * r + K].bitcast(dt.uint8), "arr%d" % r, 2 * neng, ["qb%d" % r], ["lc%d" % r])
-        send(T.lands[:, l0:l0 + K], T.qbs[:, 128 * r:128 * r + K], "arr%d" % r, 2 * neng, ["qb%d" % r], ["ls%d" % r])
+        s0, l0 = 128 * r, (0, 192, 256)[r]
+        quant(T.qbc[:, s0:s0 + 128], T.qbs[:, s0:s0 + 128], T.bt[:], btk + ["btz"], ["qb%d" % r], 128)
+        send(T.landc[:, l0:l0 + K].bitcast(dt.uint8), T.qbc[:, s0:s0 + K].bitcast(dt.uint8), "arr%d" % r, 2 * neng, ["qb%d" % r], ["lc%d" % r])
+        send(T.lands[:, l0:l0 + K], T.qbs[:, s0:s0 + K], "arr%d" % r, 2 * neng, ["qb%d" % r], ["ls%d" % r])
         if last:
             move(T.lsend[:], T.ramp[:].indirect(T.lo[:]), ["ramp", "lo", "lo1"], ["lsend"], PICK * K)
-            send(T.lland[:], T.lsend[:], "arrl", neng, ["lsend", "qb%d!" % r], ["lland"])
+            send(T.lland[:], T.lsend[:], "arrl", neng, ["lsend", "lc%d!" % r], ["lland"])
 
-        cp(T.ew[:].indirect(T.ou[:]), T.dat[:], ["ou", "dat"], ["ew"], PUT * C)
-        scan(T.en[:, 16:C + 16], T.ctf[:], T.ew[:, 256:256 + C], -256.0, A.add, A.max, ["ctf", "ew"], ["en"], H)
-        flip(T.et[:, 0:C], T.en[:, 16:C + 16], ["en"], ["et0"], H)
-        flip(T.et[:, C:2 * C + 32], T.en[:], ["en", "enz0", "enz1"], ["et1"], H + 16)
-        tt(T.em[:, 0:24], T.et[:, 0:C:16], T.et[:, 8:C:16], A.min, ["et0"], ["em0"], 24)
-        tt(T.em[:, 24:50], T.et[:, C:2 * C + 32:16], T.et[:, C + 8:2 * C + 32:16], A.min, ["et1"], ["em1"], 26)
-        ts(T.eo[:], T.em[:].indirect(T.gl[:]), 192.0, None, A.add, None, ["em0", "em1", "gl"], ["eo"], PICK * 32)
+        cp(T.ew[:].indirect(T.ou[:, 0:18]), T.dat[:, 0:288], ["ou0", "dat"], ["ew0", "ew1"], PUT * 288)
+        cp(T.ew[:, 480:1088].indirect(T.ou[:, 18:24]), T.dat[:, 288:C], ["ou1", "dat"], ["ew1"], PUT * 96)
+        scan(T.en[:, 16:240], T.ctf[:, 0:224], T.ew[:, 256:480], -256.0, A.add, A.max, ["ctf", "ew0"], ["en0"], 112)
+        scan(T.en[:, 240:C + 16], T.ctf[:, 224:C], T.ew[:, 480:256 + C], T.en[:, 239:240], A.add, A.max, ["ctf", "ew1", "en0"], ["en1"], 80)
+        for h in range(2):
+            o, ek = 448 * h, ["en0"] + ["en1", "enz1"] * h
+            n1, n2 = 224 - 32 * h, 224
+            flip(T.et[:, o:o + n1], T.en[:, 16 + H * h:16 + H * h + n1], ek, ["et%d" % (2 * h)], n1 // 2)
+            flip(T.et[:, o + 224:o + 448], T.en[:, H * h:H * h + n2], ek + ["enz0"], ["et%d" % (2 * h + 1)], n2 // 2)
+            tt(T.em[:, 32 * h:32 * h + 28], T.et[:, o:o + 448:16], T.et[:, o + 8:o + 448:16], A.min, ["et%d" % (2 * h), "et%d" % (2 * h + 1), "etz"], ["em%d" % h], 28)
+            ts(T.eo[:, 16 * h:16 * h + 16], T.em[:, 32 * h:32 * h + 28].indirect(T.gl[:, 0:1]), 192.0, None, A.add, None, ["em%d" % h, "gl"], ["eo%d" % h], PICK * 16)
 
         v0 = (0, 128, 192)[r]
         lk = ["lc%d" % r, "ls%d" % r, "landz"] + (["lc1", "ls1"] if r == 2 else [])
@@ -437,7 +455,7 @@ def rank_program(g, core, T, topo):
             n = 13 - h
             tile = (T.ta, T.tb)[h]
             for t in range(4):
-                move(tile[:, t:64 * n:4], T.xp[:, W * t:W * t + W].indirect(T.eo[:, 12 * h:12 * h + n]), ["xp%d" % t, "xa%d" % t, "eo"], ["t%d_%d" % (h, t)], PICK * 16 * n)
+                move(tile[:, t:64 * n:4], T.xp[:, W * t:W * t + W].indirect(T.eo[:, 16 * h:16 * h + n]), ["xp%d" % t, "xa%d" % t, "eo%d" % h], ["t%d_%d" % (h, t)], PICK * 16 * n)
             if h:
                 move(T.tb[:, 4 * H:4 * H + 4], T.ta[:, 0:4], ["t0_%d" % t for t in range(4)], ["tbw"], 4)
             for rot in range(2):
@@ -455,8 +473,9 @@ def rank_program(g, core, T, topo):
 
     seen.update({"ps0": 4, "ps1": 4, "qx0": 2, "qx1": 2})
     line(T.ow[:, C:W], T.lland[:], 1.0, 576.0, ["lland"], ["ow1"], K)
-    move(T.olb[:], T.ow[:].indirect(T.eo[:, 0:24]), ["ow0", "ow1", "eo"], ["olb"], PICK * C)
-    dma("y", T.ol[:], T.olb[0:128:16, :], ["olb"], [], LOAD)
+    for h in range(2):
+        move(T.olb[:, H * h:H * h + H], T.ow[:].indirect(T.eo[:, 16 * h:16 * h + 12]), ["ow0", "ow1", "eo%d" % h], ["olb%d" % h], PICK * H)
+    dma("y", T.ol[:], T.olb[0:128:16, :], ["olb0", "olb1"], [], LOAD)
     for h in range(2):
         mm(h, H, T.qvc[:], T.qvs[:], T.qxc[:, H * h:H * h + H], T.qxs[:, H * h:H * h + H], True, True, ["qv", "qx%d" % h])
         move(T.ysb[:, H * h:H * h + H], T["ps%d" % h][:, 0:H], ["ps%d" % h], ["y%d" % h], H)
@@ -470,11 +489,14 @@ def rank_program(g, core, T, topo):
     waited = {k: {} for k in queue}
     lastw, readers = {}, {}
     ndma = [0]
+    behind = {}
 
     def wait(e, tok):
         if waited[e].get(tok[0], 0) < tok[1]:
             queue[e].wait_ge(T.sem[tok[0]], tok[1])
             waited[e][tok[0]] = tok[1]
+            for s, n in behind.get(tok, {}).items():
+                waited[e][s] = max(waited[e].get(s, 0), n)
 
     for (e, make, _), (_, rd, wr, _, kind, _, _) in _layout(plan):
         toks = []
@@ -491,7 +513,7 @@ def rank_program(g, core, T, topo):
         need = {}
         for t in toks:
             need[t[0]] = max(need.get(t[0], 0), t[1])
-        for s in need:
+        for s in sorted(need, key=lambda a: -len([b for b in need if behind.get((a, need[a]), {}).get(b, 0) >= need[b]])):
             wait(e, (s, need[s]))
         if kind == "dma":
             s = "d%d" % ndma[0]
@@ -510,6 +532,8 @@ def rank_program(g, core, T, topo):
             count[kind[0]] = kind[1]
             tok = kind
             rd = []
+        if kind is None or kind in ("chain", "dma"):
+            behind[tok] = dict(waited[e])
         for k in rd:
             readers.setdefault(k, []).append(tok)
         for k in wr:
@@ -517,4 +541,4 @@ def rank_program(g, core, T, topo):
             readers[k] = []
 
     for s in count:
-        wait("q", (s, count[s]))
+        g.wait_ge(T.sem[s], count[s])

from concourse.mybir import dt, AluOpType, AxisListType, ActivationFunctionType

A, F = AluOpType, ActivationFunctionType
C, K, R = 384, 64, 3
H = C // 2
W = C + K
UNIT = 2.0 ** -10
Q4, U8, BF, F32, I32, U16, F16 = "float8_e4m3fn_x4", "uint8", "bfloat16", "float32", "int32", "uint16", "float16"
CYC, PICK, PUT, COL, LOAD, SEND, VFIX, SFIX = 0.83, 1.56, 3.8, 0.55, 1200, 2500, 50, 65
VB = 4
NV = 1
ORDER = """+cx0_0a +cx1_0a +cpia +coneka +czeroa ps2a +czpa tr5_1a cahza tr4_1a ccst1a:s +cci0a ps1a sg7a sg4a ccsa ps3a pt1a sj5a +cpja
+ccs0a sg6a xp0a:q +cuta ps4a +cnt0a +clandza +cpua sj4a tr10_1a czqa tr6_1a tr11_1a sg5a ps7a tr6_0a +cqfa tr11_0a tr10_0a tr8_0a tr9_1a
+conesa tr7_1a tr9_0a tr8_1a tr7_0a sj11a qf5a qf4a qf3a sj10a tr4_0a tr5_0a qf2a sg3a sj9a sj7a sg1a sj6a sj8a kr1a:s sg0a cgqa ps5a
ps5b ps5c ps5d qta +ciaa +cila:s ccrowa sg2a +ccst0a kr2a:s kk1a +ciq2a:s kr0a:s kk0a +cci1a +ccs1a ccua nt1a nt3a fa0a nt2a +ccu0a
+cetza nt0a +ck121a cctla:s cgla fa1a aa0a +cqua nqa ps6a aa1a k10a:s k11a:s st0a st1a st3a st2a sw1a:s sw0a:v ky0a su0a +cipa:s cctlca
su1a sx0a nb0a nb1a sx1a ccc0a:s sx2a sx3a +ciq1a:s tz0a ty0a ky1a +chf0a +ccst3a:s +cima tz1a ty1a gwa +cgta ala capla cprea:s +chf2a:s
aha cnla capha +cenz1a zza cvaa +cqx0a +cqtza sgl3a cvba sm3a cctlcb +cwpa +cpus0a +cgr0a cow0a tqa gia gha +ccst2a:s +cpus2a sgl0a cnha
sgl1a t1a sgl2a +cci3a lo1a xp3a:q loa cvca lma:s wma +cci2a bt1a:s cwqa bt2a:v +ccnla +ck120a bt0a:v ooa bt3a:s qba lsa +cbtza +ciq0a:s
chf3a:s +cpuc0a ce3a ou0a cvta lsenda:s ce0a data cctfa:s +chf1a:s ce2a ew0b ce1a ou1a en0a ew1a et0a et1a en1a em0a et2a et3a eo0a lca
ps4b xa0a:s ps7b xa3a:s +ccnha +ccst0b:s ps5e xa1a:v em1a ps6b llanda xa2a:s t0_0a:v eo1a t0_3a:s +cpuc1a t0_1a:s t1_1a:s t1_3a:s +cgr1a
+cpus1a t0_2a:v +cenz0a qt0a ps2b ps1b qt1a ps1c +crampa ps2c t1_2a:s tbwa:s x0_2a:s +cim2a ps0b ps3b ps3c ow1a:s cqva x0_3a:s t1_0a:v
qt2a qt3a x0_1a:v ps0c x0_0a:v +ew0a:q ps7c ps4c ps4d +cpuc2a ps6c ps6d ps7d ps5f ps5g olb1a:s qx0a ps0e +ps0a x1_2a:v +cc16a qx0c +cgwza
+pt0a x1_0a:s olb0a:v x1_3a:s +cqx1a x1_1a:s +xp2a:q +xp1a:q qx1a qx0e ps1e olb0b y0a:s y0b qx1c qx0f qx0g qx0d y1a:v y1b"""


def _sb(n, d):
    return ("sbuf", [128, n], d)


SCRATCH = {
    "ut": _sb(512, BF), "vt": _sb(512, BF),
    "quc": _sb(128, Q4), "qus": _sb(128, U8), "puc": _sb(384, Q4), "pus": _sb(384, U8),
    "qvc": _sb(128, Q4), "qvs": _sb(128, U8),
    "wq": _sb(512, Q4), "wp": _sb(512, U8), "zq": _sb(512, Q4), "zp": _sb(512, U8),
    "gt": _sb(516, BF), "ones": _sb(516, BF), "onek": _sb(128, BF), "ec": _sb(512, Q4), "es": _sb(512, U8),
    "ci": _sb(60, I32), "cu": _sb(60, U16), "pi": _sb(24, I32), "pj": _sb(24, I32), "pu": _sb(24, U16), "qf": _sb(2, F32),
    "ia": _sb(24, F32), "il": _sb(24, F32), "ip": _sb(8, F32),
    "im": _sb(16, I32), "im2": _sb(16, I32), "c16": _sb(16, F32),
    "ctl": _sb(C, BF), "ctlc": _sb(C, F16), "ctf": _sb(C, BF), "crow": _sb(C, BF), "pre": _sb(C, BF), "half": _sb(4, F32),
    "gr": _sb(72, F32), "gl": _sb(2, U16),
    "k12": _sb(48, F32), "nt": _sb(512, BF), "ntc": _sb(128, Q4), "nts": _sb(128, U8), "cil": _sb(24, F32),
    "zero": _sb(512, BF), "ramp": _sb(C, BF), "ow": _sb(W, F32),
    "qxc": _sb(C, Q4), "qxs": _sb(C, U8), "pt": _sb(C, F32),
    "tri2": _sb(4 * 192, BF), "tri3": _sb(4 * 256, BF), "tri4": _sb(4 * 320, BF), "tri5": _sb(4 * 384, BF),
    "sj": _sb((12 - VB) * H, BF), "sg": _sb(8 * 128, BF), "rho": _sb(24, F32),
    "qfc": _sb(896, Q4), "qfs": _sb(896, U8), "cs0": _sb(128, BF), "cs1": _sb(128, BF), "cst": _sb(512, BF), "csc": _sb(128, Q4), "css": _sb(128, U8),
    "qt": _sb(C, F32), "kr": _sb(24, F32), "kk": _sb(24, F32), "fa": _sb(48, F32), "aa": _sb(48, F32),
    "st": _sb(96, F32), "sw": _sb(128, F32), "su": _sb(128, F32), "sx": _sb(4, F32), "tz": _sb(30, F32), "ty": _sb(2, BF),
    "k1l": _sb(C, BF), "k1h": _sb(C, BF), "kyl": _sb(C, BF), "kyh": _sb(C, BF),
    "gw": _sb(C + 16, BF), "al": _sb(C, BF), "ah": _sb(C + 16, BF), "gh": _sb(C, BF), "capl": _sb(C, BF), "caph": _sb(C, BF),
    "cnl": _sb(C + 16, BF), "cnh": _sb(C + 16, BF),
    "dl": _sb(4, F32), "sgl": _sb(4 * C, BF), "sm": _sb(2 * H, BF), "lo": _sb(4, U16), "bt": _sb(512, BF), "xp": _sb(4 * W, BF),
    "qbc": _sb(R * 128, Q4), "qbs": _sb(R * 128, U8), "landc": _sb(320, Q4), "lands": _sb(320, U8),
    "lsend": _sb(K, BF), "lland": _sb(K, BF),
    "cva": _sb(C, BF), "cvb": _sb(C, BF), "cvc": _sb(C, F16),
    "t1": _sb(24, F32), "lm": _sb(24, F32), "wm": _sb(24, F32), "ou": _sb(24, U16),
    "dat": _sb(C, BF), "ew": _sb(1088, BF), "en": _sb(C + 32, BF), "et": _sb(896, BF), "em": _sb(64, F32), "eo": _sb(32, U16),
    "ta": _sb(4 * 208, BF), "tb": _sb(4 * 196, BF),
    "qtc": _sb(4 * H, Q4), "qts": _sb(4 * H, U8),
    "ysb": _sb(C, F32), "olb": _sb(C, F32),
}
for _r in range(R + 1):
    SCRATCH["xw%d" % _r] = _sb(4 * C, BF)
for _b in range(8):
    SCRATCH["ps%d" % _b] = ("psum", [128, 512], F32)

_NDMA = 17
SEMAPHORES = ["sv", "ss", "sp", "sq", "sent", "arr0", "arr1", "arr2", "arrl"] + ["d%d" % _i for _i in range(_NDMA)]


def _reach(b):
    return max(128, 64 * (b // 2 + 1))


def _preds(plan):
    pred = [set() for _ in plan]
    lastw, readers = {}, {}
    for i, p in enumerate(plan):
        rd, wr = [k.rstrip("!") for k in p[1]], p[2]
        for k in rd:
            if k in lastw:
                pred[i].add(lastw[k])
        for k in wr:
            pred[i].update(readers.get(k, []))
            if k in lastw:
                pred[i].add(lastw[k])
        for k in rd:
            readers.setdefault(k, []).append(i)
        for k in wr:
            lastw[k] = i
            readers[k] = []
        pred[i].discard(i)
    return pred


def _layout(plan):
    words = ORDER.split()
    at = {w.strip("+").split(":")[0]: (i - len(words) * (w[0] == "+"), w.partition(":")[2]) for i, w in enumerate(words)}
    pred = _preds(plan)
    succ, left = [[] for _ in plan], [len(p) for p in pred]
    for i, p in enumerate(pred):
        for j in p:
            succ[j].append(i)
    ready, out = [i for i in range(len(plan)) if not left[i]], []
    while ready:
        i = min(ready, key=lambda j: (plan[j][6] * len(words) + at[plan[j][5]][0], j))
        ready.remove(i)
        out.append(([a for a in plan[i][0] if a[0] == (at[plan[i][5]][1] or a[0])][0], plan[i]))
        for j in succ[i]:
            left[j] -= 1
            if not left[j]:
                ready.append(j)
    return out


def rank_program(g, core, T, topo):
    rank = T.rank_of(core)
    if rank is None:
        return
    nxt = T.cores[(rank + 1) % len(T.cores)]
    rid, pid = topo.addr(nxt)[0], topo.addr(nxt)[1]
    mask = topo.mask(core, nxt)
    neng = len(topo.engines(core, nxt))
    V, S, P = g.vector, g.scalar, g.tensor
    queue = {"v": V, "s": S, "p": P, "q": g, "y": g.sync}
    plan, seen, now = [], {}, [0]

    def add(alts, rd, wr, lat=0, kind=None):
        name = (wr + rd)[0]
        if name[0] == "x" and "_" in name:
            name = "x" + name[3:]
        elif name[:2] in ("qb", "lc", "ls") and len(name) == 3:
            name = name[:2]
        seen[name] = seen.get(name, 0) + 1
        plan.append((alts, rd, wr, lat, kind, ("" if "on" in seen else "c") + name + "abcdefgh"[seen[name] - 1], now[0]))

    def vec(make, n):
        return ("v", make, VFIX + CYC * n)

    def sca(make, n):
        return ("s", make, SFIX + CYC * n)

    def pool(make, n):
        return ("q", make, 170 + 2 * CYC * n)

    def ts(out, in0, s1, s2, o0, o1, rd, wr, n):
        if o1 is None:
            add([vec(lambda: V.tensor_scalar(out, in0, s1, None, o0), n)], rd, wr)
        else:
            add([vec(lambda: V.tensor_scalar(out, in0, s1, s2, o0, o1), n)], rd, wr)

    def tt(out, a, b, o, rd, wr, n):
        add([vec(lambda: V.tensor_tensor(out, a, b, o), 2 * n)], rd, wr)

    def cp(out, in_, rd, wr, n):
        add([vec(lambda: V.tensor_copy(out, in_), n)], rd, wr)

    def scan(out, d0, d1, init, o0, o1, rd, wr, n):
        add([vec(lambda: V.tensor_tensor_scan(out, d0, d1, init, o0, o1), n)], rd, wr)

    def most(out, in_, o, rd, wr, n):
        add([vec(lambda: V.tensor_reduce(out, in_, AxisListType.X, o), n)], rd, wr)

    def flip(out, in_, rd, wr, n):
        add([vec(lambda: V.transpose(out, in_), n)], rd, wr)

    def quant(oc, osc, in_, rd, wr, n):
        add([("v", lambda: V.quantize_mx(oc, osc, in_), 12 + 1.06 * CYC * n)], rd, wr)

    def act(out, in_, func, rd, wr, n, **kw):
        add([sca(lambda: S.activation(out, in_, func, **kw), n + (24 if "accum_out" in kw else 0))], rd, wr)

    def move(out, in_, rd, wr, n, nv=None, on="sv"):
        alts = {"s": sca(lambda: S.activation(out, in_, F.Copy), n), "v": vec(lambda: V.tensor_copy(out, in_), nv or n),
                "q": pool(lambda: g.affine_select(out, in_, [[0, n]], A.is_ge, 0.0, 0, 0), n)}
        add([alts[e] for e in on], rd, wr)

    def line(out, in_, scale, bias, rd, wr, n, nv=None, on="sv"):
        if isinstance(bias, float) and bias == 0.0:
            alts = {"s": sca(lambda: S.activation(out, in_, F.Copy, scale=scale), n), "v": vec(lambda: V.tensor_scalar(out, in_, scale, None, A.mult), nv or n)}
        else:
            alts = {"s": sca(lambda: S.activation(out, in_, F.Identity, bias=bias, scale=scale), n),
                    "v": vec(lambda: V.tensor_scalar(out, in_, scale, bias, A.mult, A.add), nv or n)}
        add([alts[e] for e in on], rd, wr)

    def mm(bank, n, lc, ls, rc, rs, start, stop, rd):
        add([("p", lambda: P.matmul_mx(T["ps%d" % bank][:, 0:n], lc, ls, rc, rs, start, stop), 20 + COL * (n + 16))], rd, ["ps%d" % bank], 0, None if start else "chain")

    def iota(out, pat, base, cm, wr, fl=True):
        n = 1
        for p in pat:
            n *= p[1]
        if fl:
            add([pool(lambda: g.iota(out, pat, base, cm, allow_small_or_imprecise_dtypes=True), n)], [], wr)
        else:
            add([pool(lambda: g.iota(out, pat, base, cm), n)], [], wr)

    def keep(out, in_, pat, base, cm, o, rd, wr, n, other=0.0):
        add([pool(lambda: g.affine_select(out, in_, pat, o, other, base, cm), n)], rd, wr)

    def fill(ap, c, wr, n):
        add([vec(lambda: V.memset(ap, c), n)], [], wr)

    def dma(e, out, in_, rd, wr, lat, d=60):
        add([(e, lambda: queue[e].dma_start(out, in_), d)], rd, wr, lat, "dma")

    def send(out, in_, sem, total, rd, wr):
        add([("q", lambda: g.remote_dma(out, in_, T.sem[sem], T.sem.sent, pid, rid, mask), 100)], rd, wr, SEND + 1500 * (now[0] == 0), (sem, total))

    def xkeys(r, halves=(0, 1)):
        return ["x%d_%d_%d" % (r, h, b) for h in halves for b in range(4)]

    def qx(r, h):
        quant(T.qxc[:, H * h:H * h + H], T.qxs[:, H * h:H * h + H], T["xw%d" % r][:, 4 * H * h:4 * H * (h + 1)], xkeys(r, (h,)), ["qx%d" % h], H)

    dma("s", T.ut[:], T.u[:], [], ["ut"], LOAD + 350)
    dma("y", T.xw0[:, 0:4 * H], T.x[:, 0:4 * H], [], xkeys(0, (0,)), LOAD, 500)
    dma("y", T.xw0[:, 4 * H:4 * C], T.x[:, 4 * H:4 * C], [], xkeys(0, (1,)), LOAD, 500)
    dma("y", T.wq[:].bitcast(dt.uint8), T.wc[:], [], ["wq"], LOAD, 650)
    dma("y", T.zq[:].bitcast(dt.uint8), T.zc[:], [], ["zq"], LOAD, 650)
    dma("y", T.wp[:], T.ws[:], [], ["wp"], LOAD, 200)
    dma("y", T.zp[:], T.zs[:], [], ["zp"], LOAD, 200)
    dma("y", T.vt[:], T.v[:], [], ["vt"], LOAD, 350)

    btk = ["bt0", "bt1", "bt2", "bt3"]
    iota(T.ci[:, 0:8], [[16, 8]], 0, 0, ["ci0"], False)
    iota(T.ci[:, 8:24], [[16, 2], [32, 4], [0, 2]], 0, 0, ["ci1"], False)
    iota(T.ci[:, 24:48], [[1, 12], [12, 2]], 0, 0, ["ci2"], False)
    iota(T.ci[:, 48:60], [[12, 12]], 11, 0, ["ci3"], False)
    cp(T.cu[:, 0:24], T.ci[:, 0:24], ["ci0", "ci1"], ["cu0"], 24)
    cp(T.cu[:, 24:60], T.ci[:, 24:60], ["ci2", "ci3"], ["cu"], 36)
    iota(T.pi[:], [[0, 24]], 0, 1, ["pi"], False)
    iota(T.im[:], [[1, 16]], 0, -1, ["im"], False)
    iota(T.ia[:], [[16, 24]], 0, 0, ["ia"])
    fill(T.onek[:], UNIT, ["onek"], 64)
    fill(T.zero[:], 0.0, ["zero"], 256)
    cstk = ["cst%d" % a for a in range(4)]
    fill(T.cst[:], 0.0, cstk, 256)
    fill(T.ones[:], 1.0, ["ones"], 258)
    keep(T.cs0[:], T.onek[:], [[-2, 2], [0, 16], [1, 4]], 0, 0, A.is_ge, ["onek"], ["cs0"], 128)
    keep(T.cs1[:], T.cs0[:], [[2, 2], [0, 16], [-1, 4]], 1, 0, A.is_ge, ["cs0"], ["cs1"], 128)
    for a in range(4):
        move(T.cst[32 * a:32 * a + 32, 128 * a:128 * a + 128], T.cs1[32 * a:32 * a + 32, :], ["cs1"], [cstk[a]], 128, 64)
    quant(T.csc[:], T.css[:], T.cst[:], cstk, ["cs"], 128)
    fill(T.nt[:], 0.0, ["nt0", "nt1", "nt2", "nt3"], 256)
    iota(T.qt[:, 320:C], [[0, C - 320]], 0, 0, ["qtz"])
    iota(T.cnl[:, 0:16], [[0, 16]], -K, 0, ["cnl"])
    iota(T.cnh[:, 0:16], [[0, 16]], 256 - K, 0, ["cnh"])
    iota(T.gw[:, C:C + 16], [[0, 16]], 0, 0, ["gwz"])
    iota(T.ah[:, C:C + 16], [[0, 16]], 0, 0, ["ahz"])
    iota(T.bt[:, 4 * K:512], [[0, 512 - 4 * K]], 0, 0, ["btz"])
    iota(T.ramp[:], [[1, C]], -192, 0, ["ramp"])
    iota(T.gr[:, 0:16], [[2, 8], [16, 2]], 0, 0, ["gr0"])
    iota(T.gr[:, 16:32], [[2, 8], [-14, 2]], 15, 0, ["gr1"])
    iota(T.et[:, 640:672], [[0, 32]], 0, 0, ["etz"])
    flip(T.gr[:, 32:64], T.gr[:, 0:32], ["gr0", "gr1"], ["gq"], 32)
    ts(T.gl[:], T.gr[:, 32:34], 27.0, None, A.min, None, ["gq"], ["gl"], 4)
    iota(T.en[:, 0:16], [[0, 16]], 0, 0, ["enz0"])
    iota(T.en[:, C + 16:C + 32], [[0, 16]], 0, 0, ["enz1"])
    keep(T.gt[:], T.ones[:], [[1, 516]], -3, -4, A.is_equal, ["ones"], ["gt"], 516)
    for b in range(4):
        quant(T.ec[:, 128 * b:128 * b + 128], T.es[:, 128 * b:128 * b + 128], T.gt[:, 3 - b:515 - b], ["gt"], ["e%d" % b], 128)
    iota(T.ow[:, 0:C], [[1, C]], 0, 0, ["ow0"])
    for i in range(2):
        keep(T.k12[:, 24 * i:24 * i + 24], T.zero[:, 0:24], [[0, 2], [1, 12]], 0, 0, A.is_gt, ["zero"], ["k12%d" % i], 24, 8.0 * i - 4.0)
    ts(T.pj[:], T.pi[:], 15, None, A.bitwise_and, None, ["pi"], ["pj"], 24)
    quant(T.landc[:, 64:192], T.lands[:, 64:192], T.zero[:], ["zero"], ["landz"], 128)
    ts(T.im2[:], T.im[:], 15, None, A.bitwise_and, None, ["im"], ["im2"], 16)
    cp(T.qf[:], T.pj[:, 0:2], ["pj"], ["qf"], 2)
    cp(T.pu[:], T.pj[:], ["pj"], ["pu"], 24)
    ts(T.c16[:], T.im2[:], 15.0, 128.0, A.is_equal, A.mult, ["im2"], ["c16"], 16)
    line(T.il[:], T.ia[:], 1.0, T.qf[:, 0:1], ["ia", "qf"], ["il"], 24)
    quant(T.quc[:], T.qus[:], T.ut[:], ["ut"], ["qu"], 128)
    quant(T.qvc[:], T.qvs[:], T.vt[:], ["vt"], ["qv"], 128)
    for j in range(3):
        act(T.pus[:, 128 * j:128 * j + 128], T.qus[:].indirect(T.cu[:, 8 * j:8 * j + 8]), F.Copy, ["qu", "cu0"], ["pus%d" % j], PICK * 128)
        cp(T.puc[:, 128 * j:128 * j + 128].bitcast(dt.uint32), T.quc[:].bitcast(dt.uint32).indirect(T.cu[:, 8 * j:8 * j + 8]), ["qu", "cu0"], ["puc%d" % j], PICK * 128)
    line(T.ip[:, 0:4], T.il[:, 0:4], 2.0, 1.0 - 2 * K, ["il"], ["ip"], 4)
    line(T.ip[:, 5:6], T.il[:, 3:4], 2.0, 2.0 - 2 * K, ["il"], ["iq0"], 1)
    line(T.ip[:, 6:7], T.il[:, 3:4], 2.0, -2.0 * K, ["il"], ["iq1"], 1)
    line(T.ip[:, 7:8], T.il[:, 3:4], -2.0 * H, H * (2.0 * K - 1), ["il"], ["iq2"], 1)
    line(T.ip[:, 4:5], T.c16[:, 15:16], -1.0, float(W), ["c16"], ["cc0"], 1)
    act(T.half[:, 0:1], T.qf[:, 0:1], F.Sign, ["qf"], ["hf0"], 1, bias=-7.5)
    line(T.half[:, 1:2], T.half[:, 0:1], -256.0, 0.0, ["hf0"], ["hf1"], 1)
    line(T.half[:, 2:3], T.half[:, 0:1], 256.0, 0.0, ["hf0"], ["hf2"], 1)
    line(T.half[:, 3:4], T.half[:, 0:1], 512.0, -512.0, ["hf0"], ["hf3"], 1)
    move(T.ctl[:], T.c16[:].indirect(T.pu[:]), ["c16", "pu"], ["ctl"], PICK * C)
    move(T.ctlc[:], T.ctl[:], ["ctl"], ["ctlc"], C, H, "v")
    ts(T.ctlc[:, 15:C:16], T.il[:], float(W), None, A.add, None, ["il"], ["ctlc"], 24)
    ts(T.crow[:], T.ramp[:], T.half[:, 2:3], None, A.max, None, ["ramp", "hf2"], ["crow"], H)
    line(T.ctf[:], T.zero[:, 0:C], 1.0, T.half[:, 3:4], ["zero", "hf3"], ["ctf"], C, H)
    line(T.pre[:], T.zero[:, 0:C], 1.0, T.half[:, 1:2], ["zero", "hf1"], ["pre"], C, H)
    Z = T.zero[:, 0:C]

    def score(bank, j, c0, c1, rd):
        mm(bank, c1 - c0, T.puc[:, 128 * j:128 * j + 128], T.pus[:, 128 * j:128 * j + 128], T.qxc[:, c0:c1], T.qxs[:, c0:c1], True, True, ["puc%d" % j, "pus%d" % j] + rd)

    def turn(bank, h):
        flip(T.pt[:, H * h:H * h + H], T["ps%d" % bank][:, 0:H], ["ps%d" % bank], ["pt%d" % h], H)

    def wrap(out, src, ctl, init, rd, okey):
        scan(out[:], src, ctl[:], init, A.min, A.add, rd, [okey], H)

    qx(0, 0)
    qx(0, 1)
    for r in range(R):
        last = r == R - 1
        seen.clear()
        seen["on"] = 1
        now[0] = r
        X, XN = T["xw%d" % r], T["xw%d" % (r + 1)]
        xk = xkeys(r)
        score(0, 0, 0, H, ["qx0"])
        score(1, 2, 0, _reach(VB - 1), ["qx0"])
        if VB < 6:
            score(2, 2, 0, H, ["qx0"])
        turn(0, 0)
        score(3, 0, H, C, ["qx1"])
        score(4, 2, 0, C, ["qx0", "qx1"])
        score(7, 1, 0, C, ["qx0", "qx1"])
        turn(3, 1)

        def row(e, b):
            if b < 4:
                return T.sg[:, 128 * (4 * e + b):128 * (4 * e + b) + 128], "sg%d" % (4 * e + b)
            return T["tri%d" % (b // 2)][:, 2 * e + b % 2:4 * _reach(b):4], "tr%d_%d" % (b, e)

        def sgn(e, b):
            bank = "ps1" if e else "ps7"
            out, key = row(e, b)
            act(out, T[bank][:, 0:_reach(b)], F.Sign, [bank, "pt%d" % (b // 6)], [key, "rho%d" % (12 * e + b)], _reach(b),
                bias=T.pt[:, 32 * b + 16 * e:32 * b + 16 * e + 1], scale=-1.0, accum_out=T.rho[:, 12 * e + b:12 * e + b + 1])

        def cmp(b):
            out, key = row(1, b)
            bank = "ps4" if b >= 6 else "ps2"
            ts(out, T[bank][:, 0:_reach(b)], T.pt[:, 32 * b + 16:32 * b + 17], -2.0, A.is_ge, A.mult, [bank, "pt%d" % (b // 6)], [key], _reach(b))

        def cnt(b):
            n, t, tri = _reach(b), 2 + b % 2, T["tri%d" % (b // 2)]
            e = H * (b - VB + 1)
            scan(T.sj[:, e - n // 2:e], tri[:, t:2 * n:4], tri[:, 2 * n + t:4 * n:4], 2.0 * n - C, A.add, A.add, ["tr%d_1" % b], ["sj%d" % b], n // 4)

        def cols(k):
            n = 64 * k
            o = {5: 0, 4: 320, 3: 576, 2: 768}[k]
            quant(T.qfc[:, o:o + n], T.qfs[:, o:o + n], T["tri%d" % k][:, 0:4 * n], ["tr%d_%d" % (b, e) for b in (2 * k, 2 * k + 1) for e in (0, 1)], ["qf%d" % k], n)
            mm(5, n, T.csc[:], T.css[:], T.qfc[:, o:o + n], T.qfs[:, o:o + n], k == 5, k == 2, ["cs", "qf%d" % k])

        for b in range(12):
            if b < VB:
                sgn(1, b)
            else:
                cmp(b)
                cnt(b)
        for b in range(12):
            sgn(0, b)
        for k in (5, 4, 3, 2):
            cols(k)
        for t in range(4):
            move(T.xp[:, W * t:W * t + C], X[:, t:4 * C:4], xk, ["xp%d" % t], C, H, "qs")
        move(T.ew[:, 256:256 + C], T.pre[:], ["pre"], ["ew0", "ew1"], C, H, "qs")

        line(T.kr[:, 12:12 + VB], T.rho[:, 12:12 + VB], -UNIT, (2 * C - 32 * VB) * UNIT, ["rho%d" % i for i in range(12, 12 + VB)], ["kr1"], 6)
        line(T.kr[:, 12 + VB:24], T.sj[:, H - 1:(12 - VB) * H:H], -UNIT, C * UNIT, ["sj%d" % b for b in range(VB, 12)], ["kr2"], 6)
        line(T.kr[:, 0:12], T.rho[:, 0:12], -UNIT, C * UNIT, ["rho%d" % i for i in range(12)], ["kr0"], 12)
        flip(T.qt[:, 0:320], T.ps5[:, 0:320], ["ps5"], ["qt"], 320)
        tt(T.kk[:, 12:24], T.qt[:, 16:C:32], T.kr[:, 12:24], A.add, ["qt", "qtz", "kr1", "kr2"], ["kk1"], 12)
        tt(T.kk[:, 0:12], T.qt[:, 0:C:32], T.kr[:, 0:12], A.add, ["qt", "qtz", "kr0"], ["kk0"], 12)
        kkk = ["kk0", "kk1"]
        cuts = (2 * (C - K), 2 * K)
        for i in range(2):
            for e in range(2):
                ts(T.nt[:, 48 * i + 2 * e:48 * i + 48:4], T.kk[:, 12 * e:12 * e + 12], (cuts[i] + 0.5) * UNIT, None, A.is_gt, None, ["kk%d" % e], ["nt%d" % (2 * i + e)], 12)
        quant(T.ntc[:], T.nts[:], T.nt[:], ["nt0", "nt1", "nt2", "nt3"], ["nq"], 128)
        mm(6, 128, T.csc[:], T.css[:], T.ntc[:], T.nts[:], True, True, ["cs", "nq"])
        for i in range(2):
            ts(T.fa[:, 24 * i:24 * i + 24], T.kk[:], (cuts[i] + 0.5) * UNIT, cuts[i] * UNIT, A.is_gt, A.add, kkk, ["fa%d" % i], 24)
            tt(T.aa[:, 24 * i:24 * i + 24], T.kk[:], T.fa[:, 24 * i:24 * i + 24], A.subtract, kkk + ["fa%d" % i], ["aa%d" % i], 24)
            for j, o in enumerate((A.max, A.min)):
                scan(T.st[:, 48 * i + 24 * j:48 * i + 24 * j + 24], T.k12[:, 24 * j:24 * j + 24], T.aa[:, 24 * i:24 * i + 24], 0.0, A.add, o, ["k12%d" % j, "aa%d" % i], ["st%d" % (2 * i + j)], 24)
            move(T.sw[:, 64 * i:64 * i + 64], T.st[:, 48 * i:48 * i + 48].indirect(T.cu[:, 48:52]), ["st%d" % (2 * i), "st%d" % (2 * i + 1), "cu"], ["sw%d" % i], PICK * 64)
            flip(T.su[:, 64 * i:64 * i + 64], T.sw[:, 64 * i:64 * i + 64], ["sw%d" % i], ["su%d" % i], 64)
            for j, o in enumerate((A.max, A.min)):
                most(T.sx[:, 2 * i + j:2 * i + j + 1], T.su[:, 64 * i + 32 * j:64 * i + 32 * j + 32], o, ["su%d" % i], ["sx%d" % (2 * i + j)], 32)
        for i, n in ((0, (0.5 - K) * UNIT), (1, (K - C - 0.5) * UNIT)):
            k1, ky = (T.k1l, T.k1h)[i], (T.kyl, T.kyh)[i]
            line(k1[:], T.kk[:].indirect(T.cu[:, 24:48]), 1.0, -cuts[i] * UNIT, kkk + ["cu"], ["k1%d" % i], PICK * C)
            flip(ky[:], k1[:], ["k1%d" % i], ["ky%d" % i], H)
            act(T.tz[:, 4 + 12 * i:16 + 12 * i], T.ps6[:, 12 * i:12 * i + 12], F.Identity, ["ps6"], ["nb%d" % i], 12, accum_out=T.tz[:, 2 + i:3 + i])
            act(T.tz[:, i:i + 1], T.tz[:, 2 + i:3 + i], F.Sign, ["nb%d" % i], ["tz%d" % i], 1, bias=n)
            ts(T.ty[:, i:i + 1], T.sx[:, 2 * i + 1:2 * i + 2], T.tz[:, i:i + 1], T.sx[:, 2 * i:2 * i + 1], A.add, A.max, ["tz%d" % i, "sx%d" % (2 * i), "sx%d" % (2 * i + 1)], ["ty%d" % i], 1)

        tl, th = T.ty[:, 0:1], T.ty[:, 1:2]
        act(T.tz[:, 28:29], th, F.Identity, ["ty1"], ["tq"], 1, bias=0.25 * UNIT)
        CLi, CLe, CHi, CHe = T.cnl[:, 16:C + 16], T.cnl[:, 15:C + 15], T.cnh[:, 16:C + 16], T.cnh[:, 15:C + 15]
        ts(T.gw[:, 0:C], T.kyl[:], tl, None, A.is_ge, None, ["ky0", "ty0"], ["gw"], H)
        ts(T.al[:], T.kyl[:], tl, None, A.is_gt, None, ["ky0", "ty0"], ["al"], H)
        scan(T.capl[:, ::-1], Z, T.gw[:, C:0:-1], 0.0, A.add, A.subtract, ["zero", "gw", "gwz"], ["capl"], H)
        scan(CLi, T.al[:], T.capl[:], -float(K), A.add, A.max, ["al", "capl"], ["cnl"], H)
        ts(T.ah[:, 0:C], T.kyh[:], th, None, A.is_lt, None, ["ky1", "ty1"], ["ah"], H)
        act(T.k1l[:], T.kyh[:], F.Sign, ["ky1", "tq"], ["gi", "k10"], C, bias=T.tz[:, 28:29], scale=-1.0)
        act(T.gh[:], T.k1l[:], F.Relu, ["gi", "k10"], ["gh"], C)
        scan(T.caph[:, ::-1], Z, T.ah[:, C:0:-1], 256.0, A.add, A.subtract, ["zero", "ah", "ahz"], ["caph"], H)
        scan(CHi, T.gh[:], T.caph[:], 256.0 - K, A.add, A.min, ["gh", "caph"], ["cnh"], H)

        scan(T.sm[:, 0:H], T.cnl[:, 16:C + 16:2], T.cnl[:, 17:C + 16:2], -256.0, A.max, A.add, ["cnl"], ["zz"], H // 2)
        for k in range(4 - NV):
            act(T.sgl[:, C * k:C * k + H], T.sm[:, 0:H], F.Sign, ["zz", "ip"], ["sgl%d" % k, "dl%d" % k], H, bias=T.ip[:, k:k + 1], scale=-1.0, accum_out=T.dl[:, k:k + 1])
        ts(T.lo[:, 0:4 - NV], T.dl[:, 0:4 - NV], float(H), None, A.add, None, ["dl%d" % k for k in range(4 - NV)], ["lo"], 4)
        if NV:
            ts(T.sgl[:, 3 * C:3 * C + H], T.sm[:, 0:H], T.ip[:, 5:6], T.ip[:, 6:7], A.min, A.max, ["zz", "iq0", "iq1"], ["sgl3"], H // 2)
            scan(T.sm[:, H:H + 96], T.sgl[:, 3 * C:3 * C + 96], T.sgl[:, 3 * C + 96:3 * C + H], T.ip[:, 7:8], A.add, A.add, ["sgl3", "iq2"], ["sm3"], H // 4)
            ts(T.lo[:, 3:4], T.sm[:, H + 95:H + 96], -1.0, float(H), A.mult, A.add, ["sm3"], ["lo1"], 4)
        wrap(T.cva, CLi, T.ctl, 128.0 - K, ["cnl", "ctl"], "cva")
        wrap(T.cvb, CLe, T.ctl, 128.0 - K, ["cnl", "ctl"], "cvb")
        tt(T.t1[:], T.cva[:, 15:C:16], T.cvb[:, 15:C:16], A.is_equal, ["cva", "cvb"], ["t1"], 24)
        line(T.lm[:], T.cvb[:, 15:C:16], 1.0, T.ip[:, 4:5], ["cvb", "cc0"], ["lm"], 24)
        tt(T.wm[:], T.t1[:], T.lm[:], A.mult, ["t1", "lm"], ["wm"], 24)
        wrap(T.cvc, CHe, T.ctlc, 384.0 - K, ["cnh", "ctlc"], "cvc")
        tt(T.cil[:], T.cvc[:, 15:C:16], T.wm[:], A.subtract, ["cvc", "wm"], ["oo"], 24)
        cp(T.ou[:, 0:18], T.cil[:, 0:18], ["oo"], ["ou0"], 18)
        ts(T.ou[:, 18:24], T.cil[:, 18:24], -480.0, None, A.add, None, ["oo"], ["ou1"], 6)
        scan(T.dat[:], CHe, T.crow[:], -256.0, A.max, A.min, ["cnh", "crow"], ["dat"], H)
        for t in range(4):
            move(T.bt[:, t:4 * K:4], T.xp[:, W * t:W * t + C].indirect(T.lo[:]), ["xp%d" % t, "lo", "lo1"], ["bt%d" % t], PICK * K)
        s0, l0 = 128 * r, (0, 192, 256)[r]
        quant(T.qbc[:, s0:s0 + 128], T.qbs[:, s0:s0 + 128], T.bt[:], btk + ["btz"], ["qb%d" % r], 128)
        send(T.landc[:, l0:l0 + K].bitcast(dt.uint8), T.qbc[:, s0:s0 + K].bitcast(dt.uint8), "arr%d" % r, 2 * neng, ["qb%d" % r], ["lc%d" % r])
        send(T.lands[:, l0:l0 + K], T.qbs[:, s0:s0 + K], "arr%d" % r, 2 * neng, ["qb%d" % r], ["ls%d" % r])
        if last:
            move(T.lsend[:], T.ramp[:].indirect(T.lo[:]), ["ramp", "lo", "lo1"], ["lsend"], PICK * K)
            send(T.lland[:], T.lsend[:], "arrl", neng, ["lsend", "lc%d!" % r], ["lland"])

        cp(T.ew[:].indirect(T.ou[:, 0:18]), T.dat[:, 0:288], ["ou0", "dat"], ["ew0", "ew1"], PUT * 288)
        cp(T.ew[:, 480:1088].indirect(T.ou[:, 18:24]), T.dat[:, 288:C], ["ou1", "dat"], ["ew1"], PUT * 96)
        scan(T.en[:, 16:240], T.ctf[:, 0:224], T.ew[:, 256:480], -256.0, A.add, A.max, ["ctf", "ew0"], ["en0"], 112)
        scan(T.en[:, 240:C + 16], T.ctf[:, 224:C], T.ew[:, 480:256 + C], T.en[:, 239:240], A.add, A.max, ["ctf", "ew1", "en0"], ["en1"], 80)
        for h in range(2):
            o, ek = 448 * h, ["en0"] + ["en1", "enz1"] * h
            n1, n2 = 224 - 32 * h, 224
            flip(T.et[:, o:o + n1], T.en[:, 16 + H * h:16 + H * h + n1], ek, ["et%d" % (2 * h)], n1 // 2)
            flip(T.et[:, o + 224:o + 448], T.en[:, H * h:H * h + n2], ek + ["enz0"], ["et%d" % (2 * h + 1)], n2 // 2)
            tt(T.em[:, 32 * h:32 * h + 28], T.et[:, o:o + 448:16], T.et[:, o + 8:o + 448:16], A.min, ["et%d" % (2 * h), "et%d" % (2 * h + 1), "etz"], ["em%d" % h], 28)
            ts(T.eo[:, 16 * h:16 * h + 16], T.em[:, 32 * h:32 * h + 28].indirect(T.gl[:, 0:1]), 192.0, None, A.add, None, ["em%d" % h, "gl"], ["eo%d" % h], PICK * 16)

        v0 = (0, 128, 192)[r]
        lk = ["lc%d" % r, "ls%d" % r, "landz"] + (["lc1", "ls1"] if r == 2 else [])
        for b in range(4):
            mm(4 + b, 128, T.ec[:, 128 * b:128 * b + 128], T.es[:, 128 * b:128 * b + 128], T.landc[:, v0:v0 + 128], T.lands[:, v0:v0 + 128], True, True, ["e%d" % b] + lk)
            move(T.xp[:, W * b + C:W * b + W], T["ps%d" % (4 + b)][:, l0 - v0:l0 - v0 + K], ["ps%d" % (4 + b)], ["xa%d" % b], K)

        for h in range(2):
            n = 13 - h
            tile = (T.ta, T.tb)[h]
            for t in range(4):
                move(tile[:, t:64 * n:4], T.xp[:, W * t:W * t + W].indirect(T.eo[:, 16 * h:16 * h + n]), ["xp%d" % t, "xa%d" % t, "eo%d" % h], ["t%d_%d" % (h, t)], PICK * 16 * n)
            if h:
                move(T.tb[:, 4 * H:4 * H + 4], T.ta[:, 0:4], ["t0_%d" % t for t in range(4)], ["tbw"], 4)
            for rot in range(2):
                i = 2 * h + rot
                quant(T.qtc[:, H * i:H * i + H], T.qts[:, H * i:H * i + H], tile[:, 4 * rot:4 * rot + 4 * H],
                      ["t%d_%d" % (h, t) for t in range(4)] + (["tbw"] if i == 3 else []), ["qt%d" % i], H)
            for b in range(4):
                for tap in range(2):
                    i = 2 * h + tap
                    wq, wp, kk = (T.wq, T.wp, ["wq", "wp"]) if tap == 0 else (T.zq, T.zp, ["zq", "zp"])
                    mm(4 * h + b, H, wq[:, 128 * b:128 * b + 128], wp[:, 128 * b:128 * b + 128], T.qtc[:, H * i:H * i + H], T.qts[:, H * i:H * i + H], tap == 0, tap == 1, kk + ["qt%d" % i])
                ps = "ps%d" % (4 * h + b)
                line(XN[:, 4 * H * h + b:4 * H * (h + 1):4], T[ps][:, 0:H], 0.015625, 0.0, [ps], ["x%d_%d_%d" % (r + 1, h, b)], H)
            qx(r + 1, h)

    seen.update({"ps0": 4, "ps1": 4, "qx0": 2, "qx1": 2})
    line(T.ow[:, C:W], T.lland[:], 1.0, 576.0, ["lland"], ["ow1"], K)
    for h in range(2):
        move(T.olb[:, H * h:H * h + H], T.ow[:].indirect(T.eo[:, 16 * h:16 * h + 12]), ["ow0", "ow1", "eo%d" % h], ["olb%d" % h], PICK * H)
    dma("y", T.ol[:], T.olb[0:128:16, :], ["olb0", "olb1"], [], LOAD)
    for h in range(2):
        mm(h, H, T.qvc[:], T.qvs[:], T.qxc[:, H * h:H * h + H], T.qxs[:, H * h:H * h + H], True, True, ["qv", "qx%d" % h])
        move(T.ysb[:, H * h:H * h + H], T["ps%d" % h][:, 0:H], ["ps%d" % h], ["y%d" % h], H)
        dma("y", T.y[:, H * h:H * h + H], T.ysb[:, H * h:H * h + H], ["y%d" % h], [], LOAD + 300)
        dma("y", T.oc[:, 4 * H * h:4 * H * (h + 1)], T.qxc[:, H * h:H * h + H].bitcast(dt.uint8), ["qx%d" % h], [], LOAD + 300)
    for k in range(4):
        dma("sy"[k % 2], T.osc[4 * k:4 * k + 4, :], T.qxs[32 * k:32 * k + 4, :], ["qx0", "qx1"], [], LOAD)

    semof = {"v": "sv", "s": "ss", "p": "sp", "q": "sq", "y": None}
    count = {}
    waited = {k: {} for k in queue}
    lastw, readers = {}, {}
    ndma = [0]
    behind = {}

    def wait(e, tok):
        if waited[e].get(tok[0], 0) < tok[1]:
            queue[e].wait_ge(T.sem[tok[0]], tok[1])
            waited[e][tok[0]] = tok[1]
            for s, n in behind.get(tok, {}).items():
                waited[e][s] = max(waited[e].get(s, 0), n)

    for (e, make, _), (_, rd, wr, _, kind, _, _) in _layout(plan):
        toks = []
        rd = [k for k in rd if k[-1] != "!"]
        for k in rd:
            if k in lastw:
                toks.append(lastw[k])
            if k.startswith("ps"):
                toks += [t for t in readers.get(k, []) if t[0] != semof[e]]
        for k in wr:
            toks += readers.get(k, [])
            if k in lastw and kind != "chain":
                toks.append(lastw[k])
        need = {}
        for t in toks:
            need[t[0]] = max(need.get(t[0], 0), t[1])
        for s in sorted(need, key=lambda a: -len([b for b in need if behind.get((a, need[a]), {}).get(b, 0) >= need[b]])):
            wait(e, (s, need[s]))
        if kind == "dma":
            s = "d%d" % ndma[0]
            ndma[0] += 1
            make().then_inc(T.sem[s], 16)
            count[s] = 16
            tok = (s, 16)
        elif kind is None or kind == "chain":
            s = semof[e]
            count[s] = count.get(s, 0) + 1
            make().then_inc(T.sem[s], 1)
            tok = (s, count[s])
        else:
            make()
            count["sent"] = count.get("sent", 0) + neng
            count[kind[0]] = kind[1]
            tok = kind
            rd = []
        if kind is None or kind in ("chain", "dma"):
            behind[tok] = dict(waited[e])
        for k in rd:
            readers.setdefault(k, []).append(tok)
        for k in wr:
            lastw[k] = tok
            readers[k] = []

    for s in count:
        g.wait_ge(T.sem[s], count[s])
